import numpy as np, ml_dtypes
CORES = [6,15,38,47]
N = 4
BF = ml_dtypes.bfloat16
def f(rng, *shape):
    return (rng.standard_normal(shape, dtype=np.float32) * np.exp2(rng.integers(-2, 3, shape[:-1] + (1,)))).astype(BF)
def wide(rng, *shape):
    v = f(rng, *shape).astype(np.float32); k = shape[:-2] + (1, shape[-1])
    return (v * np.exp2(rng.integers(-6, 7, k)) * (rng.random(k) > 0.0625)).astype(BF)
def gentries(a):
    return np.ascontiguousarray(a.reshape(8, 16, -1).transpose(0, 2, 1)).reshape(8, -1)
def gtable(e):
    e = np.asarray(e); return np.ascontiguousarray(e.reshape(8, -1, 16).transpose(0, 2, 1)).reshape(128, -1).astype(np.int32)
B, PI, C, F, NEED, R = 192, 16, 8, 4096, 9, 3
def faces(rng):
    v = rng.standard_normal((N, 8, 16, F), dtype=np.float32) + rng.standard_normal((N, 8, 1, F), dtype=np.float32)
    return (v * np.exp2(rng.integers(-2, 3, (N, 8, 16, 1)))).astype(BF).reshape(N, 128, F)
def parts(rng):
    return rng.integers(0, C + 1, (N, 8, PI, B)), rng.integers(0, F, (N, 8, C, PI, B)), rng.integers(0, PI, (N, 8, B))
def pack(x, c, kinds, p):
    s = np.where(np.arange(C)[:, None, None] < c[:, :, None], kinds, F)
    return {"x": x, "sd": np.stack([gtable(a.reshape(8, -1)) for a in s]), "act": np.stack([gtable(a) for a in p])}
def setup_inputs(rng):
    c, kinds, p = parts(rng)
    return pack(faces(rng), c, kinds, p)
def setup_inputs_full(rng):
    c, kinds, p = parts(rng)
    c = C - rng.choice(np.array([0, 0, 0, 1, 1, 2]), (N, 8, PI, B))
    c[:, 1:3] = C - 1; p[:, 1] = rng.integers(0, PI); p[:, 2] = rng.integers(0, PI, (N, 1)); kinds[:, 2] = rng.integers(0, F)
    n = np.take_along_axis(c, p[:, :, None, :], 2); n[..., ::2] = C; n[:, 1:3] = C
    np.put_along_axis(c, p[:, :, None, :], n, 2); c[0, 0] = C
    return pack(faces(rng), c, kinds, p)
def setup_inputs_ties(rng):
    c, kinds, p = parts(rng)
    cl = rng.choice(np.array([-1] * 7 + [0, 16 - NEED, 17 - NEED, NEED - 1, NEED, NEED + 1, 16]), (N, 8, 1, F))
    o = np.argsort(rng.random((N, 8, 16)), axis=2)[..., None]
    v = np.where(cl < 0, 1.0, np.where(o < cl, 2.0, 0.0))
    z = v[:, 1::4] - 1.0
    v[:, 1::4] = np.where(z == 0, rng.choice(np.array([0.0, -0.0]), (N, 2, 1, F)), z)
    e = rng.integers(-3, 4, (N, 8, 16, 1)); e[:, 3] = 59
    v = v * np.exp2(e)
    v[:, 2::4] = v[:, 2::4] * np.exp2(rng.choice(np.array([-57.0, 50.0]), (N, 2, 1, F)))
    c = 2 * rng.integers(0, C // 2 + 1, (N, 8, PI, B))
    return pack(v.astype(BF).reshape(N, 128, F), c, kinds, p)
def setup_inputs_sparse(rng):
    c, kinds, p = parts(rng)
    c = np.where(rng.random((N, 8, PI, B)) < 0.2, rng.integers(1, C + 1, (N, 8, PI, B)), 0)
    n = np.where(rng.random((N, 8, 1, B)) < 0.5, rng.integers(1, C + 1, (N, 8, 1, B)), 0)
    q = rng.permutation(N); n[q[0]] = 0; n[q[1]] = 1
    h = rng.permutation(8); n[:, h[1]] = 0
    np.put_along_axis(c, p[:, :, None, :], n, 2); c[:, h[0]] = 0
    return pack(faces(rng), c, kinds, p)
def setup_inputs_ends(rng):
    c, kinds, p = parts(rng); few = np.array([0, F - 1, 1, F - 2, F // 2])
    p = (PI - 1) * rng.integers(0, 2, (N, 8, B))
    kinds[:, ::2] = rng.choice(few, (N, 4, C, PI, B)); kinds[:, 0] = rng.choice(few, (1, 1, 1, B))
    return pack(faces(rng), c, kinds, p)
def setup_inputs_spread(rng):
    c, kinds, p = parts(rng)
    c = np.minimum(((C + 1) * rng.random((N, 8, PI, B)) ** np.exp2(rng.integers(-2, 3, (N, 8, 1, B)))).astype(np.int64), C)
    kinds = np.minimum((F * rng.random((N, 8, C, PI, B)) ** 3).astype(np.int64), F - 1)
    v = wide(rng, N, 128, F).astype(np.float32).reshape(N, 8, 16, F); v[:, 1::2] *= np.float32(2.0 ** 44)
    return pack(v.reshape(N, 128, F).astype(BF), c, kinds, p)
def check_inputs(d):
    bad = []
    v = np.abs(np.asarray(d["x"]).astype(np.float32))
    if not np.all((v == 0) | ((v >= 2.0 ** -60) & (v <= 2.0 ** 60))): bad.append("size of x")
    if np.min(d["sd"]) < 0 or np.max(d["sd"]) > F: bad.append("range of sd")
    if np.min(d["act"]) < 0 or np.max(d["act"]) > PI - 1: bad.append("range of act")
    s = np.stack([gentries(a) for a in d["sd"]]).reshape(N, 8, C, PI, B)
    if np.any((s[:, :, :-1] == F) & (s[:, :, 1:] != F)): bad.append("a seed above an empty slot")
    return bad
def reference(x, sd, act):
    s = np.stack([gentries(a) for a in sd]).astype(np.int64).reshape(N, 8, C, PI, B)
    p = np.stack([gentries(a) for a in act]).astype(np.int64)
    xf = np.concatenate([x.astype(np.float32).reshape(N, 8, 16, F), np.zeros((N, 8, 16, 1), np.float32)], axis=3)
    pits = np.arange(PI)[:, None]; slots = np.arange(C)[:, None, None]; score = np.zeros((N, 8, B), np.int64)
    for rnd in range(R):
        c = np.add.reduce((s != F).astype(np.int64), axis=2)
        up = np.take_along_axis(s, p[:, :, None, None, :], 3)[:, :, :, 0]
        n = np.take_along_axis(c, p[:, :, None, :], 2)[:, :, 0]
        own = pits == p[:, :, None, :]
        s = np.where(own[:, :, None], F, s); c = np.where(own, 0, c)
        up, p, n = np.roll(up, 1, axis=0), np.roll(p, 1, axis=0), np.roll(n, 1, axis=0)
        k = (pits - p[:, :, None, :] - 1) & (PI - 1)
        here = k < n[:, :, None, :]
        a = np.where(here, np.take_along_axis(up, np.minimum(k, C - 1), 2), F)
        w = np.zeros((N, 8, PI, B), np.int64)
        for r in range(N):
            fa = np.take_along_axis(xf[r], a[r].reshape(8, 1, PI * B), 2)
            for j in range(C):
                fs = np.take_along_axis(xf[r], s[r, :, j].reshape(8, 1, PI * B), 2)
                beat = np.add.reduce((fa > fs).astype(np.int64), axis=1) >= NEED
                w[r] += beat.reshape(8, PI, B) & (s[r, :, j] != F)
        cap = here & ((2 * w > c) | (c == C))
        score = score + np.add.reduce(np.where(cap, c, 0), axis=2)
        at = np.where(cap, 0, c)
        s = np.where(cap[:, :, None], F, s)
        s = np.where(here[:, :, None] & (slots == at[:, :, None]), a[:, :, None], s)
        last = (p + n) & (PI - 1)
        p = np.where(np.take_along_axis(cap, last[:, :, None, :], 2)[:, :, 0], PI - 1 - last, last)
    return {"ys": np.stack([gtable(v.reshape(8, -1)) for v in s]).astype(np.float32),
            "yp": np.stack([gtable(v) for v in p]).astype(np.float32), "yc": np.stack([gtable(v) for v in score]).astype(np.float32)}

@@ -1,0 +1,596 @@
+from concourse.mybir import AluOpType, ActivationFunctionType
+
+A = AluOpType
+F = ActivationFunctionType
+
+NCH = 2
+NB = 12 // NCH
+N8 = 8 * NB
+N16 = 16 * NB
+MW = N8 + 16
+CV = [[224, 224, 224], [224, 224, 224]]
+GCOL = 64
+GC = 100
+NENG = 8
+K = 4128
+B = 8192.0
+EMPTY = 4096.0
+SCALES = (1.0, -1.0, 100.0 / B, -101.0 / B, 100.0, B / 2, 1.0 / 512, 8.0, 528.0, -4 * B, 16 * B, -15 * B, 15.0)
+
+SCRATCH = {n: ("sbuf", [128, w], d) for n, w, d in (
+    ("xw", 2 * K, "bfloat16"), ("sdb", 1536, "int32"), ("actb", 12, "int32"), ("ypb", 12, "float32"),
+    ("ycb", 12, "float32"), ("ci", 8, "int32"), ("cf", 16, "float32"), ("i144", 144, "float32"), ("wb", 144, "bfloat16"),
+    ("idm", 128 * len(SCALES), "bfloat16"), ("idf", 128, "float32"), ("pos", N16, "float32"), ("qf", N16, "bfloat16"),
+    ("q24", N16, "float32"), ("rb", N16, "bfloat16"), ("rst", N16, "float32"), ("one", N16, "bfloat16"),
+    ("eight", N16, "bfloat16"), ("lb", 16, "uint16"), ("lu", 16, "uint16"), ("lm", 16, "uint16"), ("ln", 16, "uint16"),
+    ("ld", 48, "uint16"), ("lf", N8, "uint16"))}
+SCRATCH["ysb"] = ("sbuf", [128, 128, 12], "float32")
+for _k in range(13):
+    SCRATCH["w%d" % _k] = ("sbuf", [128, N8], "int32" if _k < 8 else "float32")
+PER_CHAIN = (
+    ("lz", N8, "uint16"), ("st", 9 * N16, "float32"), ("sel", 8 * N16, "float32"), ("lo", 9 * N16, "float32"),
+    ("off", 7 * N8, "uint16"), ("aoff", N8, "uint16"), ("fa", 16 * N8, "bfloat16"), ("fs", 112 * N8, "bfloat16"),
+    ("cm", 112 * N8, "bfloat16"), ("sg", 8 * N16, "bfloat16"), ("mo", 3 * MW, "int32"), ("mi", 3 * MW, "int32"),
+    ("mr", MW, "int32"), ("ti", N16, "int32"), ("ns", N16, "int32"), ("dsel", N16, "bfloat16"), ("sn", N16, "bfloat16"),
+    ("clr", N16, "bfloat16"), ("pb", 32, "bfloat16"), ("a16", N16, "float32"), ("cl", N16, "bfloat16"),
+    ("c16", 3 * N16, "bfloat16"), ("at", 3 * N16, "bfloat16"), ("hs", N16, "bfloat16"), ("es", N16, "bfloat16"),
+    ("oh", N16, "float32"), ("nb", N16, "float32"), ("an", N16, "float32"), ("pr", N16, "bfloat16"),
+    ("t0", N16, "float32"), ("si", 64, "int32"), ("sf", 64, "float32"))
+for _c in range(NCH):
+    for _n, _w, _d in PER_CHAIN:
+        SCRATCH["%s%d" % (_n, _c)] = ("sbuf", [128, _w], _d)
+for _k in range(8):
+    SCRATCH["ps%d" % _k] = ("psum", [128, 512], "float32")
+
+SEMAPHORES = (["cv", "cs", "cp", "cg", "sent", "dact", "dsd", "dx0", "dyp", "dyc"] + ["dy%d" % h for h in range(4)]
+              + ["arr%d_%d" % (c, t) for c in range(NCH) for t in range(3)])
+
+CASES = ((1.04, 1.56, 0.5, 40.0, 75.0, 90.0, 1.0), (0.9, 1.1, 0.45, 20.0, 60.0, 60.0, 0.9),
+         (1.15, 2.0, 0.6, 50.0, 90.0, 120.0, 1.2), (1.04, 1.56, 0.8, 60.0, 150.0, 250.0, 1.3))
+LAG = 5000.0
+TRIES = 2500
+PLAN = {}
+
+
+def build(g, T, topo, core, ops):
+    rank = T.rank_of(core)
+    nxt = T.cores[(rank + 1) % len(T.cores)]
+    rid, pid = topo.addr(nxt)[0:2]
+    emask = sum(1 << e for e in topo.engines(core, nxt)[:NENG])
+    V, S, P, Y = g.vector, g.scalar, g.tensor, g.sync
+    last_w, readers = {}, {}
+
+    def add(eng, fn, n, R=(), W=(), lat=0.0, sem=None, acq=None, rel=None):
+        i = len(ops)
+        soft = {last_w[k[1:]] for k in R if k[0] == "~"}
+        R = [k for k in R if k[0] != "~"]
+        deps = {last_w[k] for k in list(R) + list(W) if k in last_w}
+        for k in W:
+            deps.update(readers.get(k, ()))
+        for k in R:
+            readers.setdefault(k, []).append(i)
+        for k in W:
+            last_w[k] = i
+            readers[k] = []
+        deps.discard(i)
+        ops.append({"eng": eng, "fn": fn, "n": n, "lat": lat, "deps": deps, "sem": sem, "soft": soft,
+                    "nm": (list(W) + ["-"])[0], "acq": acq, "rel": rel})
+
+    def ap(x):
+        return T["ps%d" % x[0]["k"]][:, x[1]:x[2]] if isinstance(x, tuple) else x
+
+    def ts(out, in0, s1, s2, o0, o1, n, R, W):
+        if o1 is None:
+            add("v", lambda: [V.tensor_scalar(out, in0, s1, None, o0)], n, R, W)
+        else:
+            add("v", lambda: [V.tensor_scalar(out, in0, s1, s2, o0, o1)], n, R, W)
+
+    def tt(out, in0, in1, op, n, R, W, rel=None):
+        add("v", lambda: [V.tensor_tensor(out, in0, ap(in1), op)], n, R, W, rel=rel)
+
+    def cp(out, in_, n, R, W):
+        add("v", lambda: [V.tensor_copy(out, in_)], n, R, W)
+
+    def fill(out, val, n, W):
+        add("v", lambda: [V.memset(out, val)], n, (), W)
+
+    def scan(out, d0, d1, o0, o1, n, R, W, rel=None):
+        add("v", lambda: [V.tensor_tensor_scan(out, ap(d0), ap(d1), 0.0, o0, o1)], n, R, W, rel=rel)
+
+    def act(out, in_, func, bias, scale, n, R, W, acq=None, rel=None):
+        def fn():
+            if bias is None:
+                return [S.activation(ap(out), ap(in_), func)]
+            return [S.activation(ap(out), ap(in_), func, bias=bias, scale=scale)]
+        add("s", fn, n, R, W, acq=acq, rel=rel)
+
+    def mm(bank, groups, R, W, own=True):
+        def fn():
+            ps = T["ps%d" % bank["k"]]
+            return [P.matmul(ps[:, sl], l, r, i == 0, i == len(items) - 1)
+                    for items in groups for i, (sl, l, r, n) in enumerate(items)]
+        add("p", fn, sum(max(64, it[3]) for items in groups for it in items), R, W, lat=100.0, acq=bank if own else None)
+
+    def iota(out, pat, base, cm, n, W, flt=False):
+        if flt:
+            add("g", lambda: [g.iota(out, pat, base, cm, allow_small_or_imprecise_dtypes=True)], 2 * n, (), W)
+        else:
+            add("g", lambda: [g.iota(out, pat, base, cm)], 2 * n, (), W)
+
+    def dma(out, in_, sem, lat, R, W):
+        add("y", lambda: [Y.dma_start(out, in_)], 0, R, W, lat=lat, sem=(sem, 16))
+
+    dma(T.sdb[:], T.sd[:], "dsd", 4300.0, (), ["sd"])
+    add("s", lambda: [S.dma_start(T.actb[:], T.act[:])], 0, (), ["act"], lat=2500.0, sem=("dact", 16))
+    dma(T.xw[:, 0:4096], T.x[:], "dx0", 7200.0, ["~sd"], ["x0"])
+    for h in range(4):
+        act(T.xw[:, K + 1024 * h:K + 1024 * (h + 1)], T.xw[:, 1024 * h:1024 * (h + 1)], F.Copy, None, None, 1024, ["x0"],
+            ["x%d" % (3 + h)])
+    fill(T.xw[:, 4096:K], 2.0 ** 62, 16, ["x1"])
+    fill(T.xw[:, K + 4096:2 * K], 2.0 ** 62, 16, ["x2"])
+
+    ci, cf = T.ci, T.cf
+    w = [T["w%d" % k] for k in range(13)]
+    SH, AND = A.logical_shift_right, A.bitwise_and
+    iota(ci[:, 5:6], [[0, 1]], 0, 1, 1, ["ci5"])
+    p_ = ci[:, 5:6]
+    ts(ci[:, 0:1], p_, 1, 7, SH, AND, 1, ["ci5"], ["ci0"])
+    ts(ci[:, 1:2], p_, 1, None, AND, None, 1, ["ci5"], ["ci1"])
+    ts(ci[:, 2:3], p_, 7, None, AND, None, 1, ["ci5"], ["ci2"])
+    ts(ci[:, 3:4], p_, 3, 1, SH, AND, 1, ["ci5"], ["ci3"])
+    ts(ci[:, 4:5], p_, 15, None, AND, None, 1, ["ci5"], ["ci4"])
+    cp(cf[:, 0:6], ci[:, 0:6], 6, ["ci%d" % k for k in range(6)], ["cf"])
+    r0a, ha, r0b, hb, p16, pp = [cf[:, k:k + 1] for k in range(6)]
+    ts(cf[:, 6:7], ha, 8.0, r0a, A.mult, A.add, 1, ["cf"], ["cf6"])
+    ts(cf[:, 7:8], cf[:, 6:7], 12.0, None, A.mult, None, 1, ["cf6"], ["cf7"])
+    iota(w[0][:], [[1, 8], [0, NB]], 7, 0, N8, ["w0"])
+    iota(w[1][:], [[0, 8], [1, NB]], 0, 0, N8, ["w1"])
+    ts(w[2][:], w[0][:], r0a, None, A.subtract, None, N8, ["w0", "cf"], ["w2"])
+    ts(w[2][:], w[2][:], 7, None, AND, None, N8, ["w2"], ["w2"])
+    ts(w[2][:], w[2][:], 192.0, cf[:, 7:8], A.mult, A.add, N8, ["w2", "cf7"], ["w2"])
+    tt(w[2][:], w[2][:], w[1][:], A.add, 2 * N8, ["w2", "w1"], ["w2"])
+    for c in range(NCH):
+        ts(T["lz%d" % c][:], w[2][:], float(NB * c), None, A.add, None, N8, ["w2"], ["lz%d" % c])
+    iota(T.pos[:], [[0, NB], [1, 16]], 0, 0, N16, ["pos"], True)
+    iota(T.qf[:], [[0, NB], [1, 8], [8, 2]], 0, 0, N16, ["qf"], True)
+    iota(T.rb[:], [[0, NB], [8192, 8], [0, 2]], 8192, 0, N16, ["rb"], True)
+    iota(T.q24[:], [[0, NB], [-512, 8], [-4096, 2]], 24 * 512, 0, N16, ["q24"], True)
+    iota(T.i144[:], [[1, 144]], 0, 0, 144, ["i144"], True)
+    ts(T.rst[:], T.pos[:], 1.0, None, A.min, None, N16, ["pos"], ["rst"])
+    fill(T.one[:], 1.0, N16 // 2, ["one"])
+    fill(T.eight[:], 8.0, N16 // 2, ["eight"])
+    ts(cf[:, 8:9], pp, p16, 15.0, A.subtract, A.add, 1, ["cf"], ["cf8"])
+    ts(T.wb[:], T.i144[:], cf[:, 8:9], None, A.is_equal, None, 144, ["i144", "cf8"], ["wb"])
+    ts(T.idf[:], T.i144[:, 0:128], pp, None, A.is_equal, None, 128, ["i144", "cf"], ["idf"])
+    idm = [T.idm[:, 128 * k:128 * k + 128] for k in range(len(SCALES))]
+    for k, val in enumerate(SCALES):
+        act(idm[k], T.idf[:], F.Identity, 0.0, val, 128, ["idf"], ["id%d" % k])
+    cp(T.lb[:, 0:NB], w[1][:, 0:NB], NB, ["w1"], ["lb"])
+    ts(T.lu[:, 0:NB], w[1][:, 0:NB], 8.0, r0a, A.mult, A.add, NB, ["w1", "cf"], ["lu"])
+    H = NB // 2
+    ts(cf[:, 9:10], hb, 16.0, 15.0, A.mult, A.add, 1, ["cf"], ["cf9"])
+    ts(cf[:, 10:11], r0b, float(N16), cf[:, 9:10], A.mult, A.add, 1, ["cf", "cf9"], ["cf10"])
+    ts(T.lm[:, 0:H], w[1][:, 0:H], 32.0, cf[:, 10:11], A.mult, A.add, H, ["w1", "cf10"], ["lm0"])
+    ts(cf[:, 11:12], p16, float(NB - 1), 16.0, A.min, A.mult, 1, ["cf"], ["cf11"])
+    ts(T.lm[:, H:H + 1], cf[:, 11:12], float(8 * N16 + 15), None, A.add, None, 1, ["cf11"], ["lm1"])
+    iota(w[3][:, 0:7 * H], [[1, 7], [0, H]], 1, 0, 7 * H, ["w3"])
+    iota(w[4][:, 0:7 * H], [[0, 7], [32, H]], 0, 0, 7 * H, ["w4"])
+    ts(cf[:, 13:14], r0b, 2.0, cf[:, 9:10], A.mult, A.add, 1, ["cf", "cf9"], ["cf13"])
+    a3 = w[3][:, 0:7 * H]
+    ts(a3, a3, r0b, None, A.add, None, 7 * H, ["w3", "cf"], ["w3"])
+    ts(a3, a3, 7, None, AND, None, 7 * H, ["w3"], ["w3"])
+    ts(a3, a3, float(N16), cf[:, 13:14], A.mult, A.add, 7 * H, ["w3", "cf13"], ["w3"])
+    tt(a3, a3, w[4][:, 0:7 * H], A.add, 14 * H, ["w3", "w4"], ["w3"])
+    ts(T.ld[:, 0:7 * H], a3, -14.0, None, A.add, None, 7 * H, ["w3"], ["ld"])
+    ts(w[8][:], w[1][:], 16.0, p16, A.mult, A.add, N8, ["w1", "cf"], ["w8"])
+    act(w[9][:], w[8][:], F.Identity, 0.5 / NB - 0.5, 1.0 / NB, N8, ["w8"], ["w9"])
+    cp(w[5][:], w[9][:], N8, ["w9"], ["w5"])
+    ts(w[10][:], w[5][:], 8.0, -15.0, A.is_ge, A.mult, N8, ["w5"], ["w10"])
+    ts(w[11][:], w[5][:], 2.0 - 16 * NB, None, A.mult, None, N8, ["w5"], ["w11"])
+    act(w[12][:], w[8][:], F.Identity, 0.0, 16.0, N8, ["w8"], ["w12"])
+    tt(w[10][:], w[10][:], w[11][:], A.add, 2 * N8, ["w10", "w11"], ["w10"])
+    tt(w[10][:], w[10][:], w[12][:], A.add, 2 * N8, ["w10", "w12"], ["w10"])
+    cp(T.ln[:, 0:NB], w[10][:, 0:NB], NB, ["w10"], ["ln"])
+    tt(w[6][:], w[5][:], w[0][:], A.add, 2 * N8, ["w5", "w0"], ["w6"])
+    ts(w[6][:], w[6][:], 2.0, None, A.add, None, N8, ["w6"], ["w6"])
+    ts(w[6][:], w[6][:], 7, None, AND, None, N8, ["w6"], ["w6"])
+    ts(w[11][:], w[6][:], float(N16), None, A.mult, None, N8, ["w6"], ["w11"])
+    tt(w[11][:], w[11][:], w[10][:], A.add, 2 * N8, ["w11", "w10"], ["w11"])
+    cp(T.lf[:], w[11][:], N8, ["w11"], ["lf"])
+
+    for c in range(NCH):
+        chain(c, T, g, add, ts, tt, cp, fill, scan, act, mm, idm, rid, pid, emask)
+
+    dma(T.yp[:], T.ypb[:], "dyp", 2000.0, ["yp%d" % c for c in range(NCH)], ())
+    dma(T.yc[:], T.ycb[:], "dyc", 2000.0, ["yc%d" % c for c in range(NCH)], ())
+    for h in range(4):
+        dma(T.ys[:, 384 * h:384 * (h + 1)], T.ysb[:, 32 * h:32 * (h + 1), :], "dy%d" % h, 2500.0,
+            ["ys%d_%d" % (c, h) for c in range(NCH)], ())
+
+
+def chain(c, T, g, add, ts, tt, cp, fill, scan, act, mm, idm, rid, pid, emask):
+    b = {n: T["%s%d" % (n, c)] for n, _w, _d in PER_CHAIN}
+    XR = ["x%d" % i for i in range(7)]
+    SH, AND = A.logical_shift_right, A.bitwise_and
+
+    def k(*names):
+        return ["%s@%d" % (n, c) for n in names]
+
+    def ids(*which):
+        return ["id%d" % i for i in which]
+
+    st, sel, lo, si, sf, pb, mi = [b[n] for n in ("st", "sel", "lo", "si", "sf", "pb", "mi")]
+    rows = ["st%d" % r for r in range(8)]
+    lbl, lul = T.lb[:, 0:NB], T.lu[:, 0:NB]
+
+    def rg(i, n=1):
+        return slice(i * N16, (i + n) * N16)
+
+    def row(buf, r, n=1):
+        return buf[:, rg(r, n)]
+
+    def small(buf, i):
+        return buf[:, 16 * i:16 * i + NB]
+
+    def spread(src, key):
+        bank = {}
+        mm(bank, [[(rg(i), idm[0], src, N16)] for i in range(4)], k(key) + ids(0), k(key + "4"))
+        return bank
+
+    def lift(t, cb):
+        tt(b["t0"][:], sf[:, 0:16].indirect(lbl), T.pos[:], A.subtract, -N16, k("sf0") + ["pos", "lb"], k("t0"))
+        act(b["sn"][:], b["t0"][:], F.Sign, -0.5, -1.0, N16, k("t0"), k("sn"))
+        act(row(st, 8), (cb, N16, 2 * N16), F.Copy, None, None, N16, k("cn"), k("st8"))
+        bank = {}
+        mm(bank, [[(rg(i), idm[10], b["sn"][:], N16), (rg(i), idm[11], T.one[:], N16)] for i in range(5)],
+           k("sn") + ids(10, 11) + ["one"], k("dl"))
+        scan(row(lo, 0, 4), (bank, 0, 4 * N16), row(st, 0, 4), A.add, A.max, 4 * N16, k("dl", *rows[0:4]), k("lo0"))
+        scan(row(lo, 4, 5), (bank, 0, 5 * N16), row(st, 4, 5), A.add, A.max, 5 * N16, k("dl", "st8", "~lo0", *rows[4:8]),
+             k("lo1"), rel=bank)
+        cp(b["mr"][:], lo[:, :].indirect(T.lm[:, 0:MW // 16]), -MW, k("lo0", "lo1") + ["lm0", "lm1"], k("mr"))
+        mo = b["mo"][:, t * MW:(t + 1) * MW]
+        ts(mo, b["mr"][:], int(B) - 1, None, AND, None, MW, k("mr"), k("mo%d" % t))
+        sem = "arr%d_%d" % (c, t)
+        add("g", lambda: [g.remote_dma(mi[:, t * MW:(t + 1) * MW], mo, T.sem[sem], T.sem.sent, pid, rid, emask)],
+            200, k("mo%d" % t), k("mi%d" % t), lat=3000.0, sem=(sem, -NENG))
+        act(b["nb"][:], b["t0"][:], F.Abs, 0.0, 8 * B, N16, k("t0"), k("nb"))
+        tt(row(b["c16"], t), b["nb"][:], (cb, 0, N16), A.min, N16, k("cn", "nb", "st8"), k("c16_%d" % t), rel=cb)
+
+    def targets(ub, u0, shift, rpb, put):
+        for r0 in range(0, 8, rpb):
+            bank = {}
+            for r in range(r0, r0 + rpb):
+                act((bank, (r - r0) * N16, (r - r0 + 1) * N16), (ub, u0, u0 + N16), F.Abs, -B * (r + shift), 1.0, N16,
+                    k("uu") + (k("~tr%d" % (r - 1)) if r > 0 else []), k("tr%d" % r), acq=bank if r == r0 else None,
+                    rel=ub if r == 7 else None)
+            put(r0, rpb, bank, k(*["tr%d" % r for r in range(r0, r0 + rpb)]))
+
+    fill(b["dsel"][:], -128 * B, N16 // 2, k("dsel"))
+    fill(pb[:, 0:16], 0.0, 16, k("pb0"))
+    fill(sf[:, 0:16], 0.0, 16, k("sf0"))
+    for h in range(2):
+        cp(row(st, 4 * h, 4), T.sdb[:, :].indirect(b["lz"][:, 4 * h * NB:4 * (h + 1) * NB]), -4 * N16, ["sd", "lz%d" % c],
+           k(*rows[4 * h:4 * h + 4]))
+        act(row(b["sg"], 4 * h, 4), row(st, 4 * h, 4), F.Sign, EMPTY - 0.5, -1.0, 4 * N16, k(*rows[4 * h:4 * h + 4]),
+            k("sgi%d" % h))
+    cb = {}
+    mm(cb, [[(rg(1), idm[8], T.qf[:], N16), (rg(1), idm[7], T.eight[:], N16)]
+            + [(rg(1), idm[7], row(b["sg"], r), N16) for r in range(8)],
+            [(rg(0), idm[5], T.eight[:], N16)] + [(rg(0), idm[5], row(b["sg"], r), N16) for r in range(8)]],
+       k("sgi0", "sgi1") + ids(5, 7, 8) + ["qf", "eight"], k("cn", "cnt0"))
+    ac = T.actb[:, NB * c:NB * (c + 1)]
+    ts(small(sf, 2), ac, 8.0, 15.0, A.is_ge, A.mult, NB, ["act"], k("sf2"))
+    ts(small(sf, 3), ac, 2.0, None, A.mult, None, NB, ["act"], k("sf3"))
+    tt(small(sf, 0), small(sf, 3), small(sf, 2), A.subtract, 2 * NB, k("sf2", "sf3"), k("sf0"))
+    lift(0, cb)
+
+    for t in range(3):
+        m0 = t * MW
+        MI = k("mi%d" % t)
+        cv = CV[c][t]
+        ncol = 7 * N8
+        cp(b["aoff"][:], mi[:, m0:m0 + N8], N8, MI, k("aoff"))
+        act(b["fa"][:], T.xw[:, 0:K].indirect(b["aoff"][:, :]), F.Copy, None, None, -16 * N8, k("aoff") + XR[0:2], k("fa"))
+        tt(b["ti"][:], mi[:, m0 + N8:m0 + MW].indirect(lbl), T.q24[:], A.add, -N16, MI + ["q24", "lb"], k("ti"))
+        ts(b["ns"][:], b["ti"][:], 4096, None, AND, None, N16, k("ti"), k("ns"))
+        ts(b["dsel"][:, 1::2], b["ns"][:, 1::2], K / 2048.0, float(K), A.mult, A.subtract, N8, k("ns"), k("dsel"))
+        bank = spread(b["dsel"][:], "dsel")
+        for h in range(2):
+            scan(row(sel, 4 * h, 4), (bank, 0, 4 * N16), row(st, 4 * h, 4), A.add, A.max, 4 * N16,
+                 k("dsel4", *rows[4 * h:4 * h + 4]) + (k("~sel0") if h else []),
+                 k(*["sel%d" % r for r in range(4 * h, 4 * h + 4)]), rel=bank if h else None)
+        cp(b["off"][:], sel[:, :].indirect(T.ld[:, 0:7 * NB // 2]), -ncol, k("sel0", "sel4") + ["ld"], k("off"))
+        pieces = []
+        c0 = 0
+        while c0 < cv:
+            c1 = min(cv, (c0 // N8 + 1) * N8)
+            f0 = (c0 % N8) * 16
+            tt(b["cm"][:, 16 * c0:16 * c1], T.xw[:, :].indirect(b["off"][:, c0:c1]), b["fa"][:, f0:f0 + 16 * (c1 - c0)],
+               A.is_lt, -16 * (c1 - c0), k("off", "fa") + XR, k("cm%d" % c0))
+            pieces.append((c0, c1, 0))
+            c0 = c1
+        while c0 < ncol:
+            c1 = min(ncol, c0 + GCOL)
+            act(b["fs"][:, 16 * c0:16 * c1], T.xw[:, :].indirect(b["off"][:, c0:c1]), F.Copy, None, None,
+                -16 * (c1 - c0), k("off") + XR, k("fs%d" % c0))
+            d0 = c0
+            while d0 < c1:
+                d1 = min(c1, d0 + 32)
+                bank = {}
+                items = [(slice(0, 16 * (d1 - d0)), idm[1], b["fs"][:, 16 * d0:16 * d1], 16 * (d1 - d0))]
+                e0 = d0
+                while e0 < d1:
+                    e1 = min(d1, (e0 // N8 + 1) * N8)
+                    f0 = (e0 % N8) * 16
+                    items.append((slice(16 * (e0 - d0), 16 * (e1 - d0)), idm[0], b["fa"][:, f0:f0 + 16 * (e1 - e0)],
+                                  16 * (e1 - e0)))
+                    e0 = e1
+                mm(bank, [items], k("fs%d" % c0, "fa") + ids(0, 1), k("df%d" % d0))
+                act(b["cm"][:, 16 * d0:16 * d1], (bank, 0, 16 * (d1 - d0)), F.Sign, -2.0 ** -68, 1.0, 16 * (d1 - d0),
+                    k("df%d" % d0), k("cm%d" % d0), rel=bank)
+                pieces.append((d0, d1, 1))
+                d0 = d1
+            c0 = c1
+        groups = []
+        for kind in range(2):
+            mine = [p for p in pieces if p[2] == kind]
+            cur = []
+            for i, p in enumerate(mine):
+                cur.append(p)
+                if cur[-1][1] - cur[0][0] >= GC and (i == len(mine) - 1 or mine[-1][1] - p[1] >= 32):
+                    groups.append(cur)
+                    cur = []
+            if cur:
+                groups.append(cur)
+        sgk = []
+        for gr in groups:
+            g0, g1 = gr[0][0], gr[-1][1]
+            bank = {}
+            mm(bank, [[(slice(0, g1 - g0), T.wb[:, 15 - i:143 - i], b["cm"][:, 16 * g0 + i:16 * g1:16], g1 - g0)
+                       for i in range(16)]], k(*["cm%d" % p[0] for p in gr]) + ["wb"], k("ct%d" % g0))
+            act(b["sg"][:, g0:g1], (bank, 0, g1 - g0), F.Sign, -1.0 if gr[0][2] else -8.5, 1.0, g1 - g0,
+                k("ct%d" % g0, "cnt0"), k("sg%d_%d" % (t, g0)), rel=bank)
+            sgk.append("sg%d_%d" % (t, g0))
+        c16 = row(b["c16"], t)
+        at = row(b["at"], t)
+        AT = k("at%d" % t)
+        wd = mi[:, m0 + N8:m0 + N8 + NB]
+        tt(b["a16"][:], mi[:, m0:m0 + N8].indirect(lul), b["ns"][:], A.max, -N16, MI + k("ns") + ["lu"], k("a16"))
+        act(b["hs"][:], b["a16"][:], F.Sign, EMPTY - 0.5, -1.0, N16, k("a16"), k("hs"))
+        ts(b["cl"][:], c16, B, 7 * B, A.max, A.min, N16 // 2, k("c16_%d" % t), k("cl"))
+        ts(small(si, 1), wd, 3, 14, SH, AND, NB, MI, k("si1"))
+        ts(small(si, 2), wd, 7, 1, SH, AND, NB, MI, k("si2"))
+        tt(small(pb, 0), small(si, 1), small(si, 2), A.add, 2 * NB, k("si1", "si2"), k("pb0"))
+        tt(b["oh"][:], pb[:, 0:16].indirect(lbl), T.pos[:], A.is_equal, -N16, k("pb0") + ["pos", "lb"], k("oh"))
+        if t == 2:
+            ts(small(si, 3), wd, 4, 15, SH, AND, NB, MI, k("si3"))
+            cp(small(pb, 1), small(si, 3), NB, k("si3"), k("pb1"))
+        db = {}
+        items = [(rg(0), idm[2], c16, N16), (rg(0), idm[3], b["cl"][:], N16), (rg(0), idm[4], b["hs"][:], N16)]
+        for s in range(7):
+            for h in range(2):
+                items.append((slice(h, N16, 2), idm[0], b["sg"][:, s * N8:(s + 1) * N8], N8))
+        mm(db, [items], k("c16_%d" % t, "cl", "hs", *sgk) + ids(0, 2, 3, 4), k("dd"))
+        keep = (db, N16, 2 * N16)
+        act(keep, (db, 0, N16), F.Relu, 94 * 8 * B, -8 * B, N16, k("dd"), k("keep"))
+        tt(at, c16, keep, A.min, N16, k("c16_%d" % t, "keep"), AT)
+        tt(b["pr"][:], b["oh"][:], keep, A.min, N16, k("oh", "keep", "~at%d" % t), k("pr"), rel=db)
+        xb = {}
+        mm(xb, [[(slice(0, NB), idm[0], small(pb, t // 2), NB)]
+                + [(slice(0, NB), idm[12], b["pr"][:, i::16], NB) for i in range(16)]], k("pr", "pb0", "pb1") + ids(0, 12),
+           k("xs"))
+        ub = {}
+        if t < 2:
+            act(small(sf, 0), (xb, 0, NB), F.Abs, -15.0, 1.0, NB, k("xs"), k("sf0"), rel=xb)
+            mm(ub, [[(rg(0), idm[0], at, N16), (rg(0), idm[0], T.rb[:], N16)]], AT + ["rb"], k("v1", "uu"))
+            act(b["es"][:], (ub, 0, N16), F.Sign, -7.5 * B, 1.0, N16, k("v1"), k("es"))
+            mm(ub, [[(rg(1), T.idf[:], b["a16"][:], 4 * N16), (rg(1), idm[0], at, N16), (rg(1), idm[0], T.rb[:], N16),
+                     (rg(1), idm[9], b["es"][:], N16)]], AT + k("a16", "es") + ids(9), k("uu"), own=False)
+            cb = {}
+            mm(cb, [[(rg(1), idm[6], at, N16), (rg(1), idm[7], b["hs"][:], N16), (rg(1), idm[7], T.one[:], N16),
+                     (rg(1), idm[8], T.qf[:], N16)],
+                    [(rg(0), idm[0], at, N16), (rg(0), idm[5], b["hs"][:], N16), (rg(0), idm[5], T.one[:], N16)]],
+               AT + k("hs") + ids(6), k("cn"))
+            act(b["clr"][:], at, F.Relu, EMPTY, -1.0, N16, AT, k("clr"))
+            eb = spread(b["clr"][:], "clr")
+            for h in range(2):
+                blk = row(st, 4 * h, 4)
+                tt(blk, blk, (eb, 0, 4 * N16), A.max, 4 * N16, k("clr4", *rows[4 * h:4 * h + 4]) + (k("~st0") if h else []),
+                   k(*rows[4 * h:4 * h + 4]), rel=eb if h else None)
+
+            def put(r0, n, bank, keys):
+                blk = row(st, r0, n)
+                tt(blk, blk, (bank, 0, n * N16), A.min, n * N16, k(*rows[r0:r0 + n]) + keys, k(*rows[r0:r0 + n]), rel=bank)
+            targets(ub, N16, 4, 4, put)
+            lift(t + 1, cb)
+        else:
+            act(T.ypb[:, NB * c:NB * (c + 1)], (xb, 0, NB), F.Abs, -15.0, 1.0, NB, k("xs"), ["yp%d" % c], rel=xb)
+            lnl = T.ln[:, 0:NB]
+            act(b["an"][:], b["a16"][:, :].indirect(lnl), F.Copy, None, None, -N16, k("a16") + ["ln"], k("an"))
+            act(b["es"][:], at.indirect(lnl), F.Copy, None, None, -N16, AT + ["ln"], k("es"))
+            act(b["clr"][:], b["es"][:], F.Relu, EMPTY, -1.0, N16, k("es"), k("clr"))
+            eb = spread(b["clr"][:], "clr")
+            mm(ub, [[(rg(0), T.idf[:], b["an"][:], 4 * N16), (rg(0), idm[0], b["es"][:], N16)]], k("an", "es"), k("uu"))
+            for h in range(2):
+                blk = row(sel, 4 * h, 4)
+                act(blk, st[:, 0:8 * N16].indirect(T.lf[:, 4 * h * NB:4 * (h + 1) * NB]), F.Copy, None, None, -4 * N16,
+                    k("off", *rows) + ["lf"], k("fi%d" % h))
+                tt(blk, blk, (eb, 0, 4 * N16), A.max, 4 * N16, k("clr4", "fi%d" % h) + (k("~fin0") if h else []),
+                   k("fin%d" % h), rel=eb if h else None)
+
+            def put(r0, n, bank, keys):
+                tt(T.ysb[:, 16 * r0:16 * (r0 + n), NB * c:NB * (c + 1)], row(sel, r0, n), (bank, 0, n * N16), A.min, n * N16,
+                   k("fin%d" % (r0 // 4)) + keys, ["ys%d_%d" % (c, r0 // 2)], rel=bank)
+            targets(ub, 0, 0, 2, put)
+            sb = {}
+            items = []
+            for u in range(3):
+                items.append((rg(0), idm[0], row(b["c16"], u), N16))
+                items.append((rg(0), idm[1], row(b["at"], u), N16))
+            mm(sb, [items], k("c16_0", "c16_1", "c16_2", "at0", "at1", "at2"), k("sc"))
+            scan(b["t0"][:], T.rst[:], (sb, 0, N16), A.mult, A.add, N16, k("sc") + ["rst"], k("t0"), rel=sb)
+            act(T.ycb[:, NB * c:NB * (c + 1)], b["t0"][:, 15::16], F.Identity, 0.0, 1.0 / B, NB, k("t0"), ["yc%d" % c])
+
+
+def costs(ops, case):
+    cy, gg, pe, fv, fs, wake, lf = case
+    out = []
+    for o in ops:
+        e, n = o["eng"], o["n"]
+        if e == "p":
+            out.append(20.0 + n * pe)
+        elif e in "vs":
+            out.append((fv if e == "v" else fs) + (max(64, n) if n >= 0 else -n * gg + 20) * cy)
+        else:
+            out.append(160.0 + n * cy if e == "g" else 60.0)
+    return out
+
+
+def schedule(ops, succ, busy, prio):
+    wake = CASES[0][5]
+    n = len(ops)
+    left = [len(o["deps"] | o["soft"]) for o in ops]
+    ready = [i for i in range(n) if left[i] == 0]
+    rt = [0.0] * n
+    free = {e: 0.0 for e in "vspgy"}
+    banks = [[0.0, (), True] for _ in range(8)]
+    order, pick, after = [], {}, {}
+    while ready:
+        av = [j for j in range(8) if banks[j][2]]
+        kb = min(av, key=lambda j: banks[j][0]) if av else None
+        best = None
+        for i in ready:
+            o = ops[i]
+            s = max(rt[i], free[o["eng"]])
+            if o["acq"] is not None:
+                if kb is None:
+                    continue
+                s = max(s, banks[kb][0])
+            key = s - 0.005 * prio[i]
+            if best is None or key < best[0]:
+                best = (key, i, s)
+        if best is None:
+            return None
+        key, i, s = best
+        o = ops[i]
+        if o["acq"] is not None:
+            o["acq"]["k"] = pick[i] = kb
+            after[i] = banks[kb][1]
+            banks[kb][2] = False
+        free[o["eng"]] = s + busy[i]
+        fin = s + busy[i] + o["lat"] + wake
+        if o["rel"] is not None:
+            banks[o["rel"]["k"]] = [fin, [i] + list(o["soft"]), True]
+        ready.remove(i)
+        order.append(i)
+        for j in succ[i]:
+            rt[j] = max(rt[j], fin if i in ops[j]["deps"] else s + busy[i])
+            left[j] -= 1
+            if left[j] == 0:
+                ready.append(j)
+    return order, pick, after
+
+
+def replay(ops, order, after, busy, case):
+    fin = {}
+    free = {e: 0.0 for e in "vspgy"}
+    for i in order:
+        o = ops[i]
+        s = free[o["eng"]]
+        for d in o["deps"]:
+            s = max(s, fin[d])
+        for d in after.get(i, ()):
+            s = max(s, fin[d])
+        free[o["eng"]] = s + busy[i]
+        fin[i] = s + busy[i] + o["lat"] * case[6] + case[5]
+    return max(fin.values())
+
+
+def plan(ops):
+    n = len(ops)
+    succ = [[] for _ in range(n)]
+    for i, o in enumerate(ops):
+        for d in o["deps"] | o["soft"]:
+            succ[d].append(i)
+    busy = [costs(ops, case) for case in CASES]
+    prio = [0.0] * n
+    for i in range(n - 1, -1, -1):
+        prio[i] = busy[0][i] + ops[i]["lat"] + max([prio[j] + CASES[0][5] for j in succ[i]] or [0.0])
+    kinds = {}
+    for i, o in enumerate(ops):
+        kinds.setdefault(o["nm"][:2] + o["nm"][-2:], []).append(i)
+        if "@" in o["nm"]:
+            prio[i] -= LAG * int(o["nm"][-1])
+    kinds = [kinds[q] for q in sorted(kinds)]
+    seed = [12345]
+
+    def rnd():
+        seed[0] = (seed[0] * 1103515245 + 12345) % 2147483648
+        return seed[0] / 2147483648.0
+
+    best = None
+    for it in range(TRIES):
+        p = list(prio)
+        for _ in range((1, 3, 8)[int(rnd() * 3)] if it else 0):
+            d = (rnd() + rnd() - 1.0) * (4000.0, 16000.0, 40000.0)[int(rnd() * 3)]
+            for i in (kinds[int(rnd() * len(kinds))] if rnd() < 0.3 else [int(rnd() * n)]):
+                p[i] += d
+        got = schedule(ops, succ, busy[0], p)
+        if got is None:
+            continue
+        times = [replay(ops, got[0], got[2], busy[u], CASES[u]) for u in range(len(CASES))]
+        val = sum(times) + times[0]
+        if best is None or val <= best[0] + 100.0:
+            best = (val, got, times)
+            prio = p
+    return best
+
+
+def rank_program(g, core, T, topo):
+    if T.rank_of(core) is None:
+        return
+    ops = []
+    build(g, T, topo, core, ops)
+    if "p" not in PLAN:
+        PLAN["p"] = plan(ops)
+    order, pick, after = PLAN["p"][1]
+    queue = {"v": g.vector, "s": g.scalar, "p": g.tensor, "g": g, "y": g.sync}
+    total = {}
+    known = {e: {} for e in queue}
+    for at, i in enumerate(order):
+        o = ops[i]
+        e = o["eng"]
+        kn = known[e]
+        o["at"] = at
+        if i in pick:
+            o["acq"]["k"] = pick[i]
+        need = {}
+        for d in list(o["deps"]) + list(after.get(i, ())):
+            s, v = ops[d]["done"]
+            need[s] = max(need.get(s, (0, 0)), (v, d))
+        for s, (v, d) in sorted(need.items(), key=lambda it: -ops[it[1][1]]["at"]):
+            if kn.get(s, 0) < v:
+                queue[e].wait_ge(T.sem[s], v)
+                kn[s] = v
+                for s2, v2 in ops[d]["seen"].items():
+                    kn[s2] = max(kn.get(s2, 0), v2)
+        o["seen"] = dict(kn)
+        ins = o["fn"]()
+        if o["sem"] is None:
+            s = "c" + e
+            for x in ins:
+                x.then_inc(T.sem[s], 1)
+            total[s] = total.get(s, 0) + len(ins)
+            o["done"] = (s, total[s])
+        else:
+            s, v = o["sem"]
+            if v > 0:
+                ins[0].then_inc(T.sem[s], v)
+            else:
+                v = -v
+                total["sent"] = total.get("sent", 0) + v
+                o["seen"] = {}
+            total[s] = v
+            o["done"] = (s, v)
+    for s, v in total.items():
+        g.wait_ge(T.sem[s], v)

@@ -7,49 +7,60 @@ NCH = 2
 NB = 12 // NCH
 N8 = 8 * NB
 N16 = 16 * NB
-MW = N8 + 16
-CV = [[224, 224, 224], [224, 224, 224]]
+MR = NB + NB // 2
+CV = [[208, 208, 208], [208, 208, 208]]
 GCOL = 64
-GC = 100
+GL = (2, 0)
 NENG = 8
-K = 4128
-B = 8192.0
-EMPTY = 4096.0
-SCALES = (1.0, -1.0, 100.0 / B, -101.0 / B, 100.0, B / 2, 1.0 / 512, 8.0, 528.0, -4 * B, 16 * B, -15 * B, 15.0)
+NROWED = 2
+PAD = 16
+MID = 2048.0
+B = 4160.0
+CAP = 37632.0
+BIG = 2.0 ** 19
+OWN = 2.0 ** 17
+WB = (1.0, -1.0, 0.5, -0.5, 8.0, -8.0, -8.5, 16.0, -16.0, B, -B, B / 2, -B / 2, CAP / 2, -CAP / 2,
+      BIG, -BIG, BIG / 2, -BIG / 2, OWN, -OWN, 1.0 / 8192)
+WH = (1.0, -1.0, BIG / 16, -BIG / 16)
 
 SCRATCH = {n: ("sbuf", [128, w], d) for n, w, d in (
-    ("xw", 2 * K, "bfloat16"), ("sdb", 1536, "int32"), ("actb", 12, "int32"), ("ypb", 12, "float32"),
+    ("xw", 4096 + 2 * PAD, "bfloat16"), ("actb", 16, "int32"), ("ypb", 12, "float32"),
     ("ycb", 12, "float32"), ("ci", 8, "int32"), ("cf", 16, "float32"), ("i144", 144, "float32"), ("wb", 144, "bfloat16"),
-    ("idm", 128 * len(SCALES), "bfloat16"), ("idf", 128, "float32"), ("pos", N16, "float32"), ("qf", N16, "bfloat16"),
-    ("q24", N16, "float32"), ("rb", N16, "bfloat16"), ("rst", N16, "float32"), ("one", N16, "bfloat16"),
-    ("eight", N16, "bfloat16"), ("lb", 16, "uint16"), ("lu", 16, "uint16"), ("lm", 16, "uint16"), ("ln", 16, "uint16"),
-    ("ld", 48, "uint16"), ("lf", N8, "uint16"))}
+    ("idb", 128 * len(WB), "bfloat16"), ("idh", 128 * len(WH), "float16"), ("idf", 128, "float32"),
+    ("pos", N16, "float32"), ("rst", N16, "float32"), ("one", N16, "bfloat16"), ("odd", N16, "bfloat16"),
+    ("rs2", 4 * N16, "bfloat16"), ("rs16", 4 * N16, "bfloat16"),
+    ("lb", 8 * NCH, "uint16"), ("lm", 16, "uint16"), ("w0", 8 * NCH, "int32"), ("w1", 16, "int32"))}
+SCRATCH["upp"] = ("sbuf", [128, NB, 16], "bfloat16")
+SCRATCH["sdb"] = ("sbuf", [128, 128, 12], "int32")
 SCRATCH["ysb"] = ("sbuf", [128, 128, 12], "float32")
-for _k in range(13):
-    SCRATCH["w%d" % _k] = ("sbuf", [128, N8], "int32" if _k < 8 else "float32")
 PER_CHAIN = (
-    ("lz", N8, "uint16"), ("st", 9 * N16, "float32"), ("sel", 8 * N16, "float32"), ("lo", 9 * N16, "float32"),
-    ("off", 7 * N8, "uint16"), ("aoff", N8, "uint16"), ("fa", 16 * N8, "bfloat16"), ("fs", 112 * N8, "bfloat16"),
-    ("cm", 112 * N8, "bfloat16"), ("sg", 8 * N16, "bfloat16"), ("mo", 3 * MW, "int32"), ("mi", 3 * MW, "int32"),
-    ("mr", MW, "int32"), ("ti", N16, "int32"), ("ns", N16, "int32"), ("dsel", N16, "bfloat16"), ("sn", N16, "bfloat16"),
-    ("clr", N16, "bfloat16"), ("pb", 32, "bfloat16"), ("a16", N16, "float32"), ("cl", N16, "bfloat16"),
-    ("c16", 3 * N16, "bfloat16"), ("at", 3 * N16, "bfloat16"), ("hs", N16, "bfloat16"), ("es", N16, "bfloat16"),
-    ("oh", N16, "float32"), ("nb", N16, "float32"), ("an", N16, "float32"), ("pr", N16, "bfloat16"),
-    ("t0", N16, "float32"), ("si", 64, "int32"), ("sf", 64, "float32"))
+    ("st", [8 * NB, 16], "float16"), ("em", [8 * N16], "bfloat16"), ("lo", [8 * N16], "float32"),
+    ("sel", [7 * N16], "float32"), ("off", [7 * N8], "uint16"), ("aoff", [N8], "uint16"), ("fa", [16 * N8], "bfloat16"),
+    ("fs", [112 * N8], "bfloat16"), ("cm", [112 * N8], "bfloat16"), ("sg", [7 * N8], "bfloat16"),
+    ("mo", [48 * MR], "float16"), ("mi", [3 * MR, 16], "float16"), ("mr", [2 * N8], "float32"),
+    ("no", [3 * NB, 16], "bfloat16"), ("mk", [N16], "bfloat16"), ("a16", [N16], "float16"),
+    ("hs", [3 * NB, 16], "bfloat16"), ("cs", [3 * N16], "bfloat16"), ("ee", [6 * NB, 16], "bfloat16"),
+    ("ct", [3 * N16], "bfloat16"), ("z8", [N16], "bfloat16"), ("la", [N16], "bfloat16"),
+    ("t0", [2 * N16], "float32"))
 for _c in range(NCH):
     for _n, _w, _d in PER_CHAIN:
-        SCRATCH["%s%d" % (_n, _c)] = ("sbuf", [128, _w], _d)
+        SCRATCH["%s%d" % (_n, _c)] = ("sbuf", [128] + _w, _d)
 for _k in range(8):
-    SCRATCH["ps%d" % _k] = ("psum", [128, 512], "float32")
+    SCRATCH["ps%d" % _k] = ("psum", [128, 32, 16] if _k < NROWED else [128, 512], "float32")
 
-SEMAPHORES = (["cv", "cs", "cp", "cg", "sent", "dact", "dsd", "dx0", "dyp", "dyc"] + ["dy%d" % h for h in range(4)]
-              + ["arr%d_%d" % (c, t) for c in range(NCH) for t in range(3)])
+SEMAPHORES = (["cv", "cs", "cp", "cg", "sent", "dact", "dsd", "dx0", "dyp", "dyc"] + ["dy%d" % h for h in range(2)]
+              + ["%s%d_%d" % (n, c, t) for n in ("arr", "ars") for c in range(NCH) for t in range(3)])
 
-CASES = ((1.04, 1.56, 0.5, 40.0, 75.0, 90.0, 1.0), (0.9, 1.1, 0.45, 20.0, 60.0, 60.0, 0.9),
-         (1.15, 2.0, 0.6, 50.0, 90.0, 120.0, 1.2), (1.04, 1.56, 0.8, 60.0, 150.0, 250.0, 1.3))
-LAG = 5000.0
-TRIES = 2500
+CASES = ((0.9, 1.56, 0.45, 50.0, 65.0, 70.0, 0.9), (1.05, 1.15, 0.525, 50.0, 65.0, 90.0, 1.0),
+         (1.1, 2.0, 0.55, 50.0, 65.0, 70.0, 0.75))
+LAG = 6000.0
+BULK = 12000.0
+TRIES = 300
+MOVES = 40000
+HEAT = 150.0
+WAIT = 60.0
 PLAN = {}
+ALL = slice(0, 16)
 
 
 def build(g, T, topo, core, ops):
@@ -60,10 +71,8 @@ def build(g, T, topo, core, ops):
     V, S, P, Y = g.vector, g.scalar, g.tensor, g.sync
     last_w, readers = {}, {}
 
-    def add(eng, fn, n, R=(), W=(), lat=0.0, sem=None, acq=None, rel=None):
+    def add(eng, fn, n, R=(), W=(), lat=0.0, sem=None, banks=(), rel=None):
         i = len(ops)
-        soft = {last_w[k[1:]] for k in R if k[0] == "~"}
-        R = [k for k in R if k[0] != "~"]
         deps = {last_w[k] for k in list(R) + list(W) if k in last_w}
         for k in W:
             deps.update(readers.get(k, ()))
@@ -72,21 +81,38 @@ def build(g, T, topo, core, ops):
         for k in W:
             last_w[k] = i
             readers[k] = []
+        soft, acq = set(), None
+        for bank in banks:
+            if "users" not in bank:
+                bank["users"] = []
+                acq = bank
+            for j in bank["users"]:
+                (soft if ops[j]["eng"] == eng else deps).add(j)
+            bank["users"].append(i)
         deps.discard(i)
+        soft.discard(i)
         ops.append({"eng": eng, "fn": fn, "n": n, "lat": lat, "deps": deps, "sem": sem, "soft": soft,
                     "nm": (list(W) + ["-"])[0], "acq": acq, "rel": rel})
 
     def ap(x):
-        return T["ps%d" % x[0]["k"]][:, x[1]:x[2]] if isinstance(x, tuple) else x
+        if not isinstance(x, tuple):
+            return x
+        bank, rs, cs = x
+        if bank["k"] < NROWED:
+            return T["ps%d" % bank["k"]][:, rs, cs]
+        return T["ps%d" % bank["k"]][:, 16 * rs.start + cs.start:16 * rs.stop:cs.step or 1]
 
-    def ts(out, in0, s1, s2, o0, o1, n, R, W):
+    def bk(*xs):
+        return [x[0] for x in xs if isinstance(x, tuple)]
+
+    def ts(out, in0, s1, s2, o0, o1, n, R, W, rel=None):
         if o1 is None:
-            add("v", lambda: [V.tensor_scalar(out, in0, s1, None, o0)], n, R, W)
+            add("v", lambda: [V.tensor_scalar(out, ap(in0), s1, None, o0)], n, R, W, banks=bk(in0), rel=rel)
         else:
-            add("v", lambda: [V.tensor_scalar(out, in0, s1, s2, o0, o1)], n, R, W)
+            add("v", lambda: [V.tensor_scalar(out, ap(in0), s1, s2, o0, o1)], n, R, W, banks=bk(in0), rel=rel)
 
     def tt(out, in0, in1, op, n, R, W, rel=None):
-        add("v", lambda: [V.tensor_tensor(out, in0, ap(in1), op)], n, R, W, rel=rel)
+        add("v", lambda: [V.tensor_tensor(out, in0, ap(in1), op)], n, R, W, banks=bk(in1), rel=rel)
 
     def cp(out, in_, n, R, W):
         add("v", lambda: [V.tensor_copy(out, in_)], n, R, W)
@@ -95,21 +121,26 @@ def build(g, T, topo, core, ops):
         add("v", lambda: [V.memset(out, val)], n, (), W)
 
     def scan(out, d0, d1, o0, o1, n, R, W, rel=None):
-        add("v", lambda: [V.tensor_tensor_scan(out, ap(d0), ap(d1), 0.0, o0, o1)], n, R, W, rel=rel)
+        for bank in bk(d1):
+            bank["rowed"] = False
+        add("v", lambda: [V.tensor_tensor_scan(out, d0, ap(d1), 0.0, o0, o1)], n, R, W, banks=bk(d1), rel=rel)
 
-    def act(out, in_, func, bias, scale, n, R, W, acq=None, rel=None):
+    def act(out, in_, func, bias, scale, n, R, W, rel=None):
         def fn():
             if bias is None:
                 return [S.activation(ap(out), ap(in_), func)]
             return [S.activation(ap(out), ap(in_), func, bias=bias, scale=scale)]
-        add("s", fn, n, R, W, acq=acq, rel=rel)
+        add("s", fn, n, R, W, banks=bk(out, in_), rel=rel)
 
-    def mm(bank, groups, R, W, own=True):
+    def mm(bank, groups, R, W, start=True, stop=True):
+        if any(cs.stop < 16 or cs.start >= (cs.step or 1) for items in groups for rs, cs, l, r, n in items):
+            bank["rowed"] = True
+
         def fn():
-            ps = T["ps%d" % bank["k"]]
-            return [P.matmul(ps[:, sl], l, r, i == 0, i == len(items) - 1)
-                    for items in groups for i, (sl, l, r, n) in enumerate(items)]
-        add("p", fn, sum(max(64, it[3]) for items in groups for it in items), R, W, lat=100.0, acq=bank if own else None)
+            return [P.matmul(ap((bank, rs, cs)), l[0], r, start and i == 0, stop and i == len(items) - 1)
+                    for items in groups for i, (rs, cs, l, r, n) in enumerate(items)]
+        add("p", fn, sum(max(64, it[4]) for items in groups for it in items),
+            list(R) + sorted({it[2][1] for items in groups for it in items}), W, lat=100.0, banks=[bank])
 
     def iota(out, pat, base, cm, n, W, flt=False):
         if flt:
@@ -117,216 +148,204 @@ def build(g, T, topo, core, ops):
         else:
             add("g", lambda: [g.iota(out, pat, base, cm)], 2 * n, (), W)
 
-    def dma(out, in_, sem, lat, R, W):
-        add("y", lambda: [Y.dma_start(out, in_)], 0, R, W, lat=lat, sem=(sem, 16))
+    def dma(out, in_, sem, lat, R, W, n=0):
+        add("y", lambda: [Y.dma_start(out, in_)], n, R, W, lat=lat, sem=(sem, 16))
 
     dma(T.sdb[:], T.sd[:], "dsd", 4300.0, (), ["sd"])
-    add("s", lambda: [S.dma_start(T.actb[:], T.act[:])], 0, (), ["act"], lat=2500.0, sem=("dact", 16))
-    dma(T.xw[:, 0:4096], T.x[:], "dx0", 7200.0, ["~sd"], ["x0"])
-    for h in range(4):
-        act(T.xw[:, K + 1024 * h:K + 1024 * (h + 1)], T.xw[:, 1024 * h:1024 * (h + 1)], F.Copy, None, None, 1024, ["x0"],
-            ["x%d" % (3 + h)])
-    fill(T.xw[:, 4096:K], 2.0 ** 62, 16, ["x1"])
-    fill(T.xw[:, K + 4096:2 * K], 2.0 ** 62, 16, ["x2"])
+    add("s", lambda: [S.dma_start(T.actb[:, 0:12], T.act[:])], 0, (), ["act"], lat=2500.0, sem=("dact", 16))
+    dma(T.xw[:, PAD:PAD + 4096], T.x[:], "dx0", 7200.0, (), ["x0"])
+    fill(T.xw[:, 0:PAD], 2.0 ** 62, 16, ["x1"])
+    fill(T.xw[:, PAD + 4096:], 2.0 ** 62, 16, ["x2"])
+    fill(T.actb[:, 12:16], 0, 16, ["act2"])
 
     ci, cf = T.ci, T.cf
-    w = [T["w%d" % k] for k in range(13)]
     SH, AND = A.logical_shift_right, A.bitwise_and
     iota(ci[:, 5:6], [[0, 1]], 0, 1, 1, ["ci5"])
+    iota(T.i144[:], [[1, 144]], 0, 0, 144, ["i144"], True)
+    iota(T.w0[:], [[NB, NCH], [1, 8]], 0, 0, 16, ["w0"])
+    iota(T.w1[:], [[32, 16]], 15, 0, 16, ["w1"])
+    iota(T.pos[:], [[0, NB], [1, 16]], 0, 0, N16, ["pos"], True)
     p_ = ci[:, 5:6]
-    ts(ci[:, 0:1], p_, 1, 7, SH, AND, 1, ["ci5"], ["ci0"])
-    ts(ci[:, 1:2], p_, 1, None, AND, None, 1, ["ci5"], ["ci1"])
     ts(ci[:, 2:3], p_, 7, None, AND, None, 1, ["ci5"], ["ci2"])
     ts(ci[:, 3:4], p_, 3, 1, SH, AND, 1, ["ci5"], ["ci3"])
     ts(ci[:, 4:5], p_, 15, None, AND, None, 1, ["ci5"], ["ci4"])
-    cp(cf[:, 0:6], ci[:, 0:6], 6, ["ci%d" % k for k in range(6)], ["cf"])
-    r0a, ha, r0b, hb, p16, pp = [cf[:, k:k + 1] for k in range(6)]
-    ts(cf[:, 6:7], ha, 8.0, r0a, A.mult, A.add, 1, ["cf"], ["cf6"])
-    ts(cf[:, 7:8], cf[:, 6:7], 12.0, None, A.mult, None, 1, ["cf6"], ["cf7"])
-    iota(w[0][:], [[1, 8], [0, NB]], 7, 0, N8, ["w0"])
-    iota(w[1][:], [[0, 8], [1, NB]], 0, 0, N8, ["w1"])
-    ts(w[2][:], w[0][:], r0a, None, A.subtract, None, N8, ["w0", "cf"], ["w2"])
-    ts(w[2][:], w[2][:], 7, None, AND, None, N8, ["w2"], ["w2"])
-    ts(w[2][:], w[2][:], 192.0, cf[:, 7:8], A.mult, A.add, N8, ["w2", "cf7"], ["w2"])
-    tt(w[2][:], w[2][:], w[1][:], A.add, 2 * N8, ["w2", "w1"], ["w2"])
-    for c in range(NCH):
-        ts(T["lz%d" % c][:], w[2][:], float(NB * c), None, A.add, None, N8, ["w2"], ["lz%d" % c])
-    iota(T.pos[:], [[0, NB], [1, 16]], 0, 0, N16, ["pos"], True)
-    iota(T.qf[:], [[0, NB], [1, 8], [8, 2]], 0, 0, N16, ["qf"], True)
-    iota(T.rb[:], [[0, NB], [8192, 8], [0, 2]], 8192, 0, N16, ["rb"], True)
-    iota(T.q24[:], [[0, NB], [-512, 8], [-4096, 2]], 24 * 512, 0, N16, ["q24"], True)
-    iota(T.i144[:], [[1, 144]], 0, 0, 144, ["i144"], True)
-    ts(T.rst[:], T.pos[:], 1.0, None, A.min, None, N16, ["pos"], ["rst"])
-    fill(T.one[:], 1.0, N16 // 2, ["one"])
-    fill(T.eight[:], 8.0, N16 // 2, ["eight"])
+    cp(cf[:, 2:6], ci[:, 2:6], 6, ["ci%d" % k for k in range(2, 6)], ["cf"])
+    p8, hb, p16, pp = [cf[:, k:k + 1] for k in range(2, 6)]
+    ts(T.idf[:], T.i144[:, 0:128], pp, None, A.is_equal, None, 128, ["i144", "cf"], ["idf"])
     ts(cf[:, 8:9], pp, p16, 15.0, A.subtract, A.add, 1, ["cf"], ["cf8"])
     ts(T.wb[:], T.i144[:], cf[:, 8:9], None, A.is_equal, None, 144, ["i144", "cf8"], ["wb"])
-    ts(T.idf[:], T.i144[:, 0:128], pp, None, A.is_equal, None, 128, ["i144", "cf"], ["idf"])
-    idm = [T.idm[:, 128 * k:128 * k + 128] for k in range(len(SCALES))]
-    for k, val in enumerate(SCALES):
-        act(idm[k], T.idf[:], F.Identity, 0.0, val, 128, ["idf"], ["id%d" % k])
-    cp(T.lb[:, 0:NB], w[1][:, 0:NB], NB, ["w1"], ["lb"])
-    ts(T.lu[:, 0:NB], w[1][:, 0:NB], 8.0, r0a, A.mult, A.add, NB, ["w1", "cf"], ["lu"])
-    H = NB // 2
-    ts(cf[:, 9:10], hb, 16.0, 15.0, A.mult, A.add, 1, ["cf"], ["cf9"])
-    ts(cf[:, 10:11], r0b, float(N16), cf[:, 9:10], A.mult, A.add, 1, ["cf", "cf9"], ["cf10"])
-    ts(T.lm[:, 0:H], w[1][:, 0:H], 32.0, cf[:, 10:11], A.mult, A.add, H, ["w1", "cf10"], ["lm0"])
-    ts(cf[:, 11:12], p16, float(NB - 1), 16.0, A.min, A.mult, 1, ["cf"], ["cf11"])
-    ts(T.lm[:, H:H + 1], cf[:, 11:12], float(8 * N16 + 15), None, A.add, None, 1, ["cf11"], ["lm1"])
-    iota(w[3][:, 0:7 * H], [[1, 7], [0, H]], 1, 0, 7 * H, ["w3"])
-    iota(w[4][:, 0:7 * H], [[0, 7], [32, H]], 0, 0, 7 * H, ["w4"])
-    ts(cf[:, 13:14], r0b, 2.0, cf[:, 9:10], A.mult, A.add, 1, ["cf", "cf9"], ["cf13"])
-    a3 = w[3][:, 0:7 * H]
-    ts(a3, a3, r0b, None, A.add, None, 7 * H, ["w3", "cf"], ["w3"])
-    ts(a3, a3, 7, None, AND, None, 7 * H, ["w3"], ["w3"])
-    ts(a3, a3, float(N16), cf[:, 13:14], A.mult, A.add, 7 * H, ["w3", "cf13"], ["w3"])
-    tt(a3, a3, w[4][:, 0:7 * H], A.add, 14 * H, ["w3", "w4"], ["w3"])
-    ts(T.ld[:, 0:7 * H], a3, -14.0, None, A.add, None, 7 * H, ["w3"], ["ld"])
-    ts(w[8][:], w[1][:], 16.0, p16, A.mult, A.add, N8, ["w1", "cf"], ["w8"])
-    act(w[9][:], w[8][:], F.Identity, 0.5 / NB - 0.5, 1.0 / NB, N8, ["w8"], ["w9"])
-    cp(w[5][:], w[9][:], N8, ["w9"], ["w5"])
-    ts(w[10][:], w[5][:], 8.0, -15.0, A.is_ge, A.mult, N8, ["w5"], ["w10"])
-    ts(w[11][:], w[5][:], 2.0 - 16 * NB, None, A.mult, None, N8, ["w5"], ["w11"])
-    act(w[12][:], w[8][:], F.Identity, 0.0, 16.0, N8, ["w8"], ["w12"])
-    tt(w[10][:], w[10][:], w[11][:], A.add, 2 * N8, ["w10", "w11"], ["w10"])
-    tt(w[10][:], w[10][:], w[12][:], A.add, 2 * N8, ["w10", "w12"], ["w10"])
-    cp(T.ln[:, 0:NB], w[10][:, 0:NB], NB, ["w10"], ["ln"])
-    tt(w[6][:], w[5][:], w[0][:], A.add, 2 * N8, ["w5", "w0"], ["w6"])
-    ts(w[6][:], w[6][:], 2.0, None, A.add, None, N8, ["w6"], ["w6"])
-    ts(w[6][:], w[6][:], 7, None, AND, None, N8, ["w6"], ["w6"])
-    ts(w[11][:], w[6][:], float(N16), None, A.mult, None, N8, ["w6"], ["w11"])
-    tt(w[11][:], w[11][:], w[10][:], A.add, 2 * N8, ["w11", "w10"], ["w11"])
-    cp(T.lf[:], w[11][:], N8, ["w11"], ["lf"])
+    ib = {v: (T.idb[:, 128 * k:128 * k + 128], "ib%g" % v) for k, v in enumerate(WB)}
+    ih = {v: (T.idh[:, 128 * k:128 * k + 128], "ih%g" % v) for k, v in enumerate(WH)}
+    for v in WB:
+        act(ib[v][0], T.idf[:], F.Identity, 0.0, v, 128, ["idf"], [ib[v][1]])
+    for v in WH:
+        ts(ih[v][0], T.idf[:], v, None, A.mult, None, 128, ["idf"], [ih[v][1]])
+    cp(T.lb[:], T.w0[:], 16, ["w0"], ["lb"])
+    ts(cf[:, 9:10], p8, float(N16), None, A.mult, None, 1, ["cf"], ["cf9"])
+    ts(cf[:, 10:11], hb, 16.0, cf[:, 9:10], A.mult, A.add, 1, ["cf", "cf9"], ["cf10"])
+    ts(T.lm[:], T.w1[:], cf[:, 10:11], None, A.add, None, 16, ["w1", "cf10"], ["lm"])
+    fill(T.rs16[:], 0.0, 2 * N16, ["rs16"])
+    fill(T.rs16[:, 0::16], -4 * BIG, 32, ["rs16"])
+    fill(T.rs2[:], 0.0, 2 * N16, ["rs2"])
+    fill(T.rs2[:, 0::2], -4 * BIG, N16, ["rs2"])
+    fill(T.rst[:], 1.0, N16, ["rst"])
+    fill(T.rst[:, 0::16], 0.0, 8, ["rst"])
+    fill(T.one[:], 1.0, N16 // 2, ["one"])
+    fill(T.odd[:], 1.0, N16 // 2, ["odd"])
+    fill(T.odd[:, 0::2], 0.0, N16 // 2, ["odd"])
+    fill(T.upp[:], 1.0, N16 // 2, ["upp"])
+    fill(T.upp[:, :, 0:8], 0.0, N16 // 2, ["upp"])
 
     for c in range(NCH):
-        chain(c, T, g, add, ts, tt, cp, fill, scan, act, mm, idm, rid, pid, emask)
+        chain(c, T, g, add, ts, tt, fill, scan, act, mm, ib, ih, rid, pid, emask)
 
     dma(T.yp[:], T.ypb[:], "dyp", 2000.0, ["yp%d" % c for c in range(NCH)], ())
     dma(T.yc[:], T.ycb[:], "dyc", 2000.0, ["yc%d" % c for c in range(NCH)], ())
-    for h in range(4):
-        dma(T.ys[:, 384 * h:384 * (h + 1)], T.ysb[:, 32 * h:32 * (h + 1), :], "dy%d" % h, 2500.0,
-            ["ys%d_%d" % (c, h) for c in range(NCH)], ())
+    for h in range(2):
+        dma(T.ys[:, 768 * h:768 * (h + 1)], T.ysb[:, 64 * h:64 * (h + 1), :], "dy%d" % h, 3000.0,
+            ["ys%d_%d_%d" % (c, h, j) for c in range(NCH) for j in range(NB)], ())
 
 
-def chain(c, T, g, add, ts, tt, cp, fill, scan, act, mm, idm, rid, pid, emask):
+def chain(c, T, g, add, ts, tt, fill, scan, act, mm, ib, ih, rid, pid, emask):
     b = {n: T["%s%d" % (n, c)] for n, _w, _d in PER_CHAIN}
-    XR = ["x%d" % i for i in range(7)]
-    SH, AND = A.logical_shift_right, A.bitwise_and
+    XR = ["x0", "x1", "x2"]
 
     def k(*names):
         return ["%s@%d" % (n, c) for n in names]
 
-    def ids(*which):
-        return ["id%d" % i for i in which]
+    def wb(*vals):
+        return ["ib%g" % v for v in vals]
 
-    st, sel, lo, si, sf, pb, mi = [b[n] for n in ("st", "sel", "lo", "si", "sf", "pb", "mi")]
-    rows = ["st%d" % r for r in range(8)]
-    lbl, lul = T.lb[:, 0:NB], T.lu[:, 0:NB]
+    def wh(*vals):
+        return ["ih%g" % v for v in vals]
 
-    def rg(i, n=1):
-        return slice(i * N16, (i + n) * N16)
+    st, sel, lo, mi, mo = [b[n] for n in ("st", "sel", "lo", "mi", "mo")]
 
-    def row(buf, r, n=1):
-        return buf[:, rg(r, n)]
+    def rows(i, n=1):
+        return slice(i * NB, (i + n) * NB)
 
-    def small(buf, i):
-        return buf[:, 16 * i:16 * i + NB]
+    def flat(buf, i, n=1):
+        return buf[:, i * N16:(i + n) * N16]
 
-    def spread(src, key):
-        bank = {}
-        mm(bank, [[(rg(i), idm[0], src, N16)] for i in range(4)], k(key) + ids(0), k(key + "4"))
-        return bank
+    R0, R1 = rows(0), rows(1)
+    LOW, UP = slice(0, 8), slice(8, 16)
 
-    def lift(t, cb):
-        tt(b["t0"][:], sf[:, 0:16].indirect(lbl), T.pos[:], A.subtract, -N16, k("sf0") + ["pos", "lb"], k("t0"))
-        act(b["sn"][:], b["t0"][:], F.Sign, -0.5, -1.0, N16, k("t0"), k("sn"))
-        act(row(st, 8), (cb, N16, 2 * N16), F.Copy, None, None, N16, k("cn"), k("st8"))
-        bank = {}
-        mm(bank, [[(rg(i), idm[10], b["sn"][:], N16), (rg(i), idm[11], T.one[:], N16)] for i in range(5)],
-           k("sn") + ids(10, 11) + ["one"], k("dl"))
-        scan(row(lo, 0, 4), (bank, 0, 4 * N16), row(st, 0, 4), A.add, A.max, 4 * N16, k("dl", *rows[0:4]), k("lo0"))
-        scan(row(lo, 4, 5), (bank, 0, 5 * N16), row(st, 4, 5), A.add, A.max, 5 * N16, k("dl", "st8", "~lo0", *rows[4:8]),
-             k("lo1"), rel=bank)
-        cp(b["mr"][:], lo[:, :].indirect(T.lm[:, 0:MW // 16]), -MW, k("lo0", "lo1") + ["lm0", "lm1"], k("mr"))
-        mo = b["mo"][:, t * MW:(t + 1) * MW]
-        ts(mo, b["mr"][:], int(B) - 1, None, AND, None, MW, k("mr"), k("mo%d" % t))
-        sem = "arr%d_%d" % (c, t)
-        add("g", lambda: [g.remote_dma(mi[:, t * MW:(t + 1) * MW], mo, T.sem[sem], T.sem.sent, pid, rid, emask)],
-            200, k("mo%d" % t), k("mi%d" % t), lat=3000.0, sem=(sem, -NENG))
-        act(b["nb"][:], b["t0"][:], F.Abs, 0.0, 8 * B, N16, k("t0"), k("nb"))
-        tt(row(b["c16"], t), b["nb"][:], (cb, 0, N16), A.min, N16, k("cn", "nb", "st8"), k("c16_%d" % t), rel=cb)
+    stk = [k(*["sti%d" % j for j in range(NB)])] * 2
 
-    def targets(ub, u0, shift, rpb, put):
-        for r0 in range(0, 8, rpb):
+    def send(r0, r1, sem, src, dst):
+        add("g", lambda: [g.remote_dma(mi[:, r0:r1, :], mo[:, 16 * r0:16 * r1], T.sem[sem], T.sem.sent, pid, rid, emask)],
+            200, k(src), k(dst), lat=3000.0, sem=(sem, -NENG))
+
+    def lift(t, ob):
+        m0 = t * MR
+        scan(mo[:, 16 * m0:16 * (m0 + NB)], T.rst[:], (ob, R0, ALL), A.mult, A.add, N16, k("oh") + ["rst"], k("mos%d" % t), rel=ob)
+        send(m0, m0 + NB, "ars%d_%d" % (c, t), "mos%d" % t, "mis%d" % t)
+        no = b["no"][:, rows(t), :]
+        for h in range(2):
             bank = {}
-            for r in range(r0, r0 + rpb):
-                act((bank, (r - r0) * N16, (r - r0 + 1) * N16), (ub, u0, u0 + N16), F.Abs, -B * (r + shift), 1.0, N16,
-                    k("uu") + (k("~tr%d" % (r - 1)) if r > 0 else []), k("tr%d" % r), acq=bank if r == r0 else None,
-                    rel=ub if r == 7 else None)
-            put(r0, rpb, bank, k(*["tr%d" % r for r in range(r0, r0 + rpb)]))
+            items = [(rows(i), ALL, ib[-BIG], no, N16) for i in range(4)]
+            for j in range(8):
+                r = 4 * h
+                while r < 4 * h + 4:
+                    s = (r - j - 1) % 8
+                    n = min(4 * h + 4 - r, 8 - s)
+                    items.append((rows(r - 4 * h, n), slice(j, 16, 8), ih[1.0], st[:, rows(s, n), j::8], 2 * NB * n))
+                    r += n
+            mm(bank, [items], k("no%d" % t) + stk[0] + stk[1] + wb(-BIG) + wh(1.0), k("lx%d" % h))
+            scan(flat(lo, 4 * h, 4), T.rs16[:], (bank, rows(0, 4), ALL), A.add, A.max, 4 * N16, k("lx%d" % h) + ["rs16"],
+                 k("lo%d" % h), rel=bank)
+        seeds = mo[:, 16 * (m0 + NB):16 * (m0 + MR)]
+        ts(seeds, lo[:, :].indirect(T.lm[:, 0:NB // 2]), 0.0, None, A.add, None, -N8, k("lo0", "lo1") + ["lm"], k("mo%d" % t))
+        send(m0 + NB, m0 + MR, "arr%d_%d" % (c, t), "mo%d" % t, "mi%d" % t)
 
-    fill(b["dsel"][:], -128 * B, N16 // 2, k("dsel"))
-    fill(pb[:, 0:16], 0.0, 16, k("pb0"))
-    fill(sf[:, 0:16], 0.0, 16, k("sf0"))
-    for h in range(2):
-        cp(row(st, 4 * h, 4), T.sdb[:, :].indirect(b["lz"][:, 4 * h * NB:4 * (h + 1) * NB]), -4 * N16, ["sd", "lz%d" % c],
-           k(*rows[4 * h:4 * h + 4]))
-        act(row(b["sg"], 4 * h, 4), row(st, 4 * h, 4), F.Sign, EMPTY - 0.5, -1.0, 4 * N16, k(*rows[4 * h:4 * h + 4]),
-            k("sgi%d" % h))
-    cb = {}
-    mm(cb, [[(rg(1), idm[8], T.qf[:], N16), (rg(1), idm[7], T.eight[:], N16)]
-            + [(rg(1), idm[7], row(b["sg"], r), N16) for r in range(8)],
-            [(rg(0), idm[5], T.eight[:], N16)] + [(rg(0), idm[5], row(b["sg"], r), N16) for r in range(8)]],
-       k("sgi0", "sgi1") + ids(5, 7, 8) + ["qf", "eight"], k("cn", "cnt0"))
-    ac = T.actb[:, NB * c:NB * (c + 1)]
-    ts(small(sf, 2), ac, 8.0, 15.0, A.is_ge, A.mult, NB, ["act"], k("sf2"))
-    ts(small(sf, 3), ac, 2.0, None, A.mult, None, NB, ["act"], k("sf3"))
-    tt(small(sf, 0), small(sf, 3), small(sf, 2), A.subtract, 2 * NB, k("sf2", "sf3"), k("sf0"))
-    lift(0, cb)
+    def counts(t, items, bias, R):
+        bank = {}
+        mm(bank, [items + [(R0, ALL, ib[16.0], b["no"][:, rows(t), :], N16)]], R + k("no%d" % t) + wb(16.0), k("cn"))
+        act(flat(b["ct"], t), (bank, R0, ALL), F.Relu, bias - 16.0, 1.0, N16, k("cn"), k("ct%d" % t))
+        act(b["z8"][:], (bank, R0, ALL), F.Relu, 16.0 * (bias - 23.0), 16.0, N16, k("cn"), k("z8"), rel=bank)
+
+    tt(b["mk"][:], T.actb[:, :].indirect(T.lb[:, 8 * c:8 * c + NB]), T.pos[:], A.not_equal, -N16,
+       ["act", "act2", "lb", "pos"], k("mk"))
+    act(b["no"][:, R0, :], b["mk"][:], F.Copy, None, None, N16, k("mk"), k("no0"))
+    ob = {}
+    mm(ob, [[(R0, ALL, ib[16.0], T.one[:], N16), (R0, ALL, ib[-16.0], b["no"][:, R0, :], N16)]],
+       k("no0") + ["one"] + wb(16.0, -16.0), k("oh"))
+    for j in range(NB):
+        ts(st[:, j::NB, :], T.sdb[:, :, NB * c + j], -MID, None, A.add, None, 128, ["sd"], k("sti%d" % j))
+    add("v", lambda: [g.vector.tensor_scalar(b["em"][:], st[:], MID, -4 * MID, A.is_ge, A.mult)], 4 * N16,
+        stk[0], k("em"))
+    lift(0, ob)
+    counts(0, [(R0, ALL, ib[1.0 / 8192], flat(b["em"], s), N16) for s in range(8)], 8.0, k("em") + wb(1.0 / 8192))
 
     for t in range(3):
-        m0 = t * MW
-        MI = k("mi%d" % t)
+        m0 = t * MR
+        MI, MS = k("mi%d" % t), k("mis%d" % t)
         cv = CV[c][t]
         ncol = 7 * N8
-        cp(b["aoff"][:], mi[:, m0:m0 + N8], N8, MI, k("aoff"))
-        act(b["fa"][:], T.xw[:, 0:K].indirect(b["aoff"][:, :]), F.Copy, None, None, -16 * N8, k("aoff") + XR[0:2], k("fa"))
-        tt(b["ti"][:], mi[:, m0 + N8:m0 + MW].indirect(lbl), T.q24[:], A.add, -N16, MI + ["q24", "lb"], k("ti"))
-        ts(b["ns"][:], b["ti"][:], 4096, None, AND, None, N16, k("ti"), k("ns"))
-        ts(b["dsel"][:, 1::2], b["ns"][:, 1::2], K / 2048.0, float(K), A.mult, A.subtract, N8, k("ns"), k("dsel"))
-        bank = spread(b["dsel"][:], "dsel")
+        sgn = 1.0 if t < 2 else -1.0
+        clamp = (A.min, 4096.0 + PAD) if sgn > 0 else (A.max, PAD - 1.0)
+        step = lambda a, z: mi[:, m0:m0 + NB, a:z]
+        seeds = mi[:, m0 + NB:m0 + MR, :]
+        no = b["no"][:, rows(t), :]
+        NO = k("no%d" % t)
+        ts(b["aoff"][:], seeds, MID + PAD, clamp[1], A.add, clamp[0], N8 // 2, MI, k("aoff"))
+        act(b["fa"][:], T.xw[:, :].indirect(b["aoff"][:, :]), F.Copy, None, None, -16 * N8, k("aoff") + XR, k("fa"))
+        bank = {}
+        mm(bank, [[(R0, ALL, ib[-BIG], T.odd[:], N16),
+                   (R0, slice(0, 16, 2), ih[-BIG / 16], step(7, 15), N8), (R0, slice(1, 16, 2), ih[BIG / 16], step(7, 15), N8),
+                   (R0, slice(2, 16, 2), ih[BIG / 16], step(0, 7), N8), (R0, slice(3, 16, 2), ih[-BIG / 16], step(0, 7), N8),
+                   (R0, slice(0, 16, 2), ib[-sgn * OWN], b["no"][:, rows(t), LOW], N8),
+                   (R0, slice(1, 16, 2), ib[-sgn * OWN], b["no"][:, rows(t), UP], N8)]],
+           MS + NO + ["odd"] + wb(-BIG, -sgn * OWN) + wh(BIG / 16, -BIG / 16), k("mx"))
+        act(b["mk"][:], (bank, R0, ALL), F.Identity, sgn * OWN, 1.0, N16, k("mx"), k("mk"), rel=bank)
         for h in range(2):
-            scan(row(sel, 4 * h, 4), (bank, 0, 4 * N16), row(st, 4 * h, 4), A.add, A.max, 4 * N16,
-                 k("dsel4", *rows[4 * h:4 * h + 4]) + (k("~sel0") if h else []),
-                 k(*["sel%d" % r for r in range(4 * h, 4 * h + 4)]), rel=bank if h else None)
-        cp(b["off"][:], sel[:, :].indirect(T.ld[:, 0:7 * NB // 2]), -ncol, k("sel0", "sel4") + ["ld"], k("off"))
+            n = 4 - h
+            bank = {}
+            items = [(rows(i), ALL, ib[1.0], b["mk"][:], N16) for i in range(n)]
+            items += [(rows(0, n), slice(u, 16, 2), ih[1.0], st[:, rows(4 * h, n), 8 * u:8 * u + 8], n * N8) for u in range(2)]
+            mm(bank, [items], k("mk") + stk[h] + wb(1.0) + wh(1.0), k("sx%d" % h))
+            scan(flat(sel, 4 * h, n), T.rs2[:, 0:n * N16], (bank, rows(0, n), ALL), A.add, A.max, n * N16,
+                 k("sx%d" % h) + ["rs2"], k("sel%d" % h), rel=bank)
+            ts(b["off"][:, 4 * h * N8:(4 * h + n) * N8], sel[:, 4 * h * N16 + 1:(4 * h + n) * N16:2], MID + PAD, clamp[1],
+               A.add, clamp[0], n * N8, k("sel%d" % h), k("off%d" % h))
+        if t == 0:
+            for h in range(2):
+                bank = {}
+                mm(bank, [[(rows(0, 4), ALL, ib[1.0], flat(b["em"], 4 * h, 4), 4 * N16)]], k("em") + wb(1.0), k("eb%d" % h))
+                blk = st[:, rows(4 * h, 4), :]
+                tt(blk, blk, (bank, rows(0, 4), ALL), A.add, 4 * N16, k("eb%d" % h), k("st%d" % h) + stk[h], rel=bank)
+            stk[0:2] = [k("st0"), k("st1")]
+
+        def offk(c0, c1):
+            return k(*[n for n, use in (("off0", c0 < 4 * N8), ("off1", c1 > 4 * N8)) if use])
+
         pieces = []
-        c0 = 0
-        while c0 < cv:
-            c1 = min(cv, (c0 // N8 + 1) * N8)
+        c0 = ncol - cv
+        while c0 < ncol:
+            c1 = min(ncol, (c0 // N8 + 1) * N8)
             f0 = (c0 % N8) * 16
             tt(b["cm"][:, 16 * c0:16 * c1], T.xw[:, :].indirect(b["off"][:, c0:c1]), b["fa"][:, f0:f0 + 16 * (c1 - c0)],
-               A.is_lt, -16 * (c1 - c0), k("off", "fa") + XR, k("cm%d" % c0))
+               A.is_lt, -16 * (c1 - c0), offk(c0, c1) + k("fa") + XR, k("cm%d" % c0))
             pieces.append((c0, c1, 0))
             c0 = c1
-        while c0 < ncol:
-            c1 = min(ncol, c0 + GCOL)
+        c0 = 0
+        while c0 < ncol - cv:
+            c1 = min(ncol - cv, c0 + GCOL)
             act(b["fs"][:, 16 * c0:16 * c1], T.xw[:, :].indirect(b["off"][:, c0:c1]), F.Copy, None, None,
-                -16 * (c1 - c0), k("off") + XR, k("fs%d" % c0))
+                -16 * (c1 - c0), offk(c0, c1) + XR, k("fs%d" % c0))
             d0 = c0
             while d0 < c1:
                 d1 = min(c1, d0 + 32)
                 bank = {}
-                items = [(slice(0, 16 * (d1 - d0)), idm[1], b["fs"][:, 16 * d0:16 * d1], 16 * (d1 - d0))]
+                items = [(slice(0, d1 - d0), ALL, ib[-1.0], b["fs"][:, 16 * d0:16 * d1], 16 * (d1 - d0))]
                 e0 = d0
                 while e0 < d1:
                     e1 = min(d1, (e0 // N8 + 1) * N8)
                     f0 = (e0 % N8) * 16
-                    items.append((slice(16 * (e0 - d0), 16 * (e1 - d0)), idm[0], b["fa"][:, f0:f0 + 16 * (e1 - e0)],
-                                  16 * (e1 - e0)))
+                    items.append((slice(e0 - d0, e1 - d0), ALL, ib[1.0], b["fa"][:, f0:f0 + 16 * (e1 - e0)], 16 * (e1 - e0)))
                     e0 = e1
-                mm(bank, [items], k("fs%d" % c0, "fa") + ids(0, 1), k("df%d" % d0))
-                act(b["cm"][:, 16 * d0:16 * d1], (bank, 0, 16 * (d1 - d0)), F.Sign, -2.0 ** -68, 1.0, 16 * (d1 - d0),
+                mm(bank, [items], k("fs%d" % c0, "fa") + wb(1.0, -1.0), k("df%d" % d0))
+                act(b["cm"][:, 16 * d0:16 * d1], (bank, slice(0, d1 - d0), ALL), F.Sign, -2.0 ** -68, 1.0, 16 * (d1 - d0),
                     k("df%d" % d0), k("cm%d" % d0), rel=bank)
                 pieces.append((d0, d1, 1))
                 d0 = d1
@@ -334,102 +353,102 @@ def chain(c, T, g, add, ts, tt, cp, fill, scan, act, mm, idm, rid, pid, emask):
         groups = []
         for kind in range(2):
             mine = [p for p in pieces if p[2] == kind]
-            cur = []
-            for i, p in enumerate(mine):
-                cur.append(p)
-                if cur[-1][1] - cur[0][0] >= GC and (i == len(mine) - 1 or mine[-1][1] - p[1] >= 32):
-                    groups.append(cur)
-                    cur = []
-            if cur:
-                groups.append(cur)
+            cut = len(mine) - GL[kind]
+            groups += [gr for gr in (mine[:cut], mine[cut:]) if gr]
         sgk = []
         for gr in groups:
             g0, g1 = gr[0][0], gr[-1][1]
             bank = {}
-            mm(bank, [[(slice(0, g1 - g0), T.wb[:, 15 - i:143 - i], b["cm"][:, 16 * g0 + i:16 * g1:16], g1 - g0)
-                       for i in range(16)]], k(*["cm%d" % p[0] for p in gr]) + ["wb"], k("ct%d" % g0))
-            act(b["sg"][:, g0:g1], (bank, 0, g1 - g0), F.Sign, -1.0 if gr[0][2] else -8.5, 1.0, g1 - g0,
-                k("ct%d" % g0, "cnt0"), k("sg%d_%d" % (t, g0)), rel=bank)
+            part = slice(0, (g1 - g0) // 16)
+            mm(bank, [[(part, ALL, (T.wb[:, 15 - i:143 - i], "wb"), b["cm"][:, 16 * g0 + i:16 * g1:16], g1 - g0)
+                       for i in range(16)]], k(*["cm%d" % p[0] for p in gr]) + ["wb"], k("cc%d" % g0))
+            act(b["sg"][:, g0:g1], (bank, part, ALL), F.Sign, -1.0 if gr[0][2] else -8.5, 1.0, g1 - g0,
+                k("cc%d" % g0, "sgfree"), k("sg%d_%d" % (t, g0)), rel=bank)
             sgk.append("sg%d_%d" % (t, g0))
-        c16 = row(b["c16"], t)
-        at = row(b["at"], t)
-        AT = k("at%d" % t)
-        wd = mi[:, m0 + N8:m0 + N8 + NB]
-        tt(b["a16"][:], mi[:, m0:m0 + N8].indirect(lul), b["ns"][:], A.max, -N16, MI + k("ns") + ["lu"], k("a16"))
-        act(b["hs"][:], b["a16"][:], F.Sign, EMPTY - 0.5, -1.0, N16, k("a16"), k("hs"))
-        ts(b["cl"][:], c16, B, 7 * B, A.max, A.min, N16 // 2, k("c16_%d" % t), k("cl"))
-        ts(small(si, 1), wd, 3, 14, SH, AND, NB, MI, k("si1"))
-        ts(small(si, 2), wd, 7, 1, SH, AND, NB, MI, k("si2"))
-        tt(small(pb, 0), small(si, 1), small(si, 2), A.add, 2 * NB, k("si1", "si2"), k("pb0"))
-        tt(b["oh"][:], pb[:, 0:16].indirect(lbl), T.pos[:], A.is_equal, -N16, k("pb0") + ["pos", "lb"], k("oh"))
-        if t == 2:
-            ts(small(si, 3), wd, 4, 15, SH, AND, NB, MI, k("si3"))
-            cp(small(pb, 1), small(si, 3), NB, k("si3"), k("pb1"))
-        db = {}
-        items = [(rg(0), idm[2], c16, N16), (rg(0), idm[3], b["cl"][:], N16), (rg(0), idm[4], b["hs"][:], N16)]
+        hs = lambda a, z: b["hs"][:, rows(t), a:z]
+        HS = k("hs%d" % t)
+        bank = {}
+        mm(bank, [[(R0, ALL, ib[sgn * BIG], T.upp[:], N16),
+                   (R0, LOW, ih[1.0], seeds, N8), (R0, UP, ih[1.0], seeds, N8),
+                   (R0, LOW, ih[sgn * BIG / 16], step(7, 15), N8), (R0, UP, ih[-sgn * BIG / 16], step(7, 15), N8),
+                   (R0, slice(1, 8), ih[-sgn * BIG / 16], step(0, 7), N8), (R0, slice(9, 16), ih[sgn * BIG / 16], step(0, 7), N8)]],
+           MI + MS + ["upp"] + wb(sgn * BIG) + wh(1.0, BIG / 16, -BIG / 16), k("ax"))
+        act(hs(0, 16), (bank, R0, ALL), F.Sign, MID - 0.5 * sgn, -sgn, N16, k("ax"), HS, rel=bank)
+        sgn = 1.0 if t % 2 else -1.0
+        bank = {}
+        mm(bank, [[(R0, ALL, ib[-sgn * BIG / 2], hs(0, 16), N16), (R0, LOW, ih[1.0], seeds, N8), (R0, UP, ih[1.0], seeds, N8)]],
+           MI + HS + wb(-sgn * BIG / 2) + wh(1.0), k("ay"))
+        ts(b["a16"][:], (bank, R0, ALL), sgn * BIG / 2, MID if sgn > 0 else -MID - 2.0, A.add, A.min if sgn > 0 else A.max,
+           N16, k("ay"), k("a16"), rel=bank)
+        ct, cs = flat(b["ct"], t), flat(b["cs"], t)
+        CT, CS = k("ct%d" % t), k("cs%d" % t)
+        bank = {}
+        items = [(R0, ALL, ib[-1.0], ct, N16), (R0, ALL, ib[1.0], b["z8"][:], N16), (R0, ALL, ib[16.0], hs(0, 16), N16)]
         for s in range(7):
-            for h in range(2):
-                items.append((slice(h, N16, 2), idm[0], b["sg"][:, s * N8:(s + 1) * N8], N8))
-        mm(db, [items], k("c16_%d" % t, "cl", "hs", *sgk) + ids(0, 2, 3, 4), k("dd"))
-        keep = (db, N16, 2 * N16)
-        act(keep, (db, 0, N16), F.Relu, 94 * 8 * B, -8 * B, N16, k("dd"), k("keep"))
-        tt(at, c16, keep, A.min, N16, k("c16_%d" % t, "keep"), AT)
-        tt(b["pr"][:], b["oh"][:], keep, A.min, N16, k("oh", "keep", "~at%d" % t), k("pr"), rel=db)
-        xb = {}
-        mm(xb, [[(slice(0, NB), idm[0], small(pb, t // 2), NB)]
-                + [(slice(0, NB), idm[12], b["pr"][:, i::16], NB) for i in range(16)]], k("pr", "pb0", "pb1") + ids(0, 12),
-           k("xs"))
+            for half in (LOW, UP):
+                items.append((R0, half, ib[1.0], b["sg"][:, s * N8:(s + 1) * N8], N8))
+        mm(bank, [items], CT + HS + k("z8", *sgk) + wb(1.0, -1.0, 16.0), k("dd", "sgfree"))
+        act(cs, (bank, R0, ALL), F.Sign, -9.5, 1.0, N16, k("dd"), CS, rel=bank)
+
+        bank = {}
+        mm(bank, [[(R0, ALL, ib[8.0], hs(0, 16), N16), (R0, slice(0, 15), ib[-8.0], hs(1, 16), N16),
+                   (R0, slice(15, 16), ib[-8.0], hs(0, 1), NB), (R0, ALL, ih[1.0], step(0, 16), N16),
+                   (R0, slice(1, 16), ih[-1.0], step(0, 15), N16)]], HS + MS + wb(8.0, -8.0) + wh(1.0, -1.0), k("lq"))
+        act(b["la"][:], (bank, R0, ALL), F.Copy, None, None, N16, k("lq"), k("la"), rel=bank)
+
+        def last(rs):
+            return [(rs, ALL, ib[1.0], b["la"][:], N16)]
+
+        LASTK = k("la") + wb(8.0)
+        ee, cl = b["ee"][:, rows(2 * t), :], b["ee"][:, rows(2 * t + 1), :]
+        EE = k("ee%d" % t)
+        bank = {}
+        mm(bank, [[(R0, ALL, ib[1.0], ct, N16), (R0, ALL, ib[0.5], hs(0, 16), N16), (R0, ALL, ib[-8.5], cs, N16)],
+                  last(R1) + [(R1, ALL, ib[8.0], cs, N16)]], CT + CS + LASTK + wb(1.0, 0.5, -8.5), k("ex"))
+        act(b["ee"][:, rows(2 * t, 2), :], (bank, rows(0, 2), ALL), F.Relu, -8.0, 1.0, 2 * N16, k("ex"), EE, rel=bank)
         ub = {}
+        mm(ub, [[(R0, ALL, ih[1.0], b["a16"][:], N16), (R0, ALL, ib[sgn * B], ct, N16), (R0, ALL, ib[sgn * B], no, N16),
+                 (R0, ALL, ib[sgn * B / 2], hs(0, 16), N16), (R0, ALL, ib[-sgn * CAP / 2], cs, N16)]],
+           CT + CS + HS + NO + k("a16"), k("uu"))
+        fb = {}
+        mm(fb, [[(R0, ALL, ih[1.0], b["a16"][:], N16), (R0, ALL, ib[sgn * BIG / 2], hs(0, 16), N16),
+                 (R0, ALL, ib[sgn * BIG / 2], cs, N16), (R0, ALL, ib[-sgn * BIG], no, N16)]],
+           CS + HS + NO + k("a16") + wb(sgn * BIG / 2, -sgn * BIG) + wh(1.0), k("fx"))
+        for h in range(2):
+            bank = {}
+            for i in range(4):
+                s = 4 * h + i
+                act((bank, rows(i), ALL), (ub, R0, ALL), F.Identity, -sgn * (B * (s + 1.5) + CAP / 2), 1.0, N16, k("uu"), k("yr%d" % s),
+                    rel=ub if s == 7 else None)
+            blk = st[:, rows(4 * h, 4), :]
+            tt(blk, blk, (bank, rows(0, 4), ALL), A.min if sgn > 0 else A.max, 4 * N16,
+               k("st%d" % h, *["yr%d" % (4 * h + i) for i in range(4)]), k("st%d" % h), rel=bank)
+            if h == 0:
+                tt(st[:, R0, :], st[:, R0, :], (fb, R0, ALL), A.max if sgn > 0 else A.min, N16, k("st0", "fx"), k("st0"), rel=fb)
+        ob = {}
+        mm(ob, [last(R0) + [(R0, ALL, ib[-1.0], cl, N16), (R0, ALL, ib[1.0], b["ee"][:, rows(2 * t + 1), ::-1], N16)]],
+           EE + LASTK + wb(1.0, -1.0), k("oh"))
         if t < 2:
-            act(small(sf, 0), (xb, 0, NB), F.Abs, -15.0, 1.0, NB, k("xs"), k("sf0"), rel=xb)
-            mm(ub, [[(rg(0), idm[0], at, N16), (rg(0), idm[0], T.rb[:], N16)]], AT + ["rb"], k("v1", "uu"))
-            act(b["es"][:], (ub, 0, N16), F.Sign, -7.5 * B, 1.0, N16, k("v1"), k("es"))
-            mm(ub, [[(rg(1), T.idf[:], b["a16"][:], 4 * N16), (rg(1), idm[0], at, N16), (rg(1), idm[0], T.rb[:], N16),
-                     (rg(1), idm[9], b["es"][:], N16)]], AT + k("a16", "es") + ids(9), k("uu"), own=False)
-            cb = {}
-            mm(cb, [[(rg(1), idm[6], at, N16), (rg(1), idm[7], b["hs"][:], N16), (rg(1), idm[7], T.one[:], N16),
-                     (rg(1), idm[8], T.qf[:], N16)],
-                    [(rg(0), idm[0], at, N16), (rg(0), idm[5], b["hs"][:], N16), (rg(0), idm[5], T.one[:], N16)]],
-               AT + k("hs") + ids(6), k("cn"))
-            act(b["clr"][:], at, F.Relu, EMPTY, -1.0, N16, AT, k("clr"))
-            eb = spread(b["clr"][:], "clr")
-            for h in range(2):
-                blk = row(st, 4 * h, 4)
-                tt(blk, blk, (eb, 0, 4 * N16), A.max, 4 * N16, k("clr4", *rows[4 * h:4 * h + 4]) + (k("~st0") if h else []),
-                   k(*rows[4 * h:4 * h + 4]), rel=eb if h else None)
-
-            def put(r0, n, bank, keys):
-                blk = row(st, r0, n)
-                tt(blk, blk, (bank, 0, n * N16), A.min, n * N16, k(*rows[r0:r0 + n]) + keys, k(*rows[r0:r0 + n]), rel=bank)
-            targets(ub, N16, 4, 4, put)
-            lift(t + 1, cb)
+            act(b["no"][:, rows(t + 1), :], (ob, R0, ALL), F.Identity, 1.0, -1.0 / 16, N16, k("oh"), k("no%d" % (t + 1)))
+            lift(t + 1, ob)
+            counts(t + 1, [(R0, ALL, ib[1.0], ee, N16), (R0, ALL, ib[0.5], cs, N16)], 0.5, EE + CS + wb(1.0, 0.5))
         else:
-            act(T.ypb[:, NB * c:NB * (c + 1)], (xb, 0, NB), F.Abs, -15.0, 1.0, NB, k("xs"), ["yp%d" % c], rel=xb)
-            lnl = T.ln[:, 0:NB]
-            act(b["an"][:], b["a16"][:, :].indirect(lnl), F.Copy, None, None, -N16, k("a16") + ["ln"], k("an"))
-            act(b["es"][:], at.indirect(lnl), F.Copy, None, None, -N16, AT + ["ln"], k("es"))
-            act(b["clr"][:], b["es"][:], F.Relu, EMPTY, -1.0, N16, k("es"), k("clr"))
-            eb = spread(b["clr"][:], "clr")
-            mm(ub, [[(rg(0), T.idf[:], b["an"][:], 4 * N16), (rg(0), idm[0], b["es"][:], N16)]], k("an", "es"), k("uu"))
+            t0, t1 = flat(b["t0"], 0), flat(b["t0"], 1)
+            scan(t0, T.rst[:], (ob, R0, ALL), A.mult, A.add, N16, k("oh") + ["rst"], k("t0"), rel=ob)
+            scan(t1, T.rst[:], t0, A.mult, A.add, N16, k("t0") + ["rst"], k("t1"))
+            act(T.ypb[:, NB * c:NB * (c + 1)], b["t0"][:, N16 + 15::16], F.Identity, 16.0, -1.0 / 16, NB, k("t1"), ["yp%d" % c])
             for h in range(2):
-                blk = row(sel, 4 * h, 4)
-                act(blk, st[:, 0:8 * N16].indirect(T.lf[:, 4 * h * NB:4 * (h + 1) * NB]), F.Copy, None, None, -4 * N16,
-                    k("off", *rows) + ["lf"], k("fi%d" % h))
-                tt(blk, blk, (eb, 0, 4 * N16), A.max, 4 * N16, k("clr4", "fi%d" % h) + (k("~fin0") if h else []),
-                   k("fin%d" % h), rel=eb if h else None)
-
-            def put(r0, n, bank, keys):
-                tt(T.ysb[:, 16 * r0:16 * (r0 + n), NB * c:NB * (c + 1)], row(sel, r0, n), (bank, 0, n * N16), A.min, n * N16,
-                   k("fin%d" % (r0 // 4)) + keys, ["ys%d_%d" % (c, r0 // 2)], rel=bank)
-            targets(ub, 0, 0, 2, put)
-            sb = {}
+                for j in range(NB):
+                    ts(T.ysb[:, 64 * h:64 * (h + 1), NB * c + j], st[:, 4 * h * NB + j:4 * (h + 1) * NB:NB, :], MID, MID,
+                       A.min, A.add, 64, k("st%d" % h), ["ys%d_%d_%d" % (c, h, j)])
+            bank = {}
             items = []
             for u in range(3):
-                items.append((rg(0), idm[0], row(b["c16"], u), N16))
-                items.append((rg(0), idm[1], row(b["at"], u), N16))
-            mm(sb, [items], k("c16_0", "c16_1", "c16_2", "at0", "at1", "at2"), k("sc"))
-            scan(b["t0"][:], T.rst[:], (sb, 0, N16), A.mult, A.add, N16, k("sc") + ["rst"], k("t0"), rel=sb)
-            act(T.ycb[:, NB * c:NB * (c + 1)], b["t0"][:, 15::16], F.Identity, 0.0, 1.0 / B, NB, k("t0"), ["yc%d" % c])
+                items += [(R0, ALL, ib[1.0], flat(b["ct"], u), N16), (R0, ALL, ib[0.5], b["hs"][:, rows(u), :], N16),
+                          (R0, ALL, ib[-1.0], b["ee"][:, rows(2 * u), :], N16), (R0, ALL, ib[-0.5], flat(b["cs"], u), N16)]
+            mm(bank, [items], k(*["%s%d" % (n, u) for n in ("ct", "hs", "ee", "cs") for u in range(3)]) + wb(-0.5), k("sc"))
+            scan(flat(lo, 0), T.rst[:], (bank, R0, ALL), A.mult, A.add, N16, k("sc") + ["rst"], k("lo0"), rel=bank)
+            act(T.ycb[:, NB * c:NB * (c + 1)], lo[:, 15:N16:16], F.Copy, None, None, NB, k("lo0"), ["yc%d" % c])
 
 
 def costs(ops, case):
@@ -456,22 +475,24 @@ def schedule(ops, succ, busy, prio):
     banks = [[0.0, (), True] for _ in range(8)]
     order, pick, after = [], {}, {}
     while ready:
-        av = [j for j in range(8) if banks[j][2]]
-        kb = min(av, key=lambda j: banks[j][0]) if av else None
-        best = None
+        av = sorted((banks[j][0], -j) for j in range(8) if banks[j][2])
+        fit = {None: av, True: [a for a in av if -a[1] < NROWED], False: [a for a in av if -a[1] >= NROWED]}
+        able = []
         for i in ready:
             o = ops[i]
             s = max(rt[i], free[o["eng"]])
+            kb = None
             if o["acq"] is not None:
-                if kb is None:
+                can = fit[o["acq"].get("rowed")]
+                if not can:
                     continue
+                kb = -min([a for a in can if a[0] <= s], key=lambda a: a[1], default=can[0])[1]
                 s = max(s, banks[kb][0])
-            key = s - 0.005 * prio[i]
-            if best is None or key < best[0]:
-                best = (key, i, s)
-        if best is None:
+            able.append((s, i, kb))
+        if not able:
             return None
-        key, i, s = best
+        s, i, kb = min(able)
+        key, s, i, kb = max((prio[j], u, j, q) for u, j, q in able if ops[j]["eng"] == ops[i]["eng"] and u <= s + WAIT)
         o = ops[i]
         if o["acq"] is not None:
             o["acq"]["k"] = pick[i] = kb
@@ -480,7 +501,7 @@ def schedule(ops, succ, busy, prio):
         free[o["eng"]] = s + busy[i]
         fin = s + busy[i] + o["lat"] + wake
         if o["rel"] is not None:
-            banks[o["rel"]["k"]] = [fin, [i] + list(o["soft"]), True]
+            banks[o["rel"]["k"]] = [fin, list(o["rel"]["users"]), True]
         ready.remove(i)
         order.append(i)
         for j in succ[i]:
@@ -488,22 +509,7 @@ def schedule(ops, succ, busy, prio):
             left[j] -= 1
             if left[j] == 0:
                 ready.append(j)
-    return order, pick, after
-
-
-def replay(ops, order, after, busy, case):
-    fin = {}
-    free = {e: 0.0 for e in "vspgy"}
-    for i in order:
-        o = ops[i]
-        s = free[o["eng"]]
-        for d in o["deps"]:
-            s = max(s, fin[d])
-        for d in after.get(i, ()):
-            s = max(s, fin[d])
-        free[o["eng"]] = s + busy[i]
-        fin[i] = s + busy[i] + o["lat"] * case[6] + case[5]
-    return max(fin.values())
+    return order
 
 
 def plan(ops):
@@ -521,6 +527,8 @@ def plan(ops):
         kinds.setdefault(o["nm"][:2] + o["nm"][-2:], []).append(i)
         if "@" in o["nm"]:
             prio[i] -= LAG * int(o["nm"][-1])
+        if o["nm"][:2] in ("cm", "fs", "df", "cc"):
+            prio[i] -= BULK
     kinds = [kinds[q] for q in sorted(kinds)]
     seed = [12345]
 
@@ -529,6 +537,7 @@ def plan(ops):
         return seed[0] / 2147483648.0
 
     best = None
+    go = walk(ops, busy)
     for it in range(TRIES):
         p = list(prio)
         for _ in range((1, 3, 8)[int(rnd() * 3)] if it else 0):
@@ -536,13 +545,119 @@ def plan(ops):
             for i in (kinds[int(rnd() * len(kinds))] if rnd() < 0.3 else [int(rnd() * n)]):
                 p[i] += d
         got = schedule(ops, succ, busy[0], p)
+        timed = got and go(got)
+        if timed and (best is None or worth(timed[0]) <= best[0] + 60.0):
+            best = (worth(timed[0]), got)
+            prio = p
+    return polish(ops, go, best[1], rnd)
+
+
+def worth(times):
+    return sum(tm / (case[0] * (1.0 + 0.3 * case[1])) for tm, case in zip(times, CASES))
+
+
+def walk(ops, busy):
+    n = len(ops)
+    below, near = [], []
+    for o in ops:
+        deep = 0
+        for d in o["deps"]:
+            deep |= below[d]
+        near.append([d for d in o["deps"] if not deep >> d & 1])
+        below.append(deep | sum(1 << d for d in o["deps"]))
+    row = [(o["eng"], near[i], o["acq"], o["rel"], busy[0][i], busy[1][i], busy[2][i])
+           + tuple(o["lat"] * case[6] + case[5] for case in CASES) for i, o in enumerate(ops)]
+
+    def go(order):
+        fin, start, why = [None] * n, [None] * n, [None] * n
+        free = {e: (0.0, 0.0, 0.0, None) for e in "vspgy"}
+        banks = {j: (0.0, []) for j in range(8)}
+        pick, after = {}, {}
+        for i in order:
+            e, wait, bank, rel, b0, b1, b2, l0, l1, l2 = row[i]
+            s0, s1, s2, prev = free[e]
+            if bank is not None:
+                kind = bank.get("rowed")
+                can = [(max(banks[j][0], s0), -j) for j in banks if kind is None or (j < NROWED) == kind]
+                if not can:
+                    return None
+                bank["k"] = pick[i] = kb = -min(can)[1]
+                after[i] = banks.pop(kb)[1]
+                wait = wait + after[i]
+            why[i] = (prev, wait)
+            for d in wait:
+                f0, f1, f2 = fin[d]
+                if f0 > s0:
+                    s0 = f0
+                if f1 > s1:
+                    s1 = f1
+                if f2 > s2:
+                    s2 = f2
+            start[i] = (s0, s1, s2)
+            s0 += b0
+            s1 += b1
+            s2 += b2
+            free[e] = (s0, s1, s2, i)
+            fin[i] = (s0 + l0, s1 + l1, s2 + l2)
+            if rel is not None:
+                banks[rel["k"]] = (s0 + l0, [i])
+        return [max(f[u] for f in fin) for u in range(3)], pick, after, start, fin, why
+    return go
+
+
+def polish(ops, go, order, rnd):
+    cur = go(order)
+    val = worth(cur[0])
+    best = (val, (order, cur[1], cur[2]), list(cur[0]))
+    before = [o["deps"] | o["soft"] for o in ops]
+    for it in range(MOVES):
+        heat = HEAT * (1.0 - it / MOVES)
+        times, pick, after, start, fin, why = cur
+        u = int(rnd() * len(CASES))
+        i = max(range(len(ops)), key=lambda j: fin[j][u])
+        held = []
+        while i is not None:
+            prev = why[i][0]
+            late = [d for d in why[i][1] if fin[d][u] >= start[i][u] - 1e-6]
+            if late:
+                i = late[0]
+            else:
+                if prev is not None and start[i][u] > 0:
+                    held.append((prev, i))
+                i = prev if start[i][u] > 0 else None
+        at = {j: q for q, j in enumerate(order)}
+        if held and rnd() < 0.8:
+            a, z = held[int(rnd() * len(held))]
+            if rnd() < 0.3:
+                same = [j for j in order[:at[a]] if ops[j]["eng"] == ops[a]["eng"]][-3:]
+                a = same[int(rnd() * len(same))] if same else a
+        else:
+            z = int(rnd() * len(ops))
+            a = order[max(0, at[z] - 1 - int(rnd() * 12))]
+        part = order[at[a]:at[z] + 1]
+        if rnd() < 0.5:
+            move = {z}
+            for j in reversed(part):
+                if j in move:
+                    move |= before[j]
+            new = [j for j in part if j in move] + [j for j in part if j not in move]
+        else:
+            move = {a}
+            for j in part:
+                if before[j] & move:
+                    move.add(j)
+            new = [j for j in part if j not in move] + [j for j in part if j in move]
+        if new == part:
+            continue
+        trial = order[:at[a]] + new + order[at[z] + 1:]
+        got = go(trial)
         if got is None:
             continue
-        times = [replay(ops, got[0], got[2], busy[u], CASES[u]) for u in range(len(CASES))]
-        val = sum(times) + times[0]
-        if best is None or val <= best[0] + 100.0:
-            best = (val, got, times)
-            prio = p
+        v = worth(got[0])
+        if v <= val + heat * rnd():
+            order, cur, val = trial, got, v
+            if v < best[0]:
+                best = (v, (order, got[1], got[2]), list(got[0]))
     return best
 
 

@@ -7,10 +7,14 @@ NCH = 2
 NB = 12 // NCH
 N8 = 8 * NB
 N16 = 16 * NB
-MR = NB + NB // 2
 CV = [[208, 208, 208], [208, 208, 208]]
-GCOL = 64
-GL = (2, 0)
+YPE = [[0, 0, 0]] * NCH
+GCOL = 32
+VP = N8 // 2
+FA = 2
+CCP = 8
+DSPLIT = True
+GL = (96, 0)
 NENG = 8
 NROWED = 2
 PAD = 16
@@ -18,29 +22,30 @@ MID = 2048.0
 B = 4160.0
 CAP = 37632.0
 BIG = 2.0 ** 19
-OWN = 2.0 ** 17
-WB = (1.0, -1.0, 0.5, -0.5, 8.0, -8.0, -8.5, 16.0, -16.0, B, -B, B / 2, -B / 2, CAP / 2, -CAP / 2,
-      BIG, -BIG, BIG / 2, -BIG / 2, OWN, -OWN, 1.0 / 8192)
+THR = 25.5
+CLAMP = ((A.min, 4096.0 + PAD), (A.min, 4096.0 + PAD), (A.max, PAD - 2.0))
+WB = (16.0, -16.0, -BIG, -1.0 / 16, 1.0, BIG, -1.0, BIG / 2, 8.0, -8.0, 0.5, -8.5, -B, -B / 2, CAP / 2, -0.25,
+      -BIG / 2, B, B / 2, -CAP / 2, -0.5)
 WH = (1.0, -1.0, BIG / 16, -BIG / 16)
 
 SCRATCH = {n: ("sbuf", [128, w], d) for n, w, d in (
     ("xw", 4096 + 2 * PAD, "bfloat16"), ("actb", 16, "int32"), ("ypb", 12, "float32"),
     ("ycb", 12, "float32"), ("ci", 8, "int32"), ("cf", 16, "float32"), ("i144", 144, "float32"), ("wb", 144, "bfloat16"),
     ("idb", 128 * len(WB), "bfloat16"), ("idh", 128 * len(WH), "float16"), ("idf", 128, "float32"),
-    ("pos", N16, "float32"), ("rst", N16, "float32"), ("one", N16, "bfloat16"), ("odd", N16, "bfloat16"),
-    ("rs2", 4 * N16, "bfloat16"), ("rs16", 4 * N16, "bfloat16"),
+    ("pos", N16, "float32"), ("rst", N16, "float32"),
+    ("ramp", 8 * N16, "float16"), ("rs2", 4 * N16, "bfloat16"), ("rs16", 4 * N16, "bfloat16"),
     ("lb", 8 * NCH, "uint16"), ("lm", 16, "uint16"), ("w0", 8 * NCH, "int32"), ("w1", 16, "int32"))}
 SCRATCH["upp"] = ("sbuf", [128, NB, 16], "bfloat16")
 SCRATCH["sdb"] = ("sbuf", [128, 128, 12], "int32")
 SCRATCH["ysb"] = ("sbuf", [128, 128, 12], "float32")
 PER_CHAIN = (
     ("st", [8 * NB, 16], "float16"), ("em", [8 * N16], "bfloat16"), ("lo", [8 * N16], "float32"),
-    ("sel", [7 * N16], "float32"), ("off", [7 * N8], "uint16"), ("aoff", [N8], "uint16"), ("fa", [16 * N8], "bfloat16"),
+    ("gg", [N16], "bfloat16"), ("sel", [8 * N16], "float32"), ("off", [7 * N8], "uint16"), ("fa", [16 * N8], "bfloat16"),
     ("fs", [112 * N8], "bfloat16"), ("cm", [112 * N8], "bfloat16"), ("sg", [7 * N8], "bfloat16"),
-    ("mo", [48 * MR], "float16"), ("mi", [3 * MR, 16], "float16"), ("mr", [2 * N8], "float32"),
-    ("no", [3 * NB, 16], "bfloat16"), ("mk", [N16], "bfloat16"), ("a16", [N16], "float16"),
-    ("hs", [3 * NB, 16], "bfloat16"), ("cs", [3 * N16], "bfloat16"), ("ee", [6 * NB, 16], "bfloat16"),
-    ("ct", [3 * N16], "bfloat16"), ("z8", [N16], "bfloat16"), ("la", [N16], "bfloat16"),
+    ("mo", [3 * N16], "float16"), ("mi", [3 * NB, 16], "float16"), ("so", [3 * N8], "uint16"), ("si", [3 * N8], "uint16"),
+    ("sd16", [N8], "float16"), ("no", [3 * NB, 24], "bfloat16"), ("a16", [N16], "float16"),
+    ("hs", [3 * NB, 16], "bfloat16"), ("cs", [3 * N16], "bfloat16"), ("ee", [3 * N16], "bfloat16"),
+    ("ct", [3 * N16], "bfloat16"), ("z8", [N16], "bfloat16"), ("th", [N16], "bfloat16"), ("cl", [NB, 16], "bfloat16"),
     ("t0", [2 * N16], "float32"))
 for _c in range(NCH):
     for _n, _w, _d in PER_CHAIN:
@@ -48,17 +53,19 @@ for _c in range(NCH):
 for _k in range(8):
     SCRATCH["ps%d" % _k] = ("psum", [128, 32, 16] if _k < NROWED else [128, 512], "float32")
 
-SEMAPHORES = (["cv", "cs", "cp", "cg", "sent", "dact", "dsd", "dx0", "dyp", "dyc"] + ["dy%d" % h for h in range(2)]
+SEMAPHORES = (["cv", "cs", "cp", "cg", "sent", "dact", "dsd0", "dsd1", "dx0", "dyp", "dyc"] + ["dy%d" % h for h in range(2)]
               + ["%s%d_%d" % (n, c, t) for n in ("arr", "ars") for c in range(NCH) for t in range(3)])
 
 CASES = ((0.9, 1.56, 0.45, 50.0, 65.0, 70.0, 0.9), (1.05, 1.15, 0.525, 50.0, 65.0, 90.0, 1.0),
          (1.1, 2.0, 0.55, 50.0, 65.0, 70.0, 0.75))
-LAG = 6000.0
-BULK = 12000.0
-TRIES = 300
-MOVES = 40000
-HEAT = 150.0
-WAIT = 60.0
+LAG = 7000.0
+BULK = 5000.0
+STARTS = 9
+MOVES = 3000
+HEAT = 300.0
+SEED = 1
+EARLY = 0.1
+WAIT = 300.0
 PLAN = {}
 ALL = slice(0, 16)
 
@@ -69,9 +76,12 @@ def build(g, T, topo, core, ops):
     rid, pid = topo.addr(nxt)[0:2]
     emask = sum(1 << e for e in topo.engines(core, nxt)[:NENG])
     V, S, P, Y = g.vector, g.scalar, g.tensor, g.sync
-    last_w, readers = {}, {}
+    last_w, readers, held = {}, {}, []
 
     def add(eng, fn, n, R=(), W=(), lat=0.0, sem=None, banks=(), rel=None):
+        if held:
+            held[0].append((eng, fn, n, R, W, banks, rel))
+            return
         i = len(ops)
         deps = {last_w[k] for k in list(R) + list(W) if k in last_w}
         for k in W:
@@ -93,6 +103,16 @@ def build(g, T, topo, core, ops):
         soft.discard(i)
         ops.append({"eng": eng, "fn": fn, "n": n, "lat": lat, "deps": deps, "sem": sem, "soft": soft,
                     "nm": (list(W) + ["-"])[0], "acq": acq, "rel": rel})
+
+    def together(make):
+        held.append([])
+        make()
+        calls = held.pop()
+        banks = []
+        for call in calls:
+            banks += [bank for bank in call[5] if not any(bank is x for x in banks)]
+        add(calls[0][0], lambda: [ins for call in calls for ins in call[1]()], [call[2] for call in calls],
+            [x for call in calls for x in call[3]], [x for call in calls for x in call[4]], banks=banks, rel=calls[-1][6])
 
     def ap(x):
         if not isinstance(x, tuple):
@@ -151,62 +171,61 @@ def build(g, T, topo, core, ops):
     def dma(out, in_, sem, lat, R, W, n=0):
         add("y", lambda: [Y.dma_start(out, in_)], n, R, W, lat=lat, sem=(sem, 16))
 
-    dma(T.sdb[:], T.sd[:], "dsd", 4300.0, (), ["sd"])
+    for h in range(2):
+        dma(T.sdb[:, 64 * h:64 * (h + 1), :], T.sd[:, 768 * h:768 * (h + 1)], "dsd%d" % h, 3100.0 + 1200.0 * h, (), ["sd%d" % h])
+    ops[-1]["soft"].add(0)
     add("s", lambda: [S.dma_start(T.actb[:, 0:12], T.act[:])], 0, (), ["act"], lat=2500.0, sem=("dact", 16))
     dma(T.xw[:, PAD:PAD + 4096], T.x[:], "dx0", 7200.0, (), ["x0"])
-    fill(T.xw[:, 0:PAD], 2.0 ** 62, 16, ["x1"])
-    fill(T.xw[:, PAD + 4096:], 2.0 ** 62, 16, ["x2"])
-    fill(T.actb[:, 12:16], 0, 16, ["act2"])
+    ops[-1]["soft"].add(1)
 
     ci, cf = T.ci, T.cf
     SH, AND = A.logical_shift_right, A.bitwise_and
+    iota(T.i144[:], [[1, 144]], 0, -1, 144, ["i144"], True)
     iota(ci[:, 5:6], [[0, 1]], 0, 1, 1, ["ci5"])
-    iota(T.i144[:], [[1, 144]], 0, 0, 144, ["i144"], True)
     iota(T.w0[:], [[NB, NCH], [1, 8]], 0, 0, 16, ["w0"])
-    iota(T.w1[:], [[32, 16]], 15, 0, 16, ["w1"])
     iota(T.pos[:], [[0, NB], [1, 16]], 0, 0, N16, ["pos"], True)
+    iota(T.w1[:], [[32, 16]], 15, 0, 16, ["w1"])
+    for h in range(2 - max(max(y) for y in YPE), 2):
+        together(lambda: [fill(T.ramp[:, s * N16:(s + 1) * N16], B * (s + 1.5) + CAP / 2, N8, ["ramp%d" % h])
+                          for s in range(4 * h, 4 * h + 4)])
+    together(lambda: [
+        fill(T.rs16[:], 0.0, 2 * N16, ["rs16"]), fill(T.rst[:], 1.0, N16, ["rst"]), fill(T.actb[:, 12:16], 0, 16, ["act2"])]
+        + [fill(T["no%d" % c][:, :, 0:8], 1.0, 3 * N8 // 2, ["pads"]) for c in range(NCH)])
+    together(lambda: [
+        fill(T.rs2[:, 1::2], BIG, N16, ["rs2"]), fill(T.rs2[:, 0::2], -4 * BIG, N16, ["rs2"]),
+        fill(T.upp[:, :, 8:16], 1.0, N8, ["upp"]), fill(T.upp[:, :, 0:8], 0.0, N8, ["upp"]),
+        fill(T.xw[:, 0:PAD], 2.0 ** 62, 16, ["x1"]), fill(T.xw[:, PAD + 4096:], 2.0 ** 62, 16, ["x2"])])
+    together(lambda: [fill(T.rs16[:, 0::16], -4 * BIG, 32, ["rs16"]), fill(T.rst[:, 0::16], 0.0, 8, ["rst"])])
     p_ = ci[:, 5:6]
-    ts(ci[:, 2:3], p_, 7, None, AND, None, 1, ["ci5"], ["ci2"])
-    ts(ci[:, 3:4], p_, 3, 1, SH, AND, 1, ["ci5"], ["ci3"])
-    ts(ci[:, 4:5], p_, 15, None, AND, None, 1, ["ci5"], ["ci4"])
-    cp(cf[:, 2:6], ci[:, 2:6], 6, ["ci%d" % k for k in range(2, 6)], ["cf"])
-    p8, hb, p16, pp = [cf[:, k:k + 1] for k in range(2, 6)]
-    ts(T.idf[:], T.i144[:, 0:128], pp, None, A.is_equal, None, 128, ["i144", "cf"], ["idf"])
-    ts(cf[:, 8:9], pp, p16, 15.0, A.subtract, A.add, 1, ["cf"], ["cf8"])
-    ts(T.wb[:], T.i144[:], cf[:, 8:9], None, A.is_equal, None, 144, ["i144", "cf8"], ["wb"])
-    ib = {v: (T.idb[:, 128 * k:128 * k + 128], "ib%g" % v) for k, v in enumerate(WB)}
-    ih = {v: (T.idh[:, 128 * k:128 * k + 128], "ih%g" % v) for k, v in enumerate(WH)}
-    for v in WB:
-        act(ib[v][0], T.idf[:], F.Identity, 0.0, v, 128, ["idf"], [ib[v][1]])
-    for v in WH:
-        ts(ih[v][0], T.idf[:], v, None, A.mult, None, 128, ["idf"], [ih[v][1]])
+    together(lambda: [ts(ci[:, 2:3], p_, 7, None, AND, None, 1, ["ci5"], ["ci"]),
+                      ts(ci[:, 3:4], p_, 3, 1, SH, AND, 1, ["ci5"], ["ci"]),
+                      ts(ci[:, 4:5], p_, 15, None, AND, None, 1, ["ci5"], ["ci"])])
+    p8, hb, p16 = [ci[:, k:k + 1] for k in range(2, 5)]
+    together(lambda: [ts(cf[:, 8:9], p16, -1.0, 15.0, A.mult, A.add, 1, ["ci"], ["cf"]),
+                      ts(cf[:, 9:10], p8, float(N16), None, A.mult, None, 1, ["ci"], ["cf"]),
+                      ts(cf[:, 10:11], hb, 16.0, None, A.mult, None, 1, ["ci"], ["cf"])])
+    ts(T.idf[:], T.i144[:, 0:128], 0.0, None, A.is_equal, None, 128, ["i144"], ["idf"])
+    ts(T.wb[:], T.i144[:], cf[:, 8:9], None, A.is_equal, None, 144, ["i144", "cf"], ["wb"])
+    ib = {v: (T.idb[:, 128 * k:128 * k + 128], "ib%d" % (k // 4)) for k, v in enumerate(WB)}
+    ih = {v: (T.idh[:, 128 * k:128 * k + 128], "ih%d" % min(k, 1)) for k, v in enumerate(WH)}
+    for k in range(0, len(WB), 4):
+        together(lambda: [act(ib[v][0], T.idf[:], F.Identity, 0.0, v, 128, ["idf"], [ib[v][1]]) for v in WB[k:k + 4]])
+    for part in (WH[:1], WH[1:]):
+        together(lambda: [ts(ih[v][0], T.idf[:], v, None, A.mult, None, 128, ["idf"], [ih[v][1]]) for v in part])
     cp(T.lb[:], T.w0[:], 16, ["w0"], ["lb"])
-    ts(cf[:, 9:10], p8, float(N16), None, A.mult, None, 1, ["cf"], ["cf9"])
-    ts(cf[:, 10:11], hb, 16.0, cf[:, 9:10], A.mult, A.add, 1, ["cf", "cf9"], ["cf10"])
-    ts(T.lm[:], T.w1[:], cf[:, 10:11], None, A.add, None, 16, ["w1", "cf10"], ["lm"])
-    fill(T.rs16[:], 0.0, 2 * N16, ["rs16"])
-    fill(T.rs16[:, 0::16], -4 * BIG, 32, ["rs16"])
-    fill(T.rs2[:], 0.0, 2 * N16, ["rs2"])
-    fill(T.rs2[:, 0::2], -4 * BIG, N16, ["rs2"])
-    fill(T.rst[:], 1.0, N16, ["rst"])
-    fill(T.rst[:, 0::16], 0.0, 8, ["rst"])
-    fill(T.one[:], 1.0, N16 // 2, ["one"])
-    fill(T.odd[:], 1.0, N16 // 2, ["odd"])
-    fill(T.odd[:, 0::2], 0.0, N16 // 2, ["odd"])
-    fill(T.upp[:], 1.0, N16 // 2, ["upp"])
-    fill(T.upp[:, :, 0:8], 0.0, N16 // 2, ["upp"])
+    ts(T.lm[:], T.w1[:], cf[:, 9:10], cf[:, 10:11], A.add, A.add, 16, ["w1", "cf"], ["lm"])
 
     for c in range(NCH):
-        chain(c, T, g, add, ts, tt, fill, scan, act, mm, ib, ih, rid, pid, emask)
+        chain(c, T, g, add, together, ts, tt, scan, act, mm, ib, ih, rid, pid, emask)
 
     dma(T.yp[:], T.ypb[:], "dyp", 2000.0, ["yp%d" % c for c in range(NCH)], ())
     dma(T.yc[:], T.ycb[:], "dyc", 2000.0, ["yc%d" % c for c in range(NCH)], ())
     for h in range(2):
         dma(T.ys[:, 768 * h:768 * (h + 1)], T.ysb[:, 64 * h:64 * (h + 1), :], "dy%d" % h, 3000.0,
-            ["ys%d_%d_%d" % (c, h, j) for c in range(NCH) for j in range(NB)], ())
+            ["ys%d_%d" % (c, h) for c in range(NCH)], ())
 
 
-def chain(c, T, g, add, ts, tt, fill, scan, act, mm, ib, ih, rid, pid, emask):
+def chain(c, T, g, add, together, ts, tt, scan, act, mm, ib, ih, rid, pid, emask):
     b = {n: T["%s%d" % (n, c)] for n, _w, _d in PER_CHAIN}
     XR = ["x0", "x1", "x2"]
 
@@ -214,10 +233,10 @@ def chain(c, T, g, add, ts, tt, fill, scan, act, mm, ib, ih, rid, pid, emask):
         return ["%s@%d" % (n, c) for n in names]
 
     def wb(*vals):
-        return ["ib%g" % v for v in vals]
+        return []
 
     def wh(*vals):
-        return ["ih%g" % v for v in vals]
+        return []
 
     st, sel, lo, mi, mo = [b[n] for n in ("st", "sel", "lo", "mi", "mo")]
 
@@ -230,20 +249,26 @@ def chain(c, T, g, add, ts, tt, fill, scan, act, mm, ib, ih, rid, pid, emask):
     R0, R1 = rows(0), rows(1)
     LOW, UP = slice(0, 8), slice(8, 16)
 
-    stk = [k(*["sti%d" % j for j in range(NB)])] * 2
+    stk = [k("st0"), k("st1")]
 
-    def send(r0, r1, sem, src, dst):
-        add("g", lambda: [g.remote_dma(mi[:, r0:r1, :], mo[:, 16 * r0:16 * r1], T.sem[sem], T.sem.sent, pid, rid, emask)],
+    def send(out, in_, sem, src, dst):
+        add("g", lambda: [g.remote_dma(out, in_, T.sem[sem], T.sem.sent, pid, rid, emask)],
             200, k(src), k(dst), lat=3000.0, sem=(sem, -NENG))
 
-    def lift(t, ob):
-        m0 = t * MR
-        scan(mo[:, 16 * m0:16 * (m0 + NB)], T.rst[:], (ob, R0, ALL), A.mult, A.add, N16, k("oh") + ["rst"], k("mos%d" % t), rel=ob)
-        send(m0, m0 + NB, "ars%d_%d" % (c, t), "mos%d" % t, "mis%d" % t)
-        no = b["no"][:, rows(t), :]
+    def nob(t):
+        return b["no"][:, rows(t), 8:24]
+
+    def lift(t):
+        no = nob(t)
+        ob = {}
+        mm(ob, [[(R0, ALL, ib[-16.0], no, N16), (R0, ALL, ib[16.0], b["no"][:, rows(t), 0:16], N16)]],
+           k("no%d" % t) + ["pads"], k("oh"))
+        scan(flat(mo, t), T.rst[:], (ob, R0, ALL), A.mult, A.add, N16, k("oh") + ["rst"], k("mos%d" % t), rel=ob)
+        send(mi[:, rows(t), :], flat(mo, t), "ars%d_%d" % (c, t), "mos%d" % t, "mis%d" % t)
         for h in range(2):
             bank = {}
-            items = [(rows(i), ALL, ib[-BIG], no, N16) for i in range(4)]
+            mm(bank, [[(rows(i), ALL, ib[-BIG], no, N16) for i in range(4)]], k("no%d" % t), k("lw%d" % h), stop=False)
+            items = []
             for j in range(8):
                 r = 4 * h
                 while r < 4 * h + 4:
@@ -251,81 +276,80 @@ def chain(c, T, g, add, ts, tt, fill, scan, act, mm, ib, ih, rid, pid, emask):
                     n = min(4 * h + 4 - r, 8 - s)
                     items.append((rows(r - 4 * h, n), slice(j, 16, 8), ih[1.0], st[:, rows(s, n), j::8], 2 * NB * n))
                     r += n
-            mm(bank, [items], k("no%d" % t) + stk[0] + stk[1] + wb(-BIG) + wh(1.0), k("lx%d" % h))
+            mm(bank, [items], stk[0] + stk[1], k("lx%d" % h), start=False)
             scan(flat(lo, 4 * h, 4), T.rs16[:], (bank, rows(0, 4), ALL), A.add, A.max, 4 * N16, k("lx%d" % h) + ["rs16"],
                  k("lo%d" % h), rel=bank)
-        seeds = mo[:, 16 * (m0 + NB):16 * (m0 + MR)]
-        ts(seeds, lo[:, :].indirect(T.lm[:, 0:NB // 2]), 0.0, None, A.add, None, -N8, k("lo0", "lo1") + ["lm"], k("mo%d" % t))
-        send(m0 + NB, m0 + MR, "arr%d_%d" % (c, t), "mo%d" % t, "mi%d" % t)
+        part = slice(t * N8, (t + 1) * N8)
+        ts(b["so"][:, part], lo[:, :].indirect(T.lm[:, 0:NB // 2]), MID + PAD, CLAMP[t][1], A.add, CLAMP[t][0], -N8,
+           k("lo0", "lo1") + ["lm"], k("mo%d" % t))
+        send(b["si"][:, part], b["so"][:, part], "arr%d_%d" % (c, t), "mo%d" % t, "mi%d" % t)
 
     def counts(t, items, bias, R):
         bank = {}
-        mm(bank, [items + [(R0, ALL, ib[16.0], b["no"][:, rows(t), :], N16)]], R + k("no%d" % t) + wb(16.0), k("cn"))
-        act(flat(b["ct"], t), (bank, R0, ALL), F.Relu, bias - 16.0, 1.0, N16, k("cn"), k("ct%d" % t))
-        act(b["z8"][:], (bank, R0, ALL), F.Relu, 16.0 * (bias - 23.0), 16.0, N16, k("cn"), k("z8"), rel=bank)
+        mm(bank, [items + [(R0, ALL, ib[16.0], nob(t), N16)]], R + k("no%d" % t), k("cn"))
+        together(lambda: [
+            act(flat(b["ct"], t), (bank, R0, ALL), F.Relu, bias - 16.0, 1.0, N16, k("cn"), k("ct%d" % t)),
+            act(b["z8"][:], (bank, R0, ALL), F.Relu, 16.0 * (bias - 23.0), 16.0, N16, k("cn"), k("z8"), rel=bank)])
 
-    tt(b["mk"][:], T.actb[:, :].indirect(T.lb[:, 8 * c:8 * c + NB]), T.pos[:], A.not_equal, -N16,
-       ["act", "act2", "lb", "pos"], k("mk"))
-    act(b["no"][:, R0, :], b["mk"][:], F.Copy, None, None, N16, k("mk"), k("no0"))
-    ob = {}
-    mm(ob, [[(R0, ALL, ib[16.0], T.one[:], N16), (R0, ALL, ib[-16.0], b["no"][:, R0, :], N16)]],
-       k("no0") + ["one"] + wb(16.0, -16.0), k("oh"))
-    for j in range(NB):
-        ts(st[:, j::NB, :], T.sdb[:, :, NB * c + j], -MID, None, A.add, None, 128, ["sd"], k("sti%d" % j))
-    add("v", lambda: [g.vector.tensor_scalar(b["em"][:], st[:], MID, -4 * MID, A.is_ge, A.mult)], 4 * N16,
-        stk[0], k("em"))
-    lift(0, ob)
-    counts(0, [(R0, ALL, ib[1.0 / 8192], flat(b["em"], s), N16) for s in range(8)], 8.0, k("em") + wb(1.0 / 8192))
+    th, cl = b["th"], b["cl"]
+    tt(th[:], T.actb[:, :].indirect(T.lb[:, 8 * c:8 * c + NB]), T.pos[:], A.not_equal, -N16,
+       ["act", "act2", "lb", "pos"], k("th"))
+    act(nob(0), th[:], F.Copy, None, None, N16, k("th"), k("no0"))
+    if c == 0:
+        for h in range(2):
+            together(lambda: [ts(st[:, 4 * h * NB + j:4 * (h + 1) * NB:NB, :], T.sdb[:, 64 * h:64 * (h + 1), NB * c + j], -MID,
+                                 None, A.add, None, 64, ["sd%d" % h], stk[h]) for j in range(NB)])
+    else:
+        together(lambda: [ts(st[:, j::NB, :], T.sdb[:, :, NB * c + j], -MID, None, A.add, None, 128, ["sd0", "sd1"],
+                             stk[0] + stk[1]) for j in range(NB)])
+    for h in range(2):
+        bank = {}
+        mm(bank, [[(rows(0, 4), ALL, ih[1.0], st[:, rows(4 * h, 4), :], 4 * N16)]], stk[h], k("ew%d" % h))
+        act(flat(b["em"], 4 * h, 4), (bank, rows(0, 4), ALL), F.Relu, -16.0 * (MID - 1), 16.0, 4 * N16, k("ew%d" % h),
+            k("em%d" % h), rel=bank)
+    lift(0)
+    counts(0, [(R0, ALL, ib[-1.0 / 16], flat(b["em"], s), N16) for s in range(8)], 8.0, k("em0", "em1"))
 
     for t in range(3):
-        m0 = t * MR
         MI, MS = k("mi%d" % t), k("mis%d" % t)
         cv = CV[c][t]
         ncol = 7 * N8
         sgn = 1.0 if t < 2 else -1.0
-        clamp = (A.min, 4096.0 + PAD) if sgn > 0 else (A.max, PAD - 1.0)
-        step = lambda a, z: mi[:, m0:m0 + NB, a:z]
-        seeds = mi[:, m0 + NB:m0 + MR, :]
-        no = b["no"][:, rows(t), :]
+        step = lambda a, z: mi[:, rows(t), a:z]
+        seeds = b["sd16"][:]
+        no = nob(t)
         NO = k("no%d" % t)
-        ts(b["aoff"][:], seeds, MID + PAD, clamp[1], A.add, clamp[0], N8 // 2, MI, k("aoff"))
-        act(b["fa"][:], T.xw[:, :].indirect(b["aoff"][:, :]), F.Copy, None, None, -16 * N8, k("aoff") + XR, k("fa"))
-        bank = {}
-        mm(bank, [[(R0, ALL, ib[-BIG], T.odd[:], N16),
-                   (R0, slice(0, 16, 2), ih[-BIG / 16], step(7, 15), N8), (R0, slice(1, 16, 2), ih[BIG / 16], step(7, 15), N8),
-                   (R0, slice(2, 16, 2), ih[BIG / 16], step(0, 7), N8), (R0, slice(3, 16, 2), ih[-BIG / 16], step(0, 7), N8),
-                   (R0, slice(0, 16, 2), ib[-sgn * OWN], b["no"][:, rows(t), LOW], N8),
-                   (R0, slice(1, 16, 2), ib[-sgn * OWN], b["no"][:, rows(t), UP], N8)]],
-           MS + NO + ["odd"] + wb(-BIG, -sgn * OWN) + wh(BIG / 16, -BIG / 16), k("mx"))
-        act(b["mk"][:], (bank, R0, ALL), F.Identity, sgn * OWN, 1.0, N16, k("mx"), k("mk"), rel=bank)
+        FP = N8 // FA
+        for u in range(FA):
+            act(b["fa"][:, 16 * u * FP:16 * (u + 1) * FP], T.xw[:, :].indirect(b["si"][:, t * N8 + u * FP:t * N8 + (u + 1) * FP]),
+                F.Copy, None, None, -16 * FP, MI + XR, k("fa%d" % u))
+        ts(seeds, b["si"][:, t * N8:(t + 1) * N8], -MID - PAD, None, A.add, None, N8 // 2, MI, k("sd16"))
+        MI = k("sd16")
         for h in range(2):
             n = 4 - h
             bank = {}
-            items = [(rows(i), ALL, ib[1.0], b["mk"][:], N16) for i in range(n)]
-            items += [(rows(0, n), slice(u, 16, 2), ih[1.0], st[:, rows(4 * h, n), 8 * u:8 * u + 8], n * N8) for u in range(2)]
-            mm(bank, [items], k("mk") + stk[h] + wb(1.0) + wh(1.0), k("sx%d" % h))
+            mm(bank, [[(rows(0, n), slice(u, 16, 2), ih[1.0], st[:, rows(4 * h, n), 8 * u:8 * u + 8], n * N8) for u in range(2)]],
+               stk[h], k("sw%d" % h), stop=False)
+            mm(bank, [[(rows(i), slice(u, 16, 2), ih[(2 * u - 1) * BIG / 16], step(7, 15), N8) for i in range(n) for u in range(2)]],
+               MS, k("sx%d" % h), start=False)
             scan(flat(sel, 4 * h, n), T.rs2[:, 0:n * N16], (bank, rows(0, n), ALL), A.add, A.max, n * N16,
                  k("sx%d" % h) + ["rs2"], k("sel%d" % h), rel=bank)
-            ts(b["off"][:, 4 * h * N8:(4 * h + n) * N8], sel[:, 4 * h * N16 + 1:(4 * h + n) * N16:2], MID + PAD, clamp[1],
-               A.add, clamp[0], n * N8, k("sel%d" % h), k("off%d" % h))
-        if t == 0:
-            for h in range(2):
-                bank = {}
-                mm(bank, [[(rows(0, 4), ALL, ib[1.0], flat(b["em"], 4 * h, 4), 4 * N16)]], k("em") + wb(1.0), k("eb%d" % h))
-                blk = st[:, rows(4 * h, 4), :]
-                tt(blk, blk, (bank, rows(0, 4), ALL), A.add, 4 * N16, k("eb%d" % h), k("st%d" % h) + stk[h], rel=bank)
-            stk[0:2] = [k("st0"), k("st1")]
+            ts(b["off"][:, 4 * h * N8:(4 * h + n) * N8], sel[:, 4 * h * N16 + 1:(4 * h + n) * N16:2], MID + PAD - BIG,
+               CLAMP[t][1], A.add, CLAMP[t][0], n * N8, k("sel%d" % h), k("off%d" % h))
 
         def offk(c0, c1):
             return k(*[n for n, use in (("off0", c0 < 4 * N8), ("off1", c1 > 4 * N8)) if use])
 
+        def fak(c0, c1):
+            return k(*sorted({"fa%d" % (x % N8 // FP) for x in range(c0, c1)}))
+
         pieces = []
         c0 = ncol - cv
         while c0 < ncol:
-            c1 = min(ncol, (c0 // N8 + 1) * N8)
+            c1 = min(ncol, (c0 // VP + 1) * VP)
             f0 = (c0 % N8) * 16
             tt(b["cm"][:, 16 * c0:16 * c1], T.xw[:, :].indirect(b["off"][:, c0:c1]), b["fa"][:, f0:f0 + 16 * (c1 - c0)],
-               A.is_lt, -16 * (c1 - c0), offk(c0, c1) + k("fa") + XR, k("cm%d" % c0))
+               A.is_lt, -16 * (c1 - c0), offk(c0, c1) + fak(c0, c1) + XR, k("cm%d" % c0))
             pieces.append((c0, c1, 0))
             c0 = c1
         c0 = 0
@@ -344,108 +368,137 @@ def chain(c, T, g, add, ts, tt, fill, scan, act, mm, ib, ih, rid, pid, emask):
                     f0 = (e0 % N8) * 16
                     items.append((slice(e0 - d0, e1 - d0), ALL, ib[1.0], b["fa"][:, f0:f0 + 16 * (e1 - e0)], 16 * (e1 - e0)))
                     e0 = e1
-                mm(bank, [items], k("fs%d" % c0, "fa") + wb(1.0, -1.0), k("df%d" % d0))
+                mm(bank, [items], k("fs%d" % c0) + fak(d0, d1), k("df%d" % d0))
                 act(b["cm"][:, 16 * d0:16 * d1], (bank, slice(0, d1 - d0), ALL), F.Sign, -2.0 ** -68, 1.0, 16 * (d1 - d0),
                     k("df%d" % d0), k("cm%d" % d0), rel=bank)
                 pieces.append((d0, d1, 1))
                 d0 = d1
             c0 = c1
         groups = []
-        for kind in range(2):
+        for kind in (1, 0):
             mine = [p for p in pieces if p[2] == kind]
-            cut = len(mine) - GL[kind]
+            cut = len([p for p in mine if p[1] <= mine[-1][1] - GL[kind]])
             groups += [gr for gr in (mine[:cut], mine[cut:]) if gr]
-        sgk = []
         for gr in groups:
             g0, g1 = gr[0][0], gr[-1][1]
             bank = {}
             part = slice(0, (g1 - g0) // 16)
-            mm(bank, [[(part, ALL, (T.wb[:, 15 - i:143 - i], "wb"), b["cm"][:, 16 * g0 + i:16 * g1:16], g1 - g0)
-                       for i in range(16)]], k(*["cm%d" % p[0] for p in gr]) + ["wb"], k("cc%d" % g0))
+            for u in range(0, 16, CCP):
+                mm(bank, [[(part, ALL, (T.wb[:, 15 - i:143 - i], "wb"), b["cm"][:, 16 * g0 + i:16 * g1:16], g1 - g0)
+                           for i in range(u, u + CCP)]], k(*["cm%d" % p[0] for p in gr]), k("cc%d" % g0) if u + CCP == 16 else k("cc%d_%d" % (g0, u)),
+                   start=u == 0, stop=u + CCP == 16)
             act(b["sg"][:, g0:g1], (bank, part, ALL), F.Sign, -1.0 if gr[0][2] else -8.5, 1.0, g1 - g0,
                 k("cc%d" % g0, "sgfree"), k("sg%d_%d" % (t, g0)), rel=bank)
-            sgk.append("sg%d_%d" % (t, g0))
         hs = lambda a, z: b["hs"][:, rows(t), a:z]
         HS = k("hs%d" % t)
         bank = {}
         mm(bank, [[(R0, ALL, ib[sgn * BIG], T.upp[:], N16),
                    (R0, LOW, ih[1.0], seeds, N8), (R0, UP, ih[1.0], seeds, N8),
-                   (R0, LOW, ih[sgn * BIG / 16], step(7, 15), N8), (R0, UP, ih[-sgn * BIG / 16], step(7, 15), N8),
-                   (R0, slice(1, 8), ih[-sgn * BIG / 16], step(0, 7), N8), (R0, slice(9, 16), ih[sgn * BIG / 16], step(0, 7), N8)]],
-           MI + MS + ["upp"] + wb(sgn * BIG) + wh(1.0, BIG / 16, -BIG / 16), k("ax"))
-        act(hs(0, 16), (bank, R0, ALL), F.Sign, MID - 0.5 * sgn, -sgn, N16, k("ax"), HS, rel=bank)
+                   (R0, LOW, ih[sgn * BIG / 16], step(7, 15), N8), (R0, UP, ih[-sgn * BIG / 16], step(7, 15), N8)]],
+           MI + MS + ["upp"], k("ax"))
+        act(hs(0, 16), (bank, R0, ALL), F.Sign, MID - 0.5 * sgn, -sgn, N16, k("ax"), HS, rel=None if t else bank)
         sgn = 1.0 if t % 2 else -1.0
-        bank = {}
-        mm(bank, [[(R0, ALL, ib[-sgn * BIG / 2], hs(0, 16), N16), (R0, LOW, ih[1.0], seeds, N8), (R0, UP, ih[1.0], seeds, N8)]],
-           MI + HS + wb(-sgn * BIG / 2) + wh(1.0), k("ay"))
-        ts(b["a16"][:], (bank, R0, ALL), sgn * BIG / 2, MID if sgn > 0 else -MID - 2.0, A.add, A.min if sgn > 0 else A.max,
-           N16, k("ay"), k("a16"), rel=bank)
+        if t == 0:
+            bank = {}
+            mm(bank, [[(R0, ALL, ib[BIG / 2], hs(0, 16), N16), (R0, LOW, ih[1.0], seeds, N8), (R0, UP, ih[1.0], seeds, N8)]],
+               MI + HS, k("ax"))
+        ts(b["a16"][:], (bank, R0, ALL), 0.0 if t else -BIG / 2, MID if sgn > 0 else -MID - 2.0, A.add,
+           A.min if sgn > 0 else A.max, N16, k("ax"), k("a16"), rel=bank)
         ct, cs = flat(b["ct"], t), flat(b["cs"], t)
         CT, CS = k("ct%d" % t), k("cs%d" % t)
         bank = {}
-        items = [(R0, ALL, ib[-1.0], ct, N16), (R0, ALL, ib[1.0], b["z8"][:], N16), (R0, ALL, ib[16.0], hs(0, 16), N16)]
-        for s in range(7):
-            for half in (LOW, UP):
-                items.append((R0, half, ib[1.0], b["sg"][:, s * N8:(s + 1) * N8], N8))
-        mm(bank, [items], CT + HS + k("z8", *sgk) + wb(1.0, -1.0, 16.0), k("dd", "sgfree"))
-        act(cs, (bank, R0, ALL), F.Sign, -9.5, 1.0, N16, k("dd"), CS, rel=bank)
-
-        bank = {}
         mm(bank, [[(R0, ALL, ib[8.0], hs(0, 16), N16), (R0, slice(0, 15), ib[-8.0], hs(1, 16), N16),
                    (R0, slice(15, 16), ib[-8.0], hs(0, 1), NB), (R0, ALL, ih[1.0], step(0, 16), N16),
-                   (R0, slice(1, 16), ih[-1.0], step(0, 15), N16)]], HS + MS + wb(8.0, -8.0) + wh(1.0, -1.0), k("lq"))
-        act(b["la"][:], (bank, R0, ALL), F.Copy, None, None, N16, k("lq"), k("la"), rel=bank)
-
-        def last(rs):
-            return [(rs, ALL, ib[1.0], b["la"][:], N16)]
-
-        LASTK = k("la") + wb(8.0)
-        ee, cl = b["ee"][:, rows(2 * t), :], b["ee"][:, rows(2 * t + 1), :]
+                   (R0, slice(1, 16), ih[-1.0], step(0, 15), N16), (R0, UP, ih[1.0], step(0, 8), N8),
+                   (R0, slice(9, 16), ih[-1.0], step(0, 7), N8)]], HS + MS, k("lq"))
+        act(th[:], (bank, R0, ALL), F.Identity, THR + 64.0, -4.0, N16, k("lq"), k("th"), rel=bank)
+        db = {}
+        items = [(R0, ALL, ib[-1.0], ct, N16), (R0, ALL, ib[1.0], b["z8"][:], N16), (R0, ALL, ib[16.0], hs(0, 16), N16),
+                 (R0, ALL, ib[16.0], no, N16)]
+        R = CT + HS + NO + k("z8")
+        for gr in groups:
+            g0, g1 = gr[0][0], gr[-1][1]
+            R = R + k("sg%d_%d" % (t, g0))
+            done = gr is groups[-1]
+            while g0 < g1:
+                z = min(g1, (g0 // N8 + 1) * N8)
+                part = slice(g0 % N8 // 8, (z - 1) % N8 // 8 + 1)
+                items += [(part, half, ib[1.0], b["sg"][:, g0:z], z - g0) for half in (LOW, UP)]
+                g0 = z
+            if DSPLIT or done:
+                mm(db, [items], R, k("dd", "sgfree") if done else k("da%d" % g1), start="users" not in db, stop=done)
+                items, R = [], []
+        act(cs, (db, R0, ALL), F.Sign, -THR, 1.0, N16, k("dd"), CS)
+        tt(cl[:], th[:], (db, R0, ALL), A.is_lt, N16, k("dd", "th"), k("cl"), rel=db)
+        ee = flat(b["ee"], t)
         EE = k("ee%d" % t)
         bank = {}
-        mm(bank, [[(R0, ALL, ib[1.0], ct, N16), (R0, ALL, ib[0.5], hs(0, 16), N16), (R0, ALL, ib[-8.5], cs, N16)],
-                  last(R1) + [(R1, ALL, ib[8.0], cs, N16)]], CT + CS + LASTK + wb(1.0, 0.5, -8.5), k("ex"))
-        act(b["ee"][:, rows(2 * t, 2), :], (bank, rows(0, 2), ALL), F.Relu, -8.0, 1.0, 2 * N16, k("ex"), EE, rel=bank)
+        mm(bank, [[(R0, ALL, ib[1.0], ct, N16), (R0, ALL, ib[0.5], hs(0, 16), N16), (R0, ALL, ib[-8.5], cs, N16)]],
+           CT + CS + HS, k("ex"))
+        act(ee, (bank, R0, ALL), F.Relu, -8.0, 1.0, N16, k("ex"), EE, rel=bank)
         ub = {}
-        mm(ub, [[(R0, ALL, ih[1.0], b["a16"][:], N16), (R0, ALL, ib[sgn * B], ct, N16), (R0, ALL, ib[sgn * B], no, N16),
-                 (R0, ALL, ib[sgn * B / 2], hs(0, 16), N16), (R0, ALL, ib[-sgn * CAP / 2], cs, N16)]],
-           CT + CS + HS + NO + k("a16"), k("uu"))
+        if YPE[c][t] < 2:
+            mm(ub, [[(R0, ALL, ih[1.0], b["a16"][:], N16), (R0, ALL, ib[sgn * B], ct, N16), (R0, ALL, ib[sgn * B], no, N16),
+                     (R0, ALL, ib[sgn * B / 2], hs(0, 16), N16), (R0, ALL, ib[-sgn * CAP / 2], cs, N16)]],
+               CT + CS + HS + NO + k("a16"), k("uu"))
         fb = {}
         mm(fb, [[(R0, ALL, ih[1.0], b["a16"][:], N16), (R0, ALL, ib[sgn * BIG / 2], hs(0, 16), N16),
                  (R0, ALL, ib[sgn * BIG / 2], cs, N16), (R0, ALL, ib[-sgn * BIG], no, N16)]],
            CS + HS + NO + k("a16") + wb(sgn * BIG / 2, -sgn * BIG) + wh(1.0), k("fx"))
+        onpe = YPE[c][t]
+        if onpe:
+            bank = {}
+            mm(bank, [[(R0, ALL, ib[1.0], ct, N16), (R0, ALL, ib[1.0], no, N16), (R0, ALL, ib[0.5], hs(0, 16), N16)]],
+               CT + HS + NO, k("gx"))
+            act(b["gg"][:], (bank, R0, ALL), F.Copy, None, None, N16, k("gx"), k("gg"), rel=bank)
         for h in range(2):
             bank = {}
-            for i in range(4):
-                s = 4 * h + i
-                act((bank, rows(i), ALL), (ub, R0, ALL), F.Identity, -sgn * (B * (s + 1.5) + CAP / 2), 1.0, N16, k("uu"), k("yr%d" % s),
-                    rel=ub if s == 7 else None)
             blk = st[:, rows(4 * h, 4), :]
-            tt(blk, blk, (bank, rows(0, 4), ALL), A.min if sgn > 0 else A.max, 4 * N16,
-               k("st%d" % h, *["yr%d" % (4 * h + i) for i in range(4)]), k("st%d" % h), rel=bank)
+            R4 = rows(0, 4)
+            if h + onpe >= 2:
+                YR = k("yr%d" % h)
+                mm(bank, [[(R4, ALL, ih[-sgn], flat(T.ramp, 4 * h, 4), 4 * N16)]
+                          + [(rows(i), ALL, w, x, N16) for w, x in ((ih[1.0], b["a16"][:]), (ib[sgn * B], b["gg"][:]))
+                             for i in range(4)]], k("a16", "gg") + ["ramp%d" % h], k("ya%d" % h), stop=False)
+                mm(bank, [[(rows(i), ALL, ib[-sgn * CAP / 2], cs, N16) for i in range(4)]], CS, YR, start=False)
+                ramp = (bank, R4, ALL)
+            else:
+                YR = k("yr%d" % h if t else "sel%d" % h)
+                together(lambda: [
+                    act((bank, rows(s % 4), ALL) if t else flat(sel, s), (ub, R0, ALL), F.Identity,
+                        -sgn * (B * (s + 1.5) + CAP / 2), 1.0, N16, k("uu"), YR, rel=ub if h or onpe else None)
+                    for s in range(4 * h, 4 * h + 4)])
+                ramp = (bank, R4, ALL)
+            if t:
+                tt(blk, blk, ramp, A.min if sgn > 0 else A.max, 4 * N16, stk[h] + YR, stk[h], rel=bank)
+            else:
+                mm(bank, [[(R4, ALL, ib[-B / 2], flat(b["em"], 4 * h, 4), 4 * N16), (R4, ALL, ih[1.0], blk, 4 * N16)]],
+                   k("em%d" % h) + stk[h], k("eb%d" % h))
+                tt(blk, flat(sel, 4 * h, 4), ramp, A.max, 4 * N16, YR + k("eb%d" % h), stk[h], rel=bank)
             if h == 0:
                 tt(st[:, R0, :], st[:, R0, :], (fb, R0, ALL), A.max if sgn > 0 else A.min, N16, k("st0", "fx"), k("st0"), rel=fb)
         ob = {}
-        mm(ob, [last(R0) + [(R0, ALL, ib[-1.0], cl, N16), (R0, ALL, ib[1.0], b["ee"][:, rows(2 * t + 1), ::-1], N16)]],
-           EE + LASTK + wb(1.0, -1.0), k("oh"))
+        mm(ob, [[(R0, ALL, ib[-0.25], th[:], N16), (R0, ALL, ib[-16.0], cl[:], N16), (R0, ALL, ib[16.0], cl[:, :, ::-1], N16)]],
+           k("th", "cl"), k("nx"))
         if t < 2:
-            act(b["no"][:, rows(t + 1), :], (ob, R0, ALL), F.Identity, 1.0, -1.0 / 16, N16, k("oh"), k("no%d" % (t + 1)))
-            lift(t + 1, ob)
-            counts(t + 1, [(R0, ALL, ib[1.0], ee, N16), (R0, ALL, ib[0.5], cs, N16)], 0.5, EE + CS + wb(1.0, 0.5))
+            act(nob(t + 1), (ob, R0, ALL), F.Identity, -THR / 64, -1.0 / 16, N16, k("nx"), k("no%d" % (t + 1)), rel=ob)
+            lift(t + 1)
+            counts(t + 1, [(R0, ALL, ib[1.0], ee, N16), (R0, ALL, ib[0.5], cs, N16)], 0.5, EE + CS)
         else:
             t0, t1 = flat(b["t0"], 0), flat(b["t0"], 1)
-            scan(t0, T.rst[:], (ob, R0, ALL), A.mult, A.add, N16, k("oh") + ["rst"], k("t0"), rel=ob)
+            scan(t0, T.rst[:], (ob, R0, ALL), A.mult, A.add, N16, k("nx") + ["rst"], k("t0"), rel=ob)
             scan(t1, T.rst[:], t0, A.mult, A.add, N16, k("t0") + ["rst"], k("t1"))
-            act(T.ypb[:, NB * c:NB * (c + 1)], b["t0"][:, N16 + 15::16], F.Identity, 16.0, -1.0 / 16, NB, k("t1"), ["yp%d" % c])
+            act(T.ypb[:, NB * c:NB * (c + 1)], b["t0"][:, N16 + 15::16], F.Identity, 16.0 - 8.5 * (16.0 + THR / 4), -1.0 / 16,
+                NB, k("t1"), ["yp%d" % c])
             for h in range(2):
-                for j in range(NB):
+                together(lambda: [
                     ts(T.ysb[:, 64 * h:64 * (h + 1), NB * c + j], st[:, 4 * h * NB + j:4 * (h + 1) * NB:NB, :], MID, MID,
-                       A.min, A.add, 64, k("st%d" % h), ["ys%d_%d_%d" % (c, h, j)])
+                       A.min, A.add, 64, k("st%d" % h), ["ys%d_%d" % (c, h)]) for j in range(NB)])
             bank = {}
             items = []
             for u in range(3):
                 items += [(R0, ALL, ib[1.0], flat(b["ct"], u), N16), (R0, ALL, ib[0.5], b["hs"][:, rows(u), :], N16),
-                          (R0, ALL, ib[-1.0], b["ee"][:, rows(2 * u), :], N16), (R0, ALL, ib[-0.5], flat(b["cs"], u), N16)]
+                          (R0, ALL, ib[-1.0], flat(b["ee"], u), N16), (R0, ALL, ib[-0.5], flat(b["cs"], u), N16)]
             mm(bank, [items], k(*["%s%d" % (n, u) for n in ("ct", "hs", "ee", "cs") for u in range(3)]) + wb(-0.5), k("sc"))
             scan(flat(lo, 0), T.rst[:], (bank, R0, ALL), A.mult, A.add, N16, k("sc") + ["rst"], k("lo0"), rel=bank)
             act(T.ycb[:, NB * c:NB * (c + 1)], lo[:, 15:N16:16], F.Copy, None, None, NB, k("lo0"), ["yc%d" % c])
@@ -459,7 +512,8 @@ def costs(ops, case):
         if e == "p":
             out.append(20.0 + n * pe)
         elif e in "vs":
-            out.append((fv if e == "v" else fs) + (max(64, n) if n >= 0 else -n * gg + 20) * cy)
+            out.append(sum((fv if e == "v" else fs) + (max(64, m) if m >= 0 else -m * gg) * cy
+                           for m in (n if isinstance(n, list) else [n])))
         else:
             out.append(160.0 + n * cy if e == "g" else 60.0)
     return out
@@ -522,34 +576,28 @@ def plan(ops):
     prio = [0.0] * n
     for i in range(n - 1, -1, -1):
         prio[i] = busy[0][i] + ops[i]["lat"] + max([prio[j] + CASES[0][5] for j in succ[i]] or [0.0])
-    kinds = {}
-    for i, o in enumerate(ops):
-        kinds.setdefault(o["nm"][:2] + o["nm"][-2:], []).append(i)
-        if "@" in o["nm"]:
-            prio[i] -= LAG * int(o["nm"][-1])
-        if o["nm"][:2] in ("cm", "fs", "df", "cc"):
-            prio[i] -= BULK
-    kinds = [kinds[q] for q in sorted(kinds)]
-    seed = [12345]
+    seed = [SEED]
 
     def rnd():
         seed[0] = (seed[0] * 1103515245 + 12345) % 2147483648
         return seed[0] / 2147483648.0
 
-    best = None
     go = walk(ops, busy)
-    for it in range(TRIES):
-        p = list(prio)
-        for _ in range((1, 3, 8)[int(rnd() * 3)] if it else 0):
-            d = (rnd() + rnd() - 1.0) * (4000.0, 16000.0, 40000.0)[int(rnd() * 3)]
-            for i in (kinds[int(rnd() * len(kinds))] if rnd() < 0.3 else [int(rnd() * n)]):
-                p[i] += d
-        got = schedule(ops, succ, busy[0], p)
-        timed = got and go(got)
-        if timed and (best is None or worth(timed[0]) <= best[0] + 60.0):
-            best = (worth(timed[0]), got)
-            prio = p
-    return polish(ops, go, best[1], rnd)
+    field = []
+    while len(field) < STARTS:
+        lag, bulk = LAG * (0.7 + 0.6 * rnd()), BULK * (0.5 + rnd())
+        got = schedule(ops, succ, busy[0], [
+            prio[i] + 300.0 * rnd() - lag * ("@1" in o["nm"]) - bulk * (o["nm"][:2] in ("cm", "fs", "df", "cc"))
+            for i, o in enumerate(ops)])
+        if got and go(got):
+            field.append(got)
+    moves = MOVES
+    while True:
+        ends = sorted((polish(ops, go, order, rnd, moves) for order in field), key=lambda end: end[0])
+        if len(ends) == 1:
+            return ends[0]
+        field = [end[1][0] for end in ends[:len(ends) // 3]]
+        moves *= 4
 
 
 def worth(times):
@@ -565,24 +613,40 @@ def walk(ops, busy):
             deep |= below[d]
         near.append([d for d in o["deps"] if not deep >> d & 1])
         below.append(deep | sum(1 << d for d in o["deps"]))
-    row = [(o["eng"], near[i], o["acq"], o["rel"], busy[0][i], busy[1][i], busy[2][i])
-           + tuple(o["lat"] * case[6] + case[5] for case in CASES) for i, o in enumerate(ops)]
+    fits = {None: range(7, -1, -1), True: range(NROWED), False: range(7, NROWED - 1, -1)}
+    row = [("vspgy".index(o["eng"]), near[i], o["acq"] and fits[o["acq"].get("rowed")], o["rel"] and o["rel"]["users"][0],
+            busy[0][i], busy[1][i], busy[2][i]) + tuple(o["lat"] * case[6] + case[5] for case in CASES)
+           for i, o in enumerate(ops)]
+    ends = [i for i, o in enumerate(ops) if o["eng"] == "y"]
+    sends = [i for i, o in enumerate(ops) if o["nm"][:2] == "mi"]
 
-    def go(order):
-        fin, start, why = [None] * n, [None] * n, [None] * n
-        free = {e: (0.0, 0.0, 0.0, None) for e in "vspgy"}
-        banks = {j: (0.0, []) for j in range(8)}
-        pick, after = {}, {}
-        for i in order:
-            e, wait, bank, rel, b0, b1, b2, l0, l1, l2 = row[i]
+    def go(order, base=None, first=0):
+        if base is None:
+            fin, start, why, pick, after = [[None] * n for _ in range(5)]
+            free, banks, marks = [(0.0, 0.0, 0.0, None)] * 5, [(0.0, [])] * 8, []
+        else:
+            first >>= 4
+            pick, after, start, fin, why = [x[:] for x in base[1:6]]
+            marks = base[6][:first]
+            free, banks = base[6][first][0][:], base[6][first][1][:]
+            first <<= 4
+        for q in range(first, n):
+            if not q & 15:
+                marks.append((free[:], banks[:]))
+            i = order[q]
+            e, wait, fit, rel, b0, b1, b2, l0, l1, l2 = row[i]
             s0, s1, s2, prev = free[e]
-            if bank is not None:
-                kind = bank.get("rowed")
-                can = [(max(banks[j][0], s0), -j) for j in banks if kind is None or (j < NROWED) == kind]
-                if not can:
+            if fit:
+                kb = None
+                for j in fit:
+                    if banks[j] and (kb is None or banks[j][0] < banks[kb][0]):
+                        kb = j
+                        if banks[j][0] <= s0:
+                            break
+                if kb is None:
                     return None
-                bank["k"] = pick[i] = kb = -min(can)[1]
-                after[i] = banks.pop(kb)[1]
+                pick[i], after[i] = kb, banks[kb][1]
+                banks[kb] = None
                 wait = wait + after[i]
             why[i] = (prev, wait)
             for d in wait:
@@ -600,32 +664,46 @@ def walk(ops, busy):
             free[e] = (s0, s1, s2, i)
             fin[i] = (s0 + l0, s1 + l1, s2 + l2)
             if rel is not None:
-                banks[rel["k"]] = (s0 + l0, [i])
-        return [max(f[u] for f in fin) for u in range(3)], pick, after, start, fin, why
+                banks[pick[rel]] = (s0 + l0, [i])
+        times = [max(fin[i][u] for i in ends) for u in range(3)]
+        early = [sum(fin[i][u] for i in sends) / len(sends) for u in range(3)]
+        return times, pick, after, start, fin, why, marks, worth(times) + EARLY * worth(early)
     return go
 
 
-def polish(ops, go, order, rnd):
+def polish(ops, go, order, rnd, moves):
     cur = go(order)
-    val = worth(cur[0])
-    best = (val, (order, cur[1], cur[2]), list(cur[0]))
+    val = cur[7]
+    best = (worth(cur[0]), order, cur)
     before = [o["deps"] | o["soft"] for o in ops]
-    for it in range(MOVES):
-        heat = HEAT * (1.0 - it / MOVES)
-        times, pick, after, start, fin, why = cur
+    sends = [i for i, o in enumerate(ops) if o["nm"][:2] == "mi"]
+    paths = {}
+    for it in range(moves):
+        heat = HEAT * (1.0 - it / moves)
+        if it % 256 == 0:
+            trial = sorted(order, key=lambda j: cur[3][j][0])
+            got = go(trial)
+            if got and got[7] <= val + heat:
+                order, cur, val, paths = trial, got, got[7], {}
+        times, pick, after, start, fin, why = cur[:6]
         u = int(rnd() * len(CASES))
-        i = max(range(len(ops)), key=lambda j: fin[j][u])
-        held = []
-        while i is not None:
-            prev = why[i][0]
-            late = [d for d in why[i][1] if fin[d][u] >= start[i][u] - 1e-6]
-            if late:
-                i = late[0]
-            else:
-                if prev is not None and start[i][u] > 0:
-                    held.append((prev, i))
-                i = prev if start[i][u] > 0 else None
-        at = {j: q for q, j in enumerate(order)}
+        if not paths:
+            at = {j: q for q, j in enumerate(order)}
+        if it % 16 == 0:
+            paths.pop(u, None)
+        if u not in paths:
+            i = max(range(len(ops)), key=lambda j: fin[j][u]) if rnd() < 0.7 else sends[int(rnd() * len(sends))]
+            paths[u] = []
+            while i is not None:
+                prev = why[i][0]
+                late = [d for d in why[i][1] if fin[d][u] >= start[i][u] - 1e-6]
+                if late:
+                    i = late[0]
+                else:
+                    if prev is not None and start[i][u] > 0:
+                        paths[u].append((prev, i))
+                    i = prev if start[i][u] > 0 else None
+        held = paths[u]
         if held and rnd() < 0.8:
             a, z = held[int(rnd() * len(held))]
             if rnd() < 0.3:
@@ -650,15 +728,14 @@ def polish(ops, go, order, rnd):
         if new == part:
             continue
         trial = order[:at[a]] + new + order[at[z] + 1:]
-        got = go(trial)
-        if got is None:
-            continue
-        v = worth(got[0])
-        if v <= val + heat * rnd():
-            order, cur, val = trial, got, v
-            if v < best[0]:
-                best = (v, (order, got[1], got[2]), list(got[0]))
-    return best
+        got = go(trial, cur, at[a])
+        if got and got[7] <= val + heat * rnd():
+            order, cur, val, paths = trial, got, got[7], {}
+            if worth(got[0]) < best[0]:
+                best = (worth(got[0]), order, got)
+    val, order, got = best
+    held = [i for i, o in enumerate(ops) if o["acq"] is not None]
+    return val, (order, {i: got[1][i] for i in held}, {i: got[2][i] for i in held}), got[0]
 
 
 def rank_program(g, core, T, topo):

from concourse.mybir import AluOpType, ActivationFunctionType

A = AluOpType
F = ActivationFunctionType

NCH = 2
NB = 12 // NCH
N8 = 8 * NB
N16 = 16 * NB
CV = [[208, 208, 208], [208, 208, 208]]
YPE = [[0, 0, 0]] * NCH
GCOL = 32
VP = N8 // 2
FA = 2
CCP = 8
DSPLIT = True
GL = (96, 0)
NENG = 8
NROWED = 2
PAD = 16
MID = 2048.0
B = 4160.0
CAP = 37632.0
BIG = 2.0 ** 19
THR = 25.5
CLAMP = ((A.min, 4096.0 + PAD), (A.min, 4096.0 + PAD), (A.max, PAD - 2.0))
WB = (16.0, -16.0, -BIG, -1.0 / 16, 1.0, BIG, -1.0, BIG / 2, 8.0, -8.0, 0.5, -8.5, -B, -B / 2, CAP / 2, -0.25,
      -BIG / 2, B, B / 2, -CAP / 2, -0.5)
WH = (1.0, -1.0, BIG / 16, -BIG / 16)

SCRATCH = {n: ("sbuf", [128, w], d) for n, w, d in (
    ("xw", 4096 + 2 * PAD, "bfloat16"), ("actb", 16, "int32"), ("ypb", 12, "float32"),
    ("ycb", 12, "float32"), ("ci", 8, "int32"), ("cf", 16, "float32"), ("i144", 144, "float32"), ("wb", 144, "bfloat16"),
    ("idb", 128 * len(WB), "bfloat16"), ("idh", 128 * len(WH), "float16"), ("idf", 128, "float32"),
    ("pos", N16, "float32"), ("rst", N16, "float32"),
    ("ramp", 8 * N16, "float16"), ("rs2", 4 * N16, "bfloat16"), ("rs16", 4 * N16, "bfloat16"),
    ("lb", 8 * NCH, "uint16"), ("lm", 16, "uint16"), ("w0", 8 * NCH, "int32"), ("w1", 16, "int32"))}
SCRATCH["upp"] = ("sbuf", [128, NB, 16], "bfloat16")
SCRATCH["sdb"] = ("sbuf", [128, 128, 12], "int32")
SCRATCH["ysb"] = ("sbuf", [128, 128, 12], "float32")
PER_CHAIN = (
    ("st", [8 * NB, 16], "float16"), ("em", [8 * N16], "bfloat16"), ("lo", [8 * N16], "float32"),
    ("gg", [N16], "bfloat16"), ("sel", [8 * N16], "float32"), ("off", [7 * N8], "uint16"), ("fa", [16 * N8], "bfloat16"),
    ("fs", [112 * N8], "bfloat16"), ("cm", [112 * N8], "bfloat16"), ("sg", [7 * N8], "bfloat16"),
    ("mo", [3 * N16], "float16"), ("mi", [3 * NB, 16], "float16"), ("so", [3 * N8], "uint16"), ("si", [3 * N8], "uint16"),
    ("sd16", [N8], "float16"), ("no", [3 * NB, 24], "bfloat16"), ("a16", [N16], "float16"),
    ("hs", [3 * NB, 16], "bfloat16"), ("cs", [3 * N16], "bfloat16"), ("ee", [3 * N16], "bfloat16"),
    ("ct", [3 * N16], "bfloat16"), ("z8", [N16], "bfloat16"), ("th", [N16], "bfloat16"), ("cl", [NB, 16], "bfloat16"),
    ("t0", [2 * N16], "float32"))
for _c in range(NCH):
    for _n, _w, _d in PER_CHAIN:
        SCRATCH["%s%d" % (_n, _c)] = ("sbuf", [128] + _w, _d)
for _k in range(8):
    SCRATCH["ps%d" % _k] = ("psum", [128, 32, 16] if _k < NROWED else [128, 512], "float32")

SEMAPHORES = (["cv", "cs", "cp", "cg", "sent", "dact", "dsd0", "dsd1", "dx0", "dyp", "dyc"] + ["dy%d" % h for h in range(2)]
              + ["%s%d_%d" % (n, c, t) for n in ("arr", "ars") for c in range(NCH) for t in range(3)])

CASES = ((0.9, 1.56, 0.45, 50.0, 65.0, 70.0, 0.9), (1.05, 1.15, 0.525, 50.0, 65.0, 90.0, 1.0),
         (1.1, 2.0, 0.55, 50.0, 65.0, 70.0, 0.75))
LAG = 7000.0
BULK = 5000.0
STARTS = 9
MOVES = 3000
HEAT = 300.0
SEED = 1
EARLY = 0.1
WAIT = 300.0
PLAN = {}
ALL = slice(0, 16)


def build(g, T, topo, core, ops):
    rank = T.rank_of(core)
    nxt = T.cores[(rank + 1) % len(T.cores)]
    rid, pid = topo.addr(nxt)[0:2]
    emask = sum(1 << e for e in topo.engines(core, nxt)[:NENG])
    V, S, P, Y = g.vector, g.scalar, g.tensor, g.sync
    last_w, readers, held = {}, {}, []

    def add(eng, fn, n, R=(), W=(), lat=0.0, sem=None, banks=(), rel=None):
        if held:
            held[0].append((eng, fn, n, R, W, banks, rel))
            return
        i = len(ops)
        deps = {last_w[k] for k in list(R) + list(W) if k in last_w}
        for k in W:
            deps.update(readers.get(k, ()))
        for k in R:
            readers.setdefault(k, []).append(i)
        for k in W:
            last_w[k] = i
            readers[k] = []
        soft, acq = set(), None
        for bank in banks:
            if "users" not in bank:
                bank["users"] = []
                acq = bank
            for j in bank["users"]:
                (soft if ops[j]["eng"] == eng else deps).add(j)
            bank["users"].append(i)
        deps.discard(i)
        soft.discard(i)
        ops.append({"eng": eng, "fn": fn, "n": n, "lat": lat, "deps": deps, "sem": sem, "soft": soft,
                    "nm": (list(W) + ["-"])[0], "acq": acq, "rel": rel})

    def together(make):
        held.append([])
        make()
        calls = held.pop()
        banks = []
        for call in calls:
            banks += [bank for bank in call[5] if not any(bank is x for x in banks)]
        add(calls[0][0], lambda: [ins for call in calls for ins in call[1]()], [call[2] for call in calls],
            [x for call in calls for x in call[3]], [x for call in calls for x in call[4]], banks=banks, rel=calls[-1][6])

    def ap(x):
        if not isinstance(x, tuple):
            return x
        bank, rs, cs = x
        if bank["k"] < NROWED:
            return T["ps%d" % bank["k"]][:, rs, cs]
        return T["ps%d" % bank["k"]][:, 16 * rs.start + cs.start:16 * rs.stop:cs.step or 1]

    def bk(*xs):
        return [x[0] for x in xs if isinstance(x, tuple)]

    def ts(out, in0, s1, s2, o0, o1, n, R, W, rel=None):
        if o1 is None:
            add("v", lambda: [V.tensor_scalar(out, ap(in0), s1, None, o0)], n, R, W, banks=bk(in0), rel=rel)
        else:
            add("v", lambda: [V.tensor_scalar(out, ap(in0), s1, s2, o0, o1)], n, R, W, banks=bk(in0), rel=rel)

    def tt(out, in0, in1, op, n, R, W, rel=None):
        add("v", lambda: [V.tensor_tensor(out, in0, ap(in1), op)], n, R, W, banks=bk(in1), rel=rel)

    def cp(out, in_, n, R, W):
        add("v", lambda: [V.tensor_copy(out, in_)], n, R, W)

    def fill(out, val, n, W):
        add("v", lambda: [V.memset(out, val)], n, (), W)

    def scan(out, d0, d1, o0, o1, n, R, W, rel=None):
        for bank in bk(d1):
            bank["rowed"] = False
        add("v", lambda: [V.tensor_tensor_scan(out, d0, ap(d1), 0.0, o0, o1)], n, R, W, banks=bk(d1), rel=rel)

    def act(out, in_, func, bias, scale, n, R, W, rel=None):
        def fn():
            if bias is None:
                return [S.activation(ap(out), ap(in_), func)]
            return [S.activation(ap(out), ap(in_), func, bias=bias, scale=scale)]
        add("s", fn, n, R, W, banks=bk(out, in_), rel=rel)

    def mm(bank, groups, R, W, start=True, stop=True):
        if any(cs.stop < 16 or cs.start >= (cs.step or 1) for items in groups for rs, cs, l, r, n in items):
            bank["rowed"] = True

        def fn():
            return [P.matmul(ap((bank, rs, cs)), l[0], r, start and i == 0, stop and i == len(items) - 1)
                    for items in groups for i, (rs, cs, l, r, n) in enumerate(items)]
        add("p", fn, sum(max(64, it[4]) for items in groups for it in items),
            list(R) + sorted({it[2][1] for items in groups for it in items}), W, lat=100.0, banks=[bank])

    def iota(out, pat, base, cm, n, W, flt=False):
        if flt:
            add("g", lambda: [g.iota(out, pat, base, cm, allow_small_or_imprecise_dtypes=True)], 2 * n, (), W)
        else:
            add("g", lambda: [g.iota(out, pat, base, cm)], 2 * n, (), W)

    def dma(out, in_, sem, lat, R, W, n=0):
        add("y", lambda: [Y.dma_start(out, in_)], n, R, W, lat=lat, sem=(sem, 16))

    for h in range(2):
        dma(T.sdb[:, 64 * h:64 * (h + 1), :], T.sd[:, 768 * h:768 * (h + 1)], "dsd%d" % h, 3100.0 + 1200.0 * h, (), ["sd%d" % h])
    ops[-1]["soft"].add(0)
    add("s", lambda: [S.dma_start(T.actb[:, 0:12], T.act[:])], 0, (), ["act"], lat=2500.0, sem=("dact", 16))
    dma(T.xw[:, PAD:PAD + 4096], T.x[:], "dx0", 7200.0, (), ["x0"])
    ops[-1]["soft"].add(1)

    ci, cf = T.ci, T.cf
    SH, AND = A.logical_shift_right, A.bitwise_and
    iota(T.i144[:], [[1, 144]], 0, -1, 144, ["i144"], True)
    iota(ci[:, 5:6], [[0, 1]], 0, 1, 1, ["ci5"])
    iota(T.w0[:], [[NB, NCH], [1, 8]], 0, 0, 16, ["w0"])
    iota(T.pos[:], [[0, NB], [1, 16]], 0, 0, N16, ["pos"], True)
    iota(T.w1[:], [[32, 16]], 15, 0, 16, ["w1"])
    for h in range(2 - max(max(y) for y in YPE), 2):
        together(lambda: [fill(T.ramp[:, s * N16:(s + 1) * N16], B * (s + 1.5) + CAP / 2, N8, ["ramp%d" % h])
                          for s in range(4 * h, 4 * h + 4)])
    together(lambda: [
        fill(T.rs16[:], 0.0, 2 * N16, ["rs16"]), fill(T.rst[:], 1.0, N16, ["rst"]), fill(T.actb[:, 12:16], 0, 16, ["act2"])]
        + [fill(T["no%d" % c][:, :, 0:8], 1.0, 3 * N8 // 2, ["pads"]) for c in range(NCH)])
    together(lambda: [
        fill(T.rs2[:, 1::2], BIG, N16, ["rs2"]), fill(T.rs2[:, 0::2], -4 * BIG, N16, ["rs2"]),
        fill(T.upp[:, :, 8:16], 1.0, N8, ["upp"]), fill(T.upp[:, :, 0:8], 0.0, N8, ["upp"]),
        fill(T.xw[:, 0:PAD], 2.0 ** 62, 16, ["x1"]), fill(T.xw[:, PAD + 4096:], 2.0 ** 62, 16, ["x2"])])
    together(lambda: [fill(T.rs16[:, 0::16], -4 * BIG, 32, ["rs16"]), fill(T.rst[:, 0::16], 0.0, 8, ["rst"])])
    p_ = ci[:, 5:6]
    together(lambda: [ts(ci[:, 2:3], p_, 7, None, AND, None, 1, ["ci5"], ["ci"]),
                      ts(ci[:, 3:4], p_, 3, 1, SH, AND, 1, ["ci5"], ["ci"]),
                      ts(ci[:, 4:5], p_, 15, None, AND, None, 1, ["ci5"], ["ci"])])
    p8, hb, p16 = [ci[:, k:k + 1] for k in range(2, 5)]
    together(lambda: [ts(cf[:, 8:9], p16, -1.0, 15.0, A.mult, A.add, 1, ["ci"], ["cf"]),
                      ts(cf[:, 9:10], p8, float(N16), None, A.mult, None, 1, ["ci"], ["cf"]),
                      ts(cf[:, 10:11], hb, 16.0, None, A.mult, None, 1, ["ci"], ["cf"])])
    ts(T.idf[:], T.i144[:, 0:128], 0.0, None, A.is_equal, None, 128, ["i144"], ["idf"])
    ts(T.wb[:], T.i144[:], cf[:, 8:9], None, A.is_equal, None, 144, ["i144", "cf"], ["wb"])
    ib = {v: (T.idb[:, 128 * k:128 * k + 128], "ib%d" % (k // 4)) for k, v in enumerate(WB)}
    ih = {v: (T.idh[:, 128 * k:128 * k + 128], "ih%d" % min(k, 1)) for k, v in enumerate(WH)}
    for k in range(0, len(WB), 4):
        together(lambda: [act(ib[v][0], T.idf[:], F.Identity, 0.0, v, 128, ["idf"], [ib[v][1]]) for v in WB[k:k + 4]])
    for part in (WH[:1], WH[1:]):
        together(lambda: [ts(ih[v][0], T.idf[:], v, None, A.mult, None, 128, ["idf"], [ih[v][1]]) for v in part])
    cp(T.lb[:], T.w0[:], 16, ["w0"], ["lb"])
    ts(T.lm[:], T.w1[:], cf[:, 9:10], cf[:, 10:11], A.add, A.add, 16, ["w1", "cf"], ["lm"])

    for c in range(NCH):
        chain(c, T, g, add, together, ts, tt, scan, act, mm, ib, ih, rid, pid, emask)

    dma(T.yp[:], T.ypb[:], "dyp", 2000.0, ["yp%d" % c for c in range(NCH)], ())
    dma(T.yc[:], T.ycb[:], "dyc", 2000.0, ["yc%d" % c for c in range(NCH)], ())
    for h in range(2):
        dma(T.ys[:, 768 * h:768 * (h + 1)], T.ysb[:, 64 * h:64 * (h + 1), :], "dy%d" % h, 3000.0,
            ["ys%d_%d" % (c, h) for c in range(NCH)], ())


def chain(c, T, g, add, together, ts, tt, scan, act, mm, ib, ih, rid, pid, emask):
    b = {n: T["%s%d" % (n, c)] for n, _w, _d in PER_CHAIN}
    XR = ["x0", "x1", "x2"]

    def k(*names):
        return ["%s@%d" % (n, c) for n in names]

    def wb(*vals):
        return []

    def wh(*vals):
        return []

    st, sel, lo, mi, mo = [b[n] for n in ("st", "sel", "lo", "mi", "mo")]

    def rows(i, n=1):
        return slice(i * NB, (i + n) * NB)

    def flat(buf, i, n=1):
        return buf[:, i * N16:(i + n) * N16]

    R0, R1 = rows(0), rows(1)
    LOW, UP = slice(0, 8), slice(8, 16)

    stk = [k("st0"), k("st1")]

    def send(out, in_, sem, src, dst):
        add("g", lambda: [g.remote_dma(out, in_, T.sem[sem], T.sem.sent, pid, rid, emask)],
            200, k(src), k(dst), lat=3000.0, sem=(sem, -NENG))

    def nob(t):
        return b["no"][:, rows(t), 8:24]

    def lift(t):
        no = nob(t)
        ob = {}
        mm(ob, [[(R0, ALL, ib[-16.0], no, N16), (R0, ALL, ib[16.0], b["no"][:, rows(t), 0:16], N16)]],
           k("no%d" % t) + ["pads"], k("oh"))
        scan(flat(mo, t), T.rst[:], (ob, R0, ALL), A.mult, A.add, N16, k("oh") + ["rst"], k("mos%d" % t), rel=ob)
        send(mi[:, rows(t), :], flat(mo, t), "ars%d_%d" % (c, t), "mos%d" % t, "mis%d" % t)
        for h in range(2):
            bank = {}
            mm(bank, [[(rows(i), ALL, ib[-BIG], no, N16) for i in range(4)]], k("no%d" % t), k("lw%d" % h), stop=False)
            items = []
            for j in range(8):
                r = 4 * h
                while r < 4 * h + 4:
                    s = (r - j - 1) % 8
                    n = min(4 * h + 4 - r, 8 - s)
                    items.append((rows(r - 4 * h, n), slice(j, 16, 8), ih[1.0], st[:, rows(s, n), j::8], 2 * NB * n))
                    r += n
            mm(bank, [items], stk[0] + stk[1], k("lx%d" % h), start=False)
            scan(flat(lo, 4 * h, 4), T.rs16[:], (bank, rows(0, 4), ALL), A.add, A.max, 4 * N16, k("lx%d" % h) + ["rs16"],
                 k("lo%d" % h), rel=bank)
        part = slice(t * N8, (t + 1) * N8)
        ts(b["so"][:, part], lo[:, :].indirect(T.lm[:, 0:NB // 2]), MID + PAD, CLAMP[t][1], A.add, CLAMP[t][0], -N8,
           k("lo0", "lo1") + ["lm"], k("mo%d" % t))
        send(b["si"][:, part], b["so"][:, part], "arr%d_%d" % (c, t), "mo%d" % t, "mi%d" % t)

    def counts(t, items, bias, R):
        bank = {}
        mm(bank, [items + [(R0, ALL, ib[16.0], nob(t), N16)]], R + k("no%d" % t), k("cn"))
        together(lambda: [
            act(flat(b["ct"], t), (bank, R0, ALL), F.Relu, bias - 16.0, 1.0, N16, k("cn"), k("ct%d" % t)),
            act(b["z8"][:], (bank, R0, ALL), F.Relu, 16.0 * (bias - 23.0), 16.0, N16, k("cn"), k("z8"), rel=bank)])

    th, cl = b["th"], b["cl"]
    tt(th[:], T.actb[:, :].indirect(T.lb[:, 8 * c:8 * c + NB]), T.pos[:], A.not_equal, -N16,
       ["act", "act2", "lb", "pos"], k("th"))
    act(nob(0), th[:], F.Copy, None, None, N16, k("th"), k("no0"))
    if c == 0:
        for h in range(2):
            together(lambda: [ts(st[:, 4 * h * NB + j:4 * (h + 1) * NB:NB, :], T.sdb[:, 64 * h:64 * (h + 1), NB * c + j], -MID,
                                 None, A.add, None, 64, ["sd%d" % h], stk[h]) for j in range(NB)])
    else:
        together(lambda: [ts(st[:, j::NB, :], T.sdb[:, :, NB * c + j], -MID, None, A.add, None, 128, ["sd0", "sd1"],
                             stk[0] + stk[1]) for j in range(NB)])
    for h in range(2):
        bank = {}
        mm(bank, [[(rows(0, 4), ALL, ih[1.0], st[:, rows(4 * h, 4), :], 4 * N16)]], stk[h], k("ew%d" % h))
        act(flat(b["em"], 4 * h, 4), (bank, rows(0, 4), ALL), F.Relu, -16.0 * (MID - 1), 16.0, 4 * N16, k("ew%d" % h),
            k("em%d" % h), rel=bank)
    lift(0)
    counts(0, [(R0, ALL, ib[-1.0 / 16], flat(b["em"], s), N16) for s in range(8)], 8.0, k("em0", "em1"))

    for t in range(3):
        MI, MS = k("mi%d" % t), k("mis%d" % t)
        cv = CV[c][t]
        ncol = 7 * N8
        sgn = 1.0 if t < 2 else -1.0
        step = lambda a, z: mi[:, rows(t), a:z]
        seeds = b["sd16"][:]
        no = nob(t)
        NO = k("no%d" % t)
        FP = N8 // FA
        for u in range(FA):
            act(b["fa"][:, 16 * u * FP:16 * (u + 1) * FP], T.xw[:, :].indirect(b["si"][:, t * N8 + u * FP:t * N8 + (u + 1) * FP]),
                F.Copy, None, None, -16 * FP, MI + XR, k("fa%d" % u))
        ts(seeds, b["si"][:, t * N8:(t + 1) * N8], -MID - PAD, None, A.add, None, N8 // 2, MI, k("sd16"))
        MI = k("sd16")
        for h in range(2):
            n = 4 - h
            bank = {}
            mm(bank, [[(rows(0, n), slice(u, 16, 2), ih[1.0], st[:, rows(4 * h, n), 8 * u:8 * u + 8], n * N8) for u in range(2)]],
               stk[h], k("sw%d" % h), stop=False)
            mm(bank, [[(rows(i), slice(u, 16, 2), ih[(2 * u - 1) * BIG / 16], step(7, 15), N8) for i in range(n) for u in range(2)]],
               MS, k("sx%d" % h), start=False)
            scan(flat(sel, 4 * h, n), T.rs2[:, 0:n * N16], (bank, rows(0, n), ALL), A.add, A.max, n * N16,
                 k("sx%d" % h) + ["rs2"], k("sel%d" % h), rel=bank)
            ts(b["off"][:, 4 * h * N8:(4 * h + n) * N8], sel[:, 4 * h * N16 + 1:(4 * h + n) * N16:2], MID + PAD - BIG,
               CLAMP[t][1], A.add, CLAMP[t][0], n * N8, k("sel%d" % h), k("off%d" % h))

        def offk(c0, c1):
            return k(*[n for n, use in (("off0", c0 < 4 * N8), ("off1", c1 > 4 * N8)) if use])

        def fak(c0, c1):
            return k(*sorted({"fa%d" % (x % N8 // FP) for x in range(c0, c1)}))

        pieces = []
        c0 = ncol - cv
        while c0 < ncol:
            c1 = min(ncol, (c0 // VP + 1) * VP)
            f0 = (c0 % N8) * 16
            tt(b["cm"][:, 16 * c0:16 * c1], T.xw[:, :].indirect(b["off"][:, c0:c1]), b["fa"][:, f0:f0 + 16 * (c1 - c0)],
               A.is_lt, -16 * (c1 - c0), offk(c0, c1) + fak(c0, c1) + XR, k("cm%d" % c0))
            pieces.append((c0, c1, 0))
            c0 = c1
        c0 = 0
        while c0 < ncol - cv:
            c1 = min(ncol - cv, c0 + GCOL)
            act(b["fs"][:, 16 * c0:16 * c1], T.xw[:, :].indirect(b["off"][:, c0:c1]), F.Copy, None, None,
                -16 * (c1 - c0), offk(c0, c1) + XR, k("fs%d" % c0))
            d0 = c0
            while d0 < c1:
                d1 = min(c1, d0 + 32)
                bank = {}
                items = [(slice(0, d1 - d0), ALL, ib[-1.0], b["fs"][:, 16 * d0:16 * d1], 16 * (d1 - d0))]
                e0 = d0
                while e0 < d1:
                    e1 = min(d1, (e0 // N8 + 1) * N8)
                    f0 = (e0 % N8) * 16
                    items.append((slice(e0 - d0, e1 - d0), ALL, ib[1.0], b["fa"][:, f0:f0 + 16 * (e1 - e0)], 16 * (e1 - e0)))
                    e0 = e1
                mm(bank, [items], k("fs%d" % c0) + fak(d0, d1), k("df%d" % d0))
                act(b["cm"][:, 16 * d0:16 * d1], (bank, slice(0, d1 - d0), ALL), F.Sign, -2.0 ** -68, 1.0, 16 * (d1 - d0),
                    k("df%d" % d0), k("cm%d" % d0), rel=bank)
                pieces.append((d0, d1, 1))
                d0 = d1
            c0 = c1
        groups = []
        for kind in (1, 0):
            mine = [p for p in pieces if p[2] == kind]
            cut = len([p for p in mine if p[1] <= mine[-1][1] - GL[kind]])
            groups += [gr for gr in (mine[:cut], mine[cut:]) if gr]
        for gr in groups:
            g0, g1 = gr[0][0], gr[-1][1]
            bank = {}
            part = slice(0, (g1 - g0) // 16)
            for u in range(0, 16, CCP):
                mm(bank, [[(part, ALL, (T.wb[:, 15 - i:143 - i], "wb"), b["cm"][:, 16 * g0 + i:16 * g1:16], g1 - g0)
                           for i in range(u, u + CCP)]], k(*["cm%d" % p[0] for p in gr]), k("cc%d" % g0) if u + CCP == 16 else k("cc%d_%d" % (g0, u)),
                   start=u == 0, stop=u + CCP == 16)
            act(b["sg"][:, g0:g1], (bank, part, ALL), F.Sign, -1.0 if gr[0][2] else -8.5, 1.0, g1 - g0,
                k("cc%d" % g0, "sgfree"), k("sg%d_%d" % (t, g0)), rel=bank)
        hs = lambda a, z: b["hs"][:, rows(t), a:z]
        HS = k("hs%d" % t)
        bank = {}
        mm(bank, [[(R0, ALL, ib[sgn * BIG], T.upp[:], N16),
                   (R0, LOW, ih[1.0], seeds, N8), (R0, UP, ih[1.0], seeds, N8),
                   (R0, LOW, ih[sgn * BIG / 16], step(7, 15), N8), (R0, UP, ih[-sgn * BIG / 16], step(7, 15), N8)]],
           MI + MS + ["upp"], k("ax"))
        act(hs(0, 16), (bank, R0, ALL), F.Sign, MID - 0.5 * sgn, -sgn, N16, k("ax"), HS, rel=None if t else bank)
        sgn = 1.0 if t % 2 else -1.0
        if t == 0:
            bank = {}
            mm(bank, [[(R0, ALL, ib[BIG / 2], hs(0, 16), N16), (R0, LOW, ih[1.0], seeds, N8), (R0, UP, ih[1.0], seeds, N8)]],
               MI + HS, k("ax"))
        ts(b["a16"][:], (bank, R0, ALL), 0.0 if t else -BIG / 2, MID if sgn > 0 else -MID - 2.0, A.add,
           A.min if sgn > 0 else A.max, N16, k("ax"), k("a16"), rel=bank)
        ct, cs = flat(b["ct"], t), flat(b["cs"], t)
        CT, CS = k("ct%d" % t), k("cs%d" % t)
        bank = {}
        mm(bank, [[(R0, ALL, ib[8.0], hs(0, 16), N16), (R0, slice(0, 15), ib[-8.0], hs(1, 16), N16),
                   (R0, slice(15, 16), ib[-8.0], hs(0, 1), NB), (R0, ALL, ih[1.0], step(0, 16), N16),
                   (R0, slice(1, 16), ih[-1.0], step(0, 15), N16), (R0, UP, ih[1.0], step(0, 8), N8),
                   (R0, slice(9, 16), ih[-1.0], step(0, 7), N8)]], HS + MS, k("lq"))
        act(th[:], (bank, R0, ALL), F.Identity, THR + 64.0, -4.0, N16, k("lq"), k("th"), rel=bank)
        db = {}
        items = [(R0, ALL, ib[-1.0], ct, N16), (R0, ALL, ib[1.0], b["z8"][:], N16), (R0, ALL, ib[16.0], hs(0, 16), N16),
                 (R0, ALL, ib[16.0], no, N16)]
        R = CT + HS + NO + k("z8")
        for gr in groups:
            g0, g1 = gr[0][0], gr[-1][1]
            R = R + k("sg%d_%d" % (t, g0))
            done = gr is groups[-1]
            while g0 < g1:
                z = min(g1, (g0 // N8 + 1) * N8)
                part = slice(g0 % N8 // 8, (z - 1) % N8 // 8 + 1)
                items += [(part, half, ib[1.0], b["sg"][:, g0:z], z - g0) for half in (LOW, UP)]
                g0 = z
            if DSPLIT or done:
                mm(db, [items], R, k("dd", "sgfree") if done else k("da%d" % g1), start="users" not in db, stop=done)
                items, R = [], []
        act(cs, (db, R0, ALL), F.Sign, -THR, 1.0, N16, k("dd"), CS)
        tt(cl[:], th[:], (db, R0, ALL), A.is_lt, N16, k("dd", "th"), k("cl"), rel=db)
        ee = flat(b["ee"], t)
        EE = k("ee%d" % t)
        bank = {}
        mm(bank, [[(R0, ALL, ib[1.0], ct, N16), (R0, ALL, ib[0.5], hs(0, 16), N16), (R0, ALL, ib[-8.5], cs, N16)]],
           CT + CS + HS, k("ex"))
        act(ee, (bank, R0, ALL), F.Relu, -8.0, 1.0, N16, k("ex"), EE, rel=bank)
        ub = {}
        if YPE[c][t] < 2:
            mm(ub, [[(R0, ALL, ih[1.0], b["a16"][:], N16), (R0, ALL, ib[sgn * B], ct, N16), (R0, ALL, ib[sgn * B], no, N16),
                     (R0, ALL, ib[sgn * B / 2], hs(0, 16), N16), (R0, ALL, ib[-sgn * CAP / 2], cs, N16)]],
               CT + CS + HS + NO + k("a16"), k("uu"))
        fb = {}
        mm(fb, [[(R0, ALL, ih[1.0], b["a16"][:], N16), (R0, ALL, ib[sgn * BIG / 2], hs(0, 16), N16),
                 (R0, ALL, ib[sgn * BIG / 2], cs, N16), (R0, ALL, ib[-sgn * BIG], no, N16)]],
           CS + HS + NO + k("a16") + wb(sgn * BIG / 2, -sgn * BIG) + wh(1.0), k("fx"))
        onpe = YPE[c][t]
        if onpe:
            bank = {}
            mm(bank, [[(R0, ALL, ib[1.0], ct, N16), (R0, ALL, ib[1.0], no, N16), (R0, ALL, ib[0.5], hs(0, 16), N16)]],
               CT + HS + NO, k("gx"))
            act(b["gg"][:], (bank, R0, ALL), F.Copy, None, None, N16, k("gx"), k("gg"), rel=bank)
        for h in range(2):
            bank = {}
            blk = st[:, rows(4 * h, 4), :]
            R4 = rows(0, 4)
            if h + onpe >= 2:
                YR = k("yr%d" % h)
                mm(bank, [[(R4, ALL, ih[-sgn], flat(T.ramp, 4 * h, 4), 4 * N16)]
                          + [(rows(i), ALL, w, x, N16) for w, x in ((ih[1.0], b["a16"][:]), (ib[sgn * B], b["gg"][:]))
                             for i in range(4)]], k("a16", "gg") + ["ramp%d" % h], k("ya%d" % h), stop=False)
                mm(bank, [[(rows(i), ALL, ib[-sgn * CAP / 2], cs, N16) for i in range(4)]], CS, YR, start=False)
                ramp = (bank, R4, ALL)
            else:
                YR = k("yr%d" % h if t else "sel%d" % h)
                together(lambda: [
                    act((bank, rows(s % 4), ALL) if t else flat(sel, s), (ub, R0, ALL), F.Identity,
                        -sgn * (B * (s + 1.5) + CAP / 2), 1.0, N16, k("uu"), YR, rel=ub if h or onpe else None)
                    for s in range(4 * h, 4 * h + 4)])
                ramp = (bank, R4, ALL)
            if t:
                tt(blk, blk, ramp, A.min if sgn > 0 else A.max, 4 * N16, stk[h] + YR, stk[h], rel=bank)
            else:
                mm(bank, [[(R4, ALL, ib[-B / 2], flat(b["em"], 4 * h, 4), 4 * N16), (R4, ALL, ih[1.0], blk, 4 * N16)]],
                   k("em%d" % h) + stk[h], k("eb%d" % h))
                tt(blk, flat(sel, 4 * h, 4), ramp, A.max, 4 * N16, YR + k("eb%d" % h), stk[h], rel=bank)
            if h == 0:
                tt(st[:, R0, :], st[:, R0, :], (fb, R0, ALL), A.max if sgn > 0 else A.min, N16, k("st0", "fx"), k("st0"), rel=fb)
        ob = {}
        mm(ob, [[(R0, ALL, ib[-0.25], th[:], N16), (R0, ALL, ib[-16.0], cl[:], N16), (R0, ALL, ib[16.0], cl[:, :, ::-1], N16)]],
           k("th", "cl"), k("nx"))
        if t < 2:
            act(nob(t + 1), (ob, R0, ALL), F.Identity, -THR / 64, -1.0 / 16, N16, k("nx"), k("no%d" % (t + 1)), rel=ob)
            lift(t + 1)
            counts(t + 1, [(R0, ALL, ib[1.0], ee, N16), (R0, ALL, ib[0.5], cs, N16)], 0.5, EE + CS)
        else:
            t0, t1 = flat(b["t0"], 0), flat(b["t0"], 1)
            scan(t0, T.rst[:], (ob, R0, ALL), A.mult, A.add, N16, k("nx") + ["rst"], k("t0"), rel=ob)
            scan(t1, T.rst[:], t0, A.mult, A.add, N16, k("t0") + ["rst"], k("t1"))
            act(T.ypb[:, NB * c:NB * (c + 1)], b["t0"][:, N16 + 15::16], F.Identity, 16.0 - 8.5 * (16.0 + THR / 4), -1.0 / 16,
                NB, k("t1"), ["yp%d" % c])
            for h in range(2):
                together(lambda: [
                    ts(T.ysb[:, 64 * h:64 * (h + 1), NB * c + j], st[:, 4 * h * NB + j:4 * (h + 1) * NB:NB, :], MID, MID,
                       A.min, A.add, 64, k("st%d" % h), ["ys%d_%d" % (c, h)]) for j in range(NB)])
            bank = {}
            items = []
            for u in range(3):
                items += [(R0, ALL, ib[1.0], flat(b["ct"], u), N16), (R0, ALL, ib[0.5], b["hs"][:, rows(u), :], N16),
                          (R0, ALL, ib[-1.0], flat(b["ee"], u), N16), (R0, ALL, ib[-0.5], flat(b["cs"], u), N16)]
            mm(bank, [items], k(*["%s%d" % (n, u) for n in ("ct", "hs", "ee", "cs") for u in range(3)]) + wb(-0.5), k("sc"))
            scan(flat(lo, 0), T.rst[:], (bank, R0, ALL), A.mult, A.add, N16, k("sc") + ["rst"], k("lo0"), rel=bank)
            act(T.ycb[:, NB * c:NB * (c + 1)], lo[:, 15:N16:16], F.Copy, None, None, NB, k("lo0"), ["yc%d" % c])


def costs(ops, case):
    cy, gg, pe, fv, fs, wake, lf = case
    out = []
    for o in ops:
        e, n = o["eng"], o["n"]
        if e == "p":
            out.append(20.0 + n * pe)
        elif e in "vs":
            out.append(sum((fv if e == "v" else fs) + (max(64, m) if m >= 0 else -m * gg) * cy
                           for m in (n if isinstance(n, list) else [n])))
        else:
            out.append(160.0 + n * cy if e == "g" else 60.0)
    return out


def schedule(ops, succ, busy, prio):
    wake = CASES[0][5]
    n = len(ops)
    left = [len(o["deps"] | o["soft"]) for o in ops]
    ready = [i for i in range(n) if left[i] == 0]
    rt = [0.0] * n
    free = {e: 0.0 for e in "vspgy"}
    banks = [[0.0, (), True] for _ in range(8)]
    order, pick, after = [], {}, {}
    while ready:
        av = sorted((banks[j][0], -j) for j in range(8) if banks[j][2])
        fit = {None: av, True: [a for a in av if -a[1] < NROWED], False: [a for a in av if -a[1] >= NROWED]}
        able = []
        for i in ready:
            o = ops[i]
            s = max(rt[i], free[o["eng"]])
            kb = None
            if o["acq"] is not None:
                can = fit[o["acq"].get("rowed")]
                if not can:
                    continue
                kb = -min([a for a in can if a[0] <= s], key=lambda a: a[1], default=can[0])[1]
                s = max(s, banks[kb][0])
            able.append((s, i, kb))
        if not able:
            return None
        s, i, kb = min(able)
        key, s, i, kb = max((prio[j], u, j, q) for u, j, q in able if ops[j]["eng"] == ops[i]["eng"] and u <= s + WAIT)
        o = ops[i]
        if o["acq"] is not None:
            o["acq"]["k"] = pick[i] = kb
            after[i] = banks[kb][1]
            banks[kb][2] = False
        free[o["eng"]] = s + busy[i]
        fin = s + busy[i] + o["lat"] + wake
        if o["rel"] is not None:
            banks[o["rel"]["k"]] = [fin, list(o["rel"]["users"]), True]
        ready.remove(i)
        order.append(i)
        for j in succ[i]:
            rt[j] = max(rt[j], fin if i in ops[j]["deps"] else s + busy[i])
            left[j] -= 1
            if left[j] == 0:
                ready.append(j)
    return order


def plan(ops):
    n = len(ops)
    succ = [[] for _ in range(n)]
    for i, o in enumerate(ops):
        for d in o["deps"] | o["soft"]:
            succ[d].append(i)
    busy = [costs(ops, case) for case in CASES]
    prio = [0.0] * n
    for i in range(n - 1, -1, -1):
        prio[i] = busy[0][i] + ops[i]["lat"] + max([prio[j] + CASES[0][5] for j in succ[i]] or [0.0])
    seed = [SEED]

    def rnd():
        seed[0] = (seed[0] * 1103515245 + 12345) % 2147483648
        return seed[0] / 2147483648.0

    go = walk(ops, busy)
    field = []
    while len(field) < STARTS:
        lag, bulk = LAG * (0.7 + 0.6 * rnd()), BULK * (0.5 + rnd())
        got = schedule(ops, succ, busy[0], [
            prio[i] + 300.0 * rnd() - lag * ("@1" in o["nm"]) - bulk * (o["nm"][:2] in ("cm", "fs", "df", "cc"))
            for i, o in enumerate(ops)])
        if got and go(got):
            field.append(got)
    moves = MOVES
    while True:
        ends = sorted((polish(ops, go, order, rnd, moves) for order in field), key=lambda end: end[0])
        if len(ends) == 1:
            return ends[0]
        field = [end[1][0] for end in ends[:len(ends) // 3]]
        moves *= 4


def worth(times):
    return sum(tm / (case[0] * (1.0 + 0.3 * case[1])) for tm, case in zip(times, CASES))


def walk(ops, busy):
    n = len(ops)
    below, near = [], []
    for o in ops:
        deep = 0
        for d in o["deps"]:
            deep |= below[d]
        near.append([d for d in o["deps"] if not deep >> d & 1])
        below.append(deep | sum(1 << d for d in o["deps"]))
    fits = {None: range(7, -1, -1), True: range(NROWED), False: range(7, NROWED - 1, -1)}
    row = [("vspgy".index(o["eng"]), near[i], o["acq"] and fits[o["acq"].get("rowed")], o["rel"] and o["rel"]["users"][0],
            busy[0][i], busy[1][i], busy[2][i]) + tuple(o["lat"] * case[6] + case[5] for case in CASES)
           for i, o in enumerate(ops)]
    ends = [i for i, o in enumerate(ops) if o["eng"] == "y"]
    sends = [i for i, o in enumerate(ops) if o["nm"][:2] == "mi"]

    def go(order, base=None, first=0):
        if base is None:
            fin, start, why, pick, after = [[None] * n for _ in range(5)]
            free, banks, marks = [(0.0, 0.0, 0.0, None)] * 5, [(0.0, [])] * 8, []
        else:
            first >>= 4
            pick, after, start, fin, why = [x[:] for x in base[1:6]]
            marks = base[6][:first]
            free, banks = base[6][first][0][:], base[6][first][1][:]
            first <<= 4
        for q in range(first, n):
            if not q & 15:
                marks.append((free[:], banks[:]))
            i = order[q]
            e, wait, fit, rel, b0, b1, b2, l0, l1, l2 = row[i]
            s0, s1, s2, prev = free[e]
            if fit:
                kb = None
                for j in fit:
                    if banks[j] and (kb is None or banks[j][0] < banks[kb][0]):
                        kb = j
                        if banks[j][0] <= s0:
                            break
                if kb is None:
                    return None
                pick[i], after[i] = kb, banks[kb][1]
                banks[kb] = None
                wait = wait + after[i]
            why[i] = (prev, wait)
            for d in wait:
                f0, f1, f2 = fin[d]
                if f0 > s0:
                    s0 = f0
                if f1 > s1:
                    s1 = f1
                if f2 > s2:
                    s2 = f2
            start[i] = (s0, s1, s2)
            s0 += b0
            s1 += b1
            s2 += b2
            free[e] = (s0, s1, s2, i)
            fin[i] = (s0 + l0, s1 + l1, s2 + l2)
            if rel is not None:
                banks[pick[rel]] = (s0 + l0, [i])
        times = [max(fin[i][u] for i in ends) for u in range(3)]
        early = [sum(fin[i][u] for i in sends) / len(sends) for u in range(3)]
        return times, pick, after, start, fin, why, marks, worth(times) + EARLY * worth(early)
    return go


def polish(ops, go, order, rnd, moves):
    cur = go(order)
    val = cur[7]
    best = (worth(cur[0]), order, cur)
    before = [o["deps"] | o["soft"] for o in ops]
    sends = [i for i, o in enumerate(ops) if o["nm"][:2] == "mi"]
    paths = {}
    for it in range(moves):
        heat = HEAT * (1.0 - it / moves)
        if it % 256 == 0:
            trial = sorted(order, key=lambda j: cur[3][j][0])
            got = go(trial)
            if got and got[7] <= val + heat:
                order, cur, val, paths = trial, got, got[7], {}
        times, pick, after, start, fin, why = cur[:6]
        u = int(rnd() * len(CASES))
        if not paths:
            at = {j: q for q, j in enumerate(order)}
        if it % 16 == 0:
            paths.pop(u, None)
        if u not in paths:
            i = max(range(len(ops)), key=lambda j: fin[j][u]) if rnd() < 0.7 else sends[int(rnd() * len(sends))]
            paths[u] = []
            while i is not None:
                prev = why[i][0]
                late = [d for d in why[i][1] if fin[d][u] >= start[i][u] - 1e-6]
                if late:
                    i = late[0]
                else:
                    if prev is not None and start[i][u] > 0:
                        paths[u].append((prev, i))
                    i = prev if start[i][u] > 0 else None
        held = paths[u]
        if held and rnd() < 0.8:
            a, z = held[int(rnd() * len(held))]
            if rnd() < 0.3:
                same = [j for j in order[:at[a]] if ops[j]["eng"] == ops[a]["eng"]][-3:]
                a = same[int(rnd() * len(same))] if same else a
        else:
            z = int(rnd() * len(ops))
            a = order[max(0, at[z] - 1 - int(rnd() * 12))]
        part = order[at[a]:at[z] + 1]
        if rnd() < 0.5:
            move = {z}
            for j in reversed(part):
                if j in move:
                    move |= before[j]
            new = [j for j in part if j in move] + [j for j in part if j not in move]
        else:
            move = {a}
            for j in part:
                if before[j] & move:
                    move.add(j)
            new = [j for j in part if j not in move] + [j for j in part if j in move]
        if new == part:
            continue
        trial = order[:at[a]] + new + order[at[z] + 1:]
        got = go(trial, cur, at[a])
        if got and got[7] <= val + heat * rnd():
            order, cur, val, paths = trial, got, got[7], {}
            if worth(got[0]) < best[0]:
                best = (worth(got[0]), order, got)
    val, order, got = best
    held = [i for i, o in enumerate(ops) if o["acq"] is not None]
    return val, (order, {i: got[1][i] for i in held}, {i: got[2][i] for i in held}), got[0]


def rank_program(g, core, T, topo):
    if T.rank_of(core) is None:
        return
    ops = []
    build(g, T, topo, core, ops)
    if "p" not in PLAN:
        PLAN["p"] = plan(ops)
    order, pick, after = PLAN["p"][1]
    queue = {"v": g.vector, "s": g.scalar, "p": g.tensor, "g": g, "y": g.sync}
    total = {}
    known = {e: {} for e in queue}
    for at, i in enumerate(order):
        o = ops[i]
        e = o["eng"]
        kn = known[e]
        o["at"] = at
        if i in pick:
            o["acq"]["k"] = pick[i]
        need = {}
        for d in list(o["deps"]) + list(after.get(i, ())):
            s, v = ops[d]["done"]
            need[s] = max(need.get(s, (0, 0)), (v, d))
        for s, (v, d) in sorted(need.items(), key=lambda it: -ops[it[1][1]]["at"]):
            if kn.get(s, 0) < v:
                queue[e].wait_ge(T.sem[s], v)
                kn[s] = v
                for s2, v2 in ops[d]["seen"].items():
                    kn[s2] = max(kn.get(s2, 0), v2)
        o["seen"] = dict(kn)
        ins = o["fn"]()
        if o["sem"] is None:
            s = "c" + e
            for x in ins:
                x.then_inc(T.sem[s], 1)
            total[s] = total.get(s, 0) + len(ins)
            o["done"] = (s, total[s])
        else:
            s, v = o["sem"]
            if v > 0:
                ins[0].then_inc(T.sem[s], v)
            else:
                v = -v
                total["sent"] = total.get("sent", 0) + v
                o["seen"] = {}
            total[s] = v
            o["done"] = (s, v)
    for s, v in total.items():
        g.wait_ge(T.sem[s], v)
